import numpy as np, ml_dtypes
CORES = [16,17,18,19,150,151]
N = 6
BF = ml_dtypes.bfloat16
def gentries(a):
    return np.ascontiguousarray(a.reshape(8, 16, -1).transpose(0, 2, 1)).reshape(8, -1)
def gtable(e):
    e = np.asarray(e); return np.ascontiguousarray(e.reshape(8, -1, 16).transpose(0, 2, 1)).reshape(128, -1).astype(np.int32)
Q, A, S, RO, B = 640, 192, 3, 5, 2048
W, H = N * Q, A // 4
def some(rng, shape, n):
    u = rng.random(shape); u = np.where(rng.random(shape) < 0.5, u, u * u)
    return np.minimum((n * u).astype(np.int64), n - 1)
def parts(rng):
    F = (rng.integers(0, 256, (8, 16, W)) * np.sqrt(rng.random((8, 1, W)))).astype(np.int64)
    NB = np.zeros((8, 16, W), np.int64); HO = np.zeros((N, 8, A), np.int64)
    for g in range(8):
        o = rng.permutation(W); NB[g] = o[some(rng, (16, W), W)]; HO[:, g] = o[some(rng, (N, A), W)]
    return F, NB, HO
def plant(rng):
    F, NB, HO = parts(rng); own = np.zeros((N, 8, H, S + 3), np.int64); k = N * H * (S + 3)
    for g in range(8):
        o = rng.permutation(W); mine, rest = o[:k], o[k:]
        own[:, g] = mine.reshape(N, H, S + 3)
        NB[g] = rest[some(rng, (16, W), W - k)]; HO[:, g] = rest[some(rng, (N, A), W - k)]
        for r in range(N): HO[r, g, rng.permutation(A)[:H]] = own[r, g, :, 0]
        NB[g][:, mine] = mine; F[g][:, mine] = 0
    return F, NB, HO, own
def lead(rng, NB, g, t, *cs):
    z = np.argsort(rng.random((16, len(t))), axis=0)
    for i, c in enumerate(cs):
        NB[g, z[2 * i], t] = c; NB[g, z[2 * i + 1], t] = c
def climb(rng, F, NB, g, e):
    n = len(e); m = np.zeros((16, n), np.int64)
    for k in range(S + 1):
        a = rng.integers(0, 40, (16, n)) * (rng.random((16, n)) < 0.2 * rng.random((1, n))); a[rng.integers(0, 16, n), np.arange(n)] += 1
        m = m + a; F[g][:, e[:, 1 + k]] = m; lead(rng, NB, g, e[:, k], e[:, 1 + k])
def pack(F, NB, HO):
    return {"feat": np.stack([F[:, :, r * Q:(r + 1) * Q].reshape(128, Q) for r in range(N)]).astype(np.float32).astype(BF),
            "nb": np.stack([NB[:, :, r * Q:(r + 1) * Q].reshape(128, Q) for r in range(N)]).astype(np.int32),
            "home": np.stack([gtable(a) for a in HO])}
def setup_inputs(rng):
    F, NB, HO = parts(rng)
    return pack(F, NB, HO)
def setup_inputs_cut(rng):
    F, NB, HO, own = plant(rng); j = np.arange(H); odd = j % 2 == 1
    for g in range(8):
        for r in range(N):
            e = own[r, g]
            if r % 2 == 0:
                u = e[:, 1]; F[g][8:, u] = 255; lead(rng, NB, g, e[:, 0], u)
                lead(rng, NB, g, u, own[np.where(j < H // 2, (r + 1) % N, (r - 1) % N), g, j, 1])
            else:
                t = [e[:, 1 + k] for k in range(S + 1)]; alt = e[:, S + 2]
                m = np.zeros((16, H), np.int64); m[:8] = rng.integers(100, 181, (8, H)); F[g][:, t[0]] = m
                b = np.zeros((16, H), np.int64); b[8:] = rng.integers(1, 91, (8, H))
                for k in range(1, S + 1):
                    y = np.where(m > 0, m + rng.integers(1, 10, (16, H)), 0)
                    if k == 1: y = np.where(odd, b, y)
                    F[g][:, t[k]] = y; m = np.maximum(m, y); lead(rng, NB, g, t[k - 1], t[k])
                F[g][:8, alt] = rng.integers(1, 50, (8, H)); lead(rng, NB, g, alt, t[1])
                lead(rng, NB, g, e[:, 0], t[0], np.where(odd, t[1], alt))
    return pack(F, NB, HO)
def setup_inputs_full(rng):
    F, NB, HO = parts(rng); rf = int(rng.integers(0, N - 1)); n = A * (2 * S + 2); w = 16 // (2 * S - 1)
    for g in range(8):
        o = rng.permutation(W); mine, rest = o[:n], o[n:]; e = mine.reshape(A, 2 * S + 2)
        NB[g] = rest[some(rng, (16, W), W - n)]; HO[:, g] = rest[some(rng, (N, A), W - n)]
        NB[g][:, mine] = mine; F[g][:, mine] = 0; HO[rf, g] = e[:, 0]
        if g % 2 == 0: climb(rng, F, NB, g, e)
        else:
            rn = N - 1 if rf == 0 and g > 4 else rf + 1
            k = np.arange(A) % S if g % 4 == 1 else np.full(A, S - 1)
            for i in range(2 * S - 1):
                F[g][w * i:w * i + w, e[:, 1 + i]] = rng.integers(1, 256, (w, A)); lead(rng, NB, g, e[:, i], e[:, 1 + i])
            want = e[np.arange(A), 1 + k]; x = e[:, 2 * S]; HO[rn, g] = e[:, 2 * S + 1]
            if g != 7: F[g][15, x] = 1
            lead(rng, NB, g, x, want); lead(rng, NB, g, e[:, 2 * S + 1], want, x)
    return pack(F, NB, HO)
def setup_inputs_same(rng):
    F, NB, HO = parts(rng)
    for g in range(8):
        if g % 2 == 0:
            kinds = rng.integers(0, 256, (16, 6)); kinds[:, 0] = 0; F[g] = kinds[:, rng.integers(0, 6, W)]
        if g < 2: HO[:, g] = rng.permutation(W)[:24][rng.integers(0, 24, (N, A))]
        if g % 4 == 3: NB[g, 8:] = NB[g, :8]
        if g in (4, 5):
            h = int(rng.integers(0, W)); t = int(rng.integers(0, N)) * Q + rng.permutation(Q)[:5]; t = t[t != h][:1 if g == 4 else 4]
            HO[:, g] = h; NB[g][:, h] = t[np.arange(16) % len(t)]; F[g][:, t] = rng.integers(1, 256, (16, len(t)))
    return pack(F, NB, HO)
def setup_inputs_ends(rng):
    F, NB, HO = parts(rng)
    F = 255 * (rng.random((8, 16, W)) < 0.6 * rng.random((8, 1, W))).astype(np.int64); F[:, :, 0] = 255; F[:, :, W - 1] = 255
    ends = np.concatenate([np.arange(N) * Q, np.arange(N) * Q + Q - 1])
    for g in range(8):
        if g % 2 == 0:
            NB[g] = np.where(rng.random((16, W)) < 0.3, rng.choice(ends, (16, W)), NB[g])
            HO[:, g, ::3] = rng.choice(ends, HO[:, g, ::3].shape)
        if g % 4 == 1:
            m = np.nonzero(rng.random(W) < 0.3)[0]; NB[g][:, m] = m
        if g % 4 == 3:
            q = int(rng.integers(0, N)); NB[g] = q * Q + NB[g] % Q; HO[:, g] = q * Q + HO[:, g] % Q
    return pack(F, NB, HO)
def setup_inputs_spread(rng):
    F, NB, HO = parts(rng)
    F = (rng.random((8, 16, W)) * np.exp2(rng.integers(0, 9, (8, 1, W))) * (rng.random((8, 1, W)) > 0.0625)).astype(np.int64)
    for g in range(8):
        o = rng.permutation(W)
        NB[g] = o[np.minimum((W * rng.random((16, W)) ** 4).astype(np.int64), W - 1)]; HO[:, g] = o[np.minimum((W * rng.random((N, A)) ** 3).astype(np.int64), W - 1)]
    return pack(F, NB, HO)
def check_inputs(d):
    bad = []; v = np.asarray(d["feat"]).astype(np.float32)
    if not (np.min(v) >= 0 and np.max(v) <= 255 and np.all(v == np.floor(v))): bad.append("feat: whole numbers from 0 to 255")
    for k in ("nb", "home"):
        if np.min(d[k]) < 0 or np.max(d[k]) > W - 1: bad.append("range of " + k)
    return bad
def reference(feat, nb, home):
    F = np.concatenate([a.astype(np.float32).astype(np.int64).reshape(8, 16, Q) for a in feat], axis=2)
    C = np.concatenate([a.astype(np.int64).reshape(8, 16, Q) for a in nb], axis=2)
    F = np.ascontiguousarray(F.transpose(0, 2, 1)); C = np.ascontiguousarray(C.transpose(0, 2, 1))
    h = np.stack([gentries(a) for a in home]).astype(np.int64)
    ri = np.arange(N)[:, None, None]; gi = np.arange(8)[None, :, None]; ids = np.arange(N * A).reshape(N, 1, A, 1)
    bt = np.zeros((N, 8, S, A), np.int64); bk = np.zeros((N, 8, S, A), np.int64); cnt = np.zeros((N, 8, A), np.int64)
    T = np.zeros((N, 8, W), np.int64)
    for rnd in range(RO):
        V = np.maximum(T, np.maximum(np.roll(T, 1, axis=0), np.roll(T, -1, axis=0)))
        still = np.ones((N, 8, A), bool); n = np.zeros((N, 8, A), np.int64); M = np.zeros((N, 8, A, 16), np.int64); last = h
        for k in range(S):
            b = bt[:, :, k]
            still = still & (k < cnt) & (V[ri, gi, b] == bk[:, :, k])
            M = np.where(still[..., None], np.maximum(M, F[gi, b]), M); last = np.where(still, b, last); n = n + still
        c = C[gi, last]
        gain = np.add.reduce(np.maximum(F[gi[..., None], c] - M[:, :, :, None, :], 0), axis=-1)
        key = B * gain + (B - 1) - ids
        ok = (n < S)[..., None] & (gain > 0) & (key > V[ri[..., None], gi[..., None], c])
        p = np.argmax(np.where(ok, gain, 0), axis=-1)[..., None]
        ct = np.take_along_axis(c, p, -1)[..., 0]; kt = np.take_along_axis(key, p, -1)[..., 0]; bid = np.any(ok, axis=-1)
        best = np.zeros((N, 8, W), np.int64); np.maximum.at(best, (ri, gi, ct), np.where(bid, kt, 0))
        win = bid & (best[ri, gi, ct] == kt)
        T = np.zeros((N, 8, W), np.int64)
        for k in range(S):
            w = np.nonzero(k < n); T[w[0], w[1], bt[:, :, k][w]] = bk[:, :, k][w]
        w = np.nonzero(win); T[w[0], w[1], ct[w]] = kt[w]
        bt[w[0], w[1], n[w], w[2]] = ct[w]; bk[w[0], w[1], n[w], w[2]] = kt[w]; cnt = n + win
    yb = np.where(np.arange(S)[None, None, :, None] < cnt[:, :, None, :], bt, -1)
    return {"yb": yb.reshape(N, 8, S * A).astype(np.float32), "yt": T.astype(np.float32)}

@@ -1,0 +1,582 @@
+from concourse.bass import DstId, RemoteDMATransfer
+from concourse.mybir import AluOpType as ALU, AxisListType, ActivationFunctionType as AF
+
+N, Q, A, RO = 6, 640, 192, 5
+W = N * Q
+U23 = float(2 ** 23)
+M64 = 1.5 * 2.0 ** 29
+M2K = 1.5 * 2.0 ** 34
+M32K = 1.5 * 2.0 ** 38
+MV = 1.5 * 2.0 ** 54
+FW, CW, TW = 4224, 4032, 4608
+RELAY = True
+GENG = "aav"
+RENG = "aaaaaa"
+ORDER = "g0 g1 A I s0 P g2 B c0 s1 c1 s2 t0 c2 t1 t2 N T S"
+NMV = 4
+CSPLIT = {1: 6, 2: 12, 3: 18}
+VSPLIT = {1: (64, 128), 2: (76, 152), 3: (86, 172)}
+
+f32, bf, i32, u16 = "float32", "bfloat16", "int32", "uint16"
+SB = {
+    bf: dict(Fw=FW, Vw=W, BW=4096, E1=144, E2=144, Z=640, BLK=128, BLV=128, Ib=128, Nb=128, WK1=128, WK2=128, UT=192,
+             Vs=576, Vg=3072, xx=24, H=192, Bt=192, B=192, junk=1152, Mn=192, Mw=192, Fg=3072, X=3072, Pc=720),
+    u16: dict(Cu=W, hU=12, btU=36, koU=36, pvU=12, noU=12, cU=192, ctU=12, oU=12, woU=12, cG=192),
+    i32: dict(Cw=CW, hI=12, pI=4, cI=192, chl=384),
+    f32: dict(Tw=TW, CA=2880, col=16, AR=192, JG=128, XP=160, I23=128, I1=128, MC=8, FL=12, OH=16, io2=24, IDL=192, PST=192,
+              RS=384, aL=12, aT=12, aK=12, mK=12, mK1=12, no=12, t12=12, KS=72, KT=72, M1=36, dumB=12, dmpK=12, idl1=12,
+              nbS=12, FLO=240, ZER=240, rs=36, kv=576, S12=384, G=192, sc=384, sT=384, rm=384, Hh=24, GT=12, ck=24, nb1=12,
+              nbb=12, Wr=12, oF=12, ktR=192, lw=12, nlw=12, ee=72, Sn=384, Tc=960, NL=960, NR=960, Vc=240,
+              yL=36, yB=36, yE=36, yW=36, yo=576),
+}
+SCRATCH = {n_: ("sbuf", [128, c_], d_) for d_, t_ in SB.items() for n_, c_ in t_.items()}
+SCRATCH.update({n_: ("sbuf", [128, 24, 4], f32) for n_ in ("K2", "K23", "St", "kept")})
+SCRATCH.update({n_: ("sbuf", [128, 12, 4], f32) for n_ in ("DUM", "dl", "ko")})
+SCRATCH["Abd"] = ("sbuf", [128, 12, 8, 16], bf)
+BANKS = ["pb0", "pb1", "pb2", "pb3", "pb4", "pb5", "pS", "pP"]
+SCRATCH.update({n_: ("psum", [128, 512], f32) for n_ in BANKS})
+NDS = 32
+SEMAPHORES = (["qv", "qa", "qp", "qg", "sent"] + ["aF%d" % j for j in range(N)] + ["aC%d" % j for j in range(N)]
+              + ["aL%d" % t for t in range(4)] + ["aR%d" % t for t in range(4)] + ["d%d" % i for i in range(NDS)])
+
+
+def bits(es):
+    m = 0
+    for e in es:
+        m |= 1 << e
+    return m
+
+
+def plan(T, topo):
+    cores = list(T.cores)
+    place = [(topo.host(c), topo.chip(c)) for c in cores]
+    big = [r for r in range(N) if place[r] == place[0]]
+    small = [r for r in range(N) if place[r] != place[0]]
+    helpers = [c for c in topo.cores_of(cores[0]) if c not in cores and topo.die(c) != topo.die(cores[0])
+               and all(topo.may_write(c, cores[r]) for r in small)]
+    return cores, big, small, helpers
+
+
+def xfer(topo, src_core, dst_cores, src, dst, sem, engines):
+    ids = []
+    for d in dst_cores:
+        rid, pid = topo.addr(d, src_core)
+        ids.append(DstId(rid=rid, pnc=pid))
+    return RemoteDMATransfer(dst_ids=ids, dma_engine_mask=bits(engines), remote_sem=sem, srcs=[src], dsts=[dst] * len(ids))
+
+
+def helper_program(g, core, T, topo, cores, big, small, helpers):
+    i = helpers.index(core)
+    if i >= len(big) or not RELAY:
+        return
+    r = big[i]
+    dst = cores[small[(i + 1) % 2]]
+    off = topo.engines(core, dst)
+    ap = T.Fw[:, r * Q:(r + 1) * Q]
+    g.wait_ge(T.sem["aF%d" % r], len(off))
+    g.remote_dma_fused([xfer(topo, core, [dst], ap, ap, T.sem["aF%d" % r], off)], local_sem=T.sem.sent)
+    g.wait_ge(T.sem.sent, len(off))
+
+
+def rank_program(g, core, T, topo):
+    cores, big, small, helpers = plan(T, topo)
+    rank = T.rank_of(core)
+    if rank is None:
+        if core in helpers:
+            helper_program(g, core, T, topo, cores, big, small, helpers)
+        return
+
+    V, S, P = g.vector, g.scalar, g.tensor
+    QU = {"v": V, "a": S, "p": P, "g": g, "s": g.sync}
+    cnt = {"v": 0, "a": 0, "p": 0, "g": 0}
+    seen = {q: {} for q in QU}
+    wr, rd, total = {}, {}, {}
+    nd, sent = [0], [0]
+
+    def wait(q, ev):
+        if seen[q].get(ev[0], 0) < ev[1]:
+            QU[q].wait_ge(T.sem[ev[0]], ev[1])
+            seen[q][ev[0]] = ev[1]
+
+    def deps(q, r, w):
+        need = {}
+        own = "q" + q
+        evs = [ev for k in r for ev in wr.get(k, [])]
+        evs += [ev for k in w for ev in wr.get(k, []) + rd.get(k, [])]
+        evs += [ev for k in r if k in BANKS for ev in rd.get(k, []) if ev[0] != own]
+        for ev in evs:
+            need[ev[0]] = max(need.get(ev[0], 0), ev[1])
+        for s_, v_ in need.items():
+            if not (q == "p" and s_ == own):
+                wait(q, (s_, v_))
+
+    def mark(ev, r, w):
+        for k in r:
+            rd.setdefault(k, []).append(ev)
+        for k in w:
+            wr[k] = [ev]
+            rd[k] = []
+        total[ev[0]] = max(total.get(ev[0], 0), ev[1])
+
+    def op(q, fn, r, w, inc=True):
+        deps(q, r, w)
+        ins = fn()
+        if inc:
+            cnt[q] += 1
+            ins.then_inc(T.sem["q" + q], 1)
+            mark(("q" + q, cnt[q]), r, w)
+        else:
+            mark(("q" + q, cnt[q] + 1), r, w)
+
+    def dma(q, out, in_, r, w):
+        deps(q, r, w)
+        s_ = "d%d" % nd[0]
+        nd[0] += 1
+        QU[q].dma_start(out, in_).then_inc(T.sem[s_], 16)
+        mark((s_, 16), r, w)
+
+    def ts(out, in0, s1, op0, r, w, s2=None, op1=None):
+        if op1 is None:
+            op("v", lambda: V.tensor_scalar(out, in0, s1, None, op0), r, w)
+        else:
+            op("v", lambda: V.tensor_scalar(out, in0, s1, s2, op0, op1), r, w)
+
+    def tt(out, a, b, o, r, w):
+        op("v", lambda: V.tensor_tensor(out, a, b, o), r, w)
+
+    def cp(out, in_, r, w):
+        op("v", lambda: V.tensor_copy(out, in_), r, w)
+
+    def ms(ap, val, w):
+        op("v", lambda: V.memset(ap, val), [], w)
+
+    def act(out, in_, r, w, func=AF.Copy, **kw):
+        op("a", lambda: S.activation(out, in_, func, **kw), r, w)
+
+    def aff(out, in_, scale, bias, r, w):
+        act(out, in_, r, w, func=AF.Identity, scale=scale, bias=bias)
+
+    def mm(out, lhsT, rhs, start, stop, r, w, inc=False):
+        op("p", lambda: P.matmul(out, lhsT, rhs, start, stop), r, w, inc)
+
+    def iota(out, pat, base, w):
+        op("g", lambda: g.iota(out, pat, base, 0, allow_small_or_imprecise_dtypes=True), [], w)
+
+    def gather(e, out, win, off_, r, w):
+        if e == "v":
+            cp(out, win.indirect(off_), r, w)
+        else:
+            act(out, win.indirect(off_), r, w)
+
+    def send(trs, r):
+        deps("g", r, [])
+        g.remote_dma_fused([xfer(topo, core, d, a, b, T.sem[s_], es) for d, a, b, s_, es in trs], local_sem=T.sem.sent)
+        sent[0] += sum(len(t_[4]) for t_ in trs)
+
+    FK = ["F%d" % j for j in range(N)] + ["Fpad"]
+    CK = ["C%d" % j for j in range(N)] + ["Cpad"]
+    VK = ["V0", "V1", "V2"]
+    me = slice(rank * Q, (rank + 1) * Q)
+    fme = "F%d" % rank
+
+    dma("s", T.Fw[:, me], T.feat[:], [], [fme])
+    dma("a", T.Cw[:, me], T.nb[:], [], ["C%d" % rank])
+    dma("s", T.hI[:], T.home[:], [], ["hI"])
+    op("g", lambda: g.iota(T.pI[:, 0:1], [[0, 1]], 0, 1), [], ["pI"])
+    iota(T.AR[:], [[1, 192]], 0, ["AR"])
+    iota(T.JG[:], [[1, 8], [0, 16]], 0, ["JG"])
+    iota(T.io2[:, 0:12], [[-256, 3], [-96, 2], [-64, 2]], 1536, ["ioa"])
+    iota(T.io2[:, 12:24], [[-255, 3], [-128, 2], [-64, 2]], 828, ["iob"])
+
+    mine, other = (big, small) if rank in big else (small, big)
+    i = mine.index(rank)
+    peers = [cores[r] for r in mine if r != rank]
+    on = topo.engines(core, peers[0])
+    off = topo.engines(core, cores[other[0]])
+    up = [e for e in on if e not in off]
+    if rank in big:
+        dF = helpers[i] if RELAY else cores[small[(i + 1) % 2]]
+        dC = cores[small[i % 2]]
+        fwd = [("F" if i % 2 == 0 else "C", small[i // 2])]
+    else:
+        dF, dC = cores[big[2 * i]], cores[big[2 * i + 1]]
+        fwd = [("C", r) for j, r in enumerate(big) if j % 2 == i] + [("F", r) for j, r in enumerate(big) if (j + 1) % 2 == i]
+    for j in range(N):
+        if j != rank:
+            for kind in "FC":
+                n_ = len(up) if j in mine else (len(off) if (kind, j) in fwd else len(on))
+                mark(("a%s%d" % (kind, j), n_), [], [("F%d" if kind == "F" else "U%d") % j])
+    a_ = T.Fw[:, me]
+    send([([dF], a_, a_, "aF%d" % rank, off), (peers, a_, a_, "aF%d" % rank, up)], [fme])
+
+    c_ = lambda j: T.col[:, j:j + 1]
+    ts(T.pI[:, 1:2], T.pI[:, 0:1], 15, ALU.bitwise_and, ["pI"], ["pI1"])
+    ts(T.pI[:, 2:3], T.pI[:, 0:1], 4, ALU.arith_shift_right, ["pI"], ["pI2"])
+    ts(T.pI[:, 3:4], T.pI[:, 0:1], 31, ALU.bitwise_and, ["pI"], ["pI3"])
+    ms(T.Fw[:, W:FW], 0.0, ["Fpad"])
+    ms(T.Cw[:, W:CW], 0, ["Cpad"])
+    cp(T.col[:, 0:3], T.pI[:, 0:3], ["pI", "pI1", "pI2"], ["c0"])
+    cp(c_(4), T.pI[:, 3:4], ["pI3"], ["c4"])
+    ms(T.FLO[:], -2047.0 * U23, ["FLO"])
+    ms(T.RS[:], 2.0 ** 24, ["RS"])
+    cp(T.Cu[:, me], T.Cw[:, me], ["C%d" % rank], ["U%d" % rank])
+    a_ = T.Cu[:, me]
+    send([([dC], a_, a_, "aC%d" % rank, off), (peers, a_, a_, "aC%d" % rank, up)], ["U%d" % rank])
+    for kind, j in fwd:
+        a_ = (T.Fw if kind == "F" else T.Cu)[:, j * Q:(j + 1) * Q]
+        send([(peers, a_, a_, "a%s%d" % (kind, j), on)], [("F%d" if kind == "F" else "U%d") % j])
+
+    others = [j for j in mine if j != rank] + [j for k_, j in fwd if k_ == "C"]
+    others += [j for j in other if j not in others]
+
+    def widen(n_):
+        for _ in range(n_):
+            if others:
+                j = others.pop(0)
+                cp(T.Cw[:, j * Q:(j + 1) * Q], T.Cu[:, j * Q:(j + 1) * Q], ["U%d" % j], ["C%d" % j])
+
+    dma("s", T.Tw[0:128:16, 0:W], T.FLO[:], ["FLO"], ["Tw"])
+    ts(T.mK[:], T.AR[:, 0:12], 1024.0, ALU.mult, ["AR"], ["mK"], 4096.0, ALU.add)
+    ts(T.aL[:], T.AR[:, 0:192:16], c_(1), ALU.add, ["AR", "c0"], ["aL"])
+    ts(c_(3), c_(2), 16.0, ALU.mult, ["c0"], ["c3"])
+    ts(c_(5), c_(4), 16.0, ALU.is_lt, ["c4"], ["c5"])
+    ts(c_(6), c_(4), 16.0, ALU.is_ge, ["c4"], ["c6"])
+    ts(c_(7), c_(1), 12.0, ALU.is_lt, ["c0"], ["c7"], 1023.0, ALU.mult)
+    ts(c_(8), c_(1), -64.0 / U23, ALU.mult, ["c0"], ["c8"], 480.5 / U23, ALU.add)
+    tt(T.aK[:], T.aL[:], T.mK[:], ALU.subtract, ["aL", "mK"], ["aK"])
+    ts(T.XP[:], T.AR[:, 0:160], c_(0), ALU.subtract, ["AR", "c0"], ["XP"])
+    ts(T.OH[:], T.AR[:, 0:16], c_(1), ALU.is_equal, ["AR", "c0"], ["OH"])
+    ts(T.BLK[:], T.JG[:], c_(2), ALU.is_equal, ["JG", "c0"], ["BLK"])
+    ts(T.E1[:], T.AR[:, 0:144], c_(3), ALU.subtract, ["AR", "c3"], ["E1"], 15.0, ALU.is_equal)
+    ts(T.BW[:, 0:1], c_(7), 1.0, ALU.add, ["c7"], ["BW"])
+    ts(T.FL[:], T.OH[:, 0:12], -2.0, ALU.mult, ["OH"], ["FL"], 1.0, ALU.add)
+    ts(T.I1[:], T.XP[:, 0:128], 0.0, ALU.is_equal, ["XP"], ["I1"])
+    ts(T.Z[:, 0:160], T.XP[:], 16.0, ALU.is_equal, ["XP", "c5"], ["Z0"], c_(5), ALU.mult)
+    ts(T.Z[:, 160:320], T.XP[:], 16.0, ALU.is_equal, ["XP", "c6"], ["Z1"], c_(6), ALU.mult)
+    tt(c_(11), T.OH[:, 12:13], T.OH[:, 13:14], ALU.add, ["OH"], ["c11"])
+    cp(T.hU[:], T.hI[:], ["hI"], ["hU"])
+    ms(T.UT[:], 1.0, ["UT"])
+    ts(c_(12), c_(11), -3584.0, ALU.mult, ["c11"], ["c12"], 4096.0, ALU.add)
+    ts(c_(13), T.OH[:, 0:1], float(1856 - A * rank), ALU.mult, ["OH", "c11"], ["c13"], c_(11), ALU.add)
+    ts(T.RS[:, 0:192:16], T.io2[:, 0:12], c_(4), ALU.add, ["ioa", "c4", "RS"], ["RSa"], 31.5, ALU.subtract)
+    ts(c_(9), T.OH[:, 15:16], -4096.0, ALU.mult, ["OH", "c12"], ["c9"], c_(12), ALU.add)
+    tt(c_(10), c_(13), T.OH[:, 14:15], ALU.add, ["OH", "c13"], ["c10"])
+    ts(T.RS[:, 192:384:16], T.io2[:, 12:24], 31.5, ALU.subtract, ["iob", "RS"], ["RSb"])
+    ts(T.MC[:], T.AR[:, 0:8], c_(2), ALU.is_equal, ["AR", "c0", "c9"], ["MC"], c_(9), ALU.mult)
+    ts(T.WK1[:], T.BLK[:], c_(10), ALU.mult, ["BLK", "c10"], ["WK1"], -U23, ALU.mult)
+    widen(len(mine) - 1)
+    fill = [lambda: ms(T.St[:], 0.0, ["St"]), lambda: ms(T.M1[:], -1.0, ["M1"]), lambda: ms(T.DUM[:], 0.0, ["DUM"]),
+            lambda: ms(T.ZER[:], 0.0, ["ZER"]), lambda: ms(T.KT[:], 0.0, ["KT0"])]
+    for j in range(12):
+        ts(T.BW[:, 2 ** j:2 ** (j + 1)], T.BW[:, 0:2 ** j], T.FL[:, j:j + 1], ALU.mult, ["BW", "FL"], ["BW"])
+        if j < len(fill):
+            fill[j]()
+    widen(N)
+
+    aff(T.IDL[:], T.AR[:], -1.0, float(2047 - A * rank), ["AR"], ["IDL"])
+    CZ = ["CAz%d" % j for j in range(5)]
+    for j in range(5):
+        n_ = min(Q, 2880 - Q * j)
+        act(T.CA[:, Q * j:Q * j + n_], T.Fw[:, rank * Q:rank * Q + n_], [fme], [CZ[j]], scale=0.0)
+    aff(T.PST[:], T.AR[:], 0.0, c_(8), ["AR", "c8"], ["PST"])
+    act(T.I23[:], T.I1[:], ["I1"], ["I23"], scale=U23)
+    act(T.E2[:], T.E1[:], ["E1"], ["E2"], scale=2048.0)
+    act(T.Z[:, 320:640], T.Z[:, 0:320], ["Z0", "Z1"], ["Z2"], scale=64.0)
+    for h in range(2):
+        aff(T.aT[:, h:12:2], T.AR[:, 0:192:32], 1.0, c_(4), ["AR", "c4"], ["aT%d" % h])
+    aff(T.dumB[:], T.aL[:], 1.0, float(W), ["aL"], ["dumB"])
+    aff(T.dmpK[:], T.aK[:], 1.0, float(2 * A), ["aK"], ["dmpK"])
+    aff(T.idl1[:], T.aL[:], -1.0, float(2048 - A * rank), ["aL"], ["idl1"])
+    aff(T.nbS[:], T.aL[:], 4096.0, -4096.0 * (12 * 2 ** 20 + 191), ["aL"], ["nbS"])
+    aff(T.UT[:, 14:192:16], T.aT[:], -1.0, 191.0, ["aT0", "aT1", "UT"], ["UTs"])
+    aff(T.mK1[:], T.mK[:], 1.0, float(A), ["mK"], ["mK1"])
+    for kk in range(4):
+        for h in range(2):
+            aff(T.K2[:, 12 * h:12 * h + 12, kk], T.aK[:], 1.0, float((4, 2, 1, 0)[kk] * A), ["aK"], ["K2"])
+    act(T.K23[:], T.K2[:], ["K2"], ["K23"], scale=U23)
+    act(T.Ib[:], T.I1[:], ["I1"], ["Ib"])
+    act(T.Nb[:], T.I1[:], ["I1"], ["Nb"], scale=-1.0)
+    for kk in range(1, 4):
+        aff(T.DUM[:, :, kk], T.aL[:], 1.0, float(W + A + (3 - kk) * A), ["aL", "DUM"], ["DUMk"])
+    for s in (1, 2, 3):
+        o_ = 6 * s * (s - 1)
+        act(T.KS[:, o_:o_ + 12 * s], T.K2[:, 0:12, 4 - s:4], ["K2"], ["KS"])
+        act(T.KT[:, o_:o_ + 12 * s:s], T.K2[:, 0:12, 3 - s], ["K2", "KT0"], ["KT"], scale=1.0 / U23)
+    act(T.BLV[:], T.BLK[:], ["BLK"], ["BLV"], scale=-1.0 / U23)
+    act(T.WK2[:], T.WK1[:], ["WK1"], ["WK2"], scale=-1.0 / U23)
+    for j in range(N):
+        act(T.Vw[:, Q * j:Q * j + Q], T.Fw[:, me], [fme], VK, scale=0.0)
+
+    CAc, CA2, CA1 = T.CA[:, 0:960], T.CA[:, 960:1920], T.CA[:, 1920:2880]
+    banks = [T.pb0, T.pb1, T.pb2, T.pb3, T.pb4, T.pb5]
+
+    def parts(t, lst, lk):
+        cp(T.cI[:], T.Cw[:].indirect(lst), CK + [lk], ["cI"])
+        ts(T.chl[:, 0:192], T.cI[:], 63, ALU.bitwise_and, ["cI"], ["clo"])
+        ts(T.chl[:, 192:384], T.cI[:], 6, ALU.arith_shift_right, ["cI"], ["chi"])
+        if t < 2:
+            cp(T.CA[:, t * A:t * A + A], T.cI[:], ["cI"] + CZ, ["CAc"])
+        else:
+            cp(CAc.indirect(T.woU[:]), T.cI[:], ["cI", "woU"], ["CAc"])
+
+    def scores(t):
+        if t < 2:
+            tt(T.CA[:, 960 + t * A:960 + t * A + A], T.pb0[:, 0:192], T.chl[:, 0:192], ALU.add, ["pb0", "clo"] + CZ, ["CA2"])
+            tt(T.CA[:, 1920 + t * A:1920 + t * A + A], T.pb0[:, 0:192], T.chl[:, 192:384], ALU.add, ["pb0", "chi"] + CZ, ["CA1"])
+        else:
+            tt(T.Sn[:, 192:384], T.pb0[:, 0:192], T.chl[:, 192:384], ALU.add, ["pb0", "chi"], ["Sn1"])
+            tt(T.Sn[:, 0:192], T.pb0[:, 0:192], T.chl[:, 0:192], ALU.add, ["pb0", "clo"], ["Sn2"])
+            cp(CA1.indirect(T.woU[:]), T.Sn[:, 192:384], ["Sn1", "woU"], ["CA1"])
+            cp(CA2.indirect(T.woU[:]), T.Sn[:, 0:192], ["Sn2", "woU"], ["CA2"])
+
+    cp(T.cG[:], T.Cw[:].indirect(T.hU[:]), CK + ["hU"], ["cG"])
+    mm(T.pb0[:, 0:192], T.I23[:], T.PST[:], True, False, ["I23", "PST"], ["pb0"])
+    for ch, (lo, hi) in enumerate(((0, 38), (38, 96), (96, 132), (132, 192))):
+        if ch == 2:
+            parts(0, T.hU[:], "hU")
+        gather("va"[ch % 2], T.X[:, 16 * lo:16 * hi], T.Fw[:], T.cG[:, lo:hi], FK + ["cG"], ["X%d" % ch])
+        if ch % 2:
+            a0 = 48 * (ch - 1)
+            for p in range(16):
+                last = ch == 3 and p == 15
+                mm(T.pb0[:, a0:a0 + 96], T.E2[:, 15 - p:143 - p], T.X[:, 16 * a0 + p:16 * a0 + 1536:16], False, last,
+                   ["E2", "X%d" % (ch - 1), "X%d" % ch], ["pb0"], last)
+    aff(T.pS[:, 0:192], T.pb0[:, 0:192], 4.0, -2176.0, ["pb0"], ["pS"])
+    scores(0)
+
+    left, right = (rank - 1) % N, (rank + 1) % N
+    for t in range(1, RO + 1):
+        s = min(t - 1, 3)
+        s1 = min(s, 2) + 1
+        lastr = t == RO
+        if s:
+            n_ = A * s
+            o_ = 6 * s * (s - 1)
+            nl = T.rs[:, s - 1:12 * s:s]
+            hk = CSPLIT[s]
+            cp(T.Vs[:, 0:16 * hk], T.Vw[:].indirect(T.btU[:, 0:hk]), VK + ["btU"], ["Vs0"])
+            act(T.Vs[:, 16 * hk:n_], T.Vw[:].indirect(T.btU[:, hk:12 * s]), VK + ["btU"], ["Vs1"])
+            mm(T.pP[:, 0:12 * s], T.I23[:], T.St[:, 12:24, 4 - s:4], True, False, ["I23", "St"], ["pP"])
+            mm(T.pP[:, 0:12 * s], T.I23[:], T.M1[:, 0:12 * s], False, False, ["M1"], ["pP"])
+            for q in range(16):
+                mm(T.pP[:, 0:12 * s], T.E1[:, 15 - q:143 - q], T.Vs[:, q:n_:16], False, False, ["E1", "Vs0", "Vs1"], ["pP"])
+            mm(T.pP[:, 0:12 * s], T.I23[:], T.KT[:, o_:o_ + 12 * s], False, True, ["KT"], ["pP"], True)
+            wv, wk_ = (T.BLV, "BLV") if lastr else (T.BLK, "BLK")
+            n1 = min(n_, 384)
+            mm(T.pb1[:, 0:n1], wv[:], T.Vs[:, 0:n1], True, True, [wk_, "Vs0", "Vs1"], ["pb1"], True)
+            act(T.kv[:, 0:n1], T.pb1[:, 0:n1], ["pb1"], ["kv0"])
+            if n1 < n_:
+                mm(T.pb2[:, 0:n_ - n1], wv[:], T.Vs[:, n1:n_], True, True, [wk_, "Vs0", "Vs1"], ["pb2"], True)
+                act(T.kv[:, n1:n_], T.pb2[:, 0:n_ - n1], ["pb2"], ["kv1"])
+            op("v", lambda: V.tensor_tensor_scan(T.rs[:, 0:12 * s], T.pP[:, 0:12 * s], T.KS[:, o_:o_ + 12 * s], 0.0, ALU.min, ALU.max),
+               ["pP", "KS"], ["rs"])
+            tt(T.no[:], nl, T.mK[:], ALU.add, ["rs", "mK"], ["no"])
+            cp(T.noU[:], T.no[:], ["no"], ["noU"])
+            cp(T.cU[:], CAc.indirect(T.noU[:]), ["CAc", "noU"], ["cU"])
+            a1, a2 = VSPLIT[s]
+            act(T.Vg[:, 0:16 * a1], T.Vw[:].indirect(T.cU[:, 0:a1]), VK + ["cU"], ["Vg0"])
+            act(T.Vg[:, 16 * a1:16 * a2], T.Vw[:].indirect(T.cU[:, a1:a2]), VK + ["cU"], ["Vg1"])
+            for j in range(2 * s):
+                b0 = 12 * s * (j // s)
+                mm(T.pb3[:, b0 + j % s:b0 + 12 * s:s], T.I23[:], nl, True, True, ["rs"], ["pb3"], j == 2 * s - 1)
+            cp(T.S12[:, 192:384], CA1.indirect(T.noU[:]), ["CA1", "noU"], ["S1"])
+            cp(T.S12[:, 0:192], CA2.indirect(T.noU[:]), ["CA2", "noU"], ["S2"])
+            S2, S1, k2, k1 = T.S12[:, 0:192], T.S12[:, 192:384], "S2", "S1"
+            mm(T.pS[:, 0:192], T.I23[:], T.IDL[:], True, False, ["I23", "IDL"], ["pS"])
+            ts(T.G[:], S1, M2K, ALU.add, [k1], ["G"], M2K, ALU.subtract)
+            mm(T.pS[:, 0:192], T.I23[:], T.G[:], False, False, ["G"], ["pS"])
+            u_ = slice(4 - s, 4)
+            tt(T.kept[:, :, u_], T.pb3[:, 0:24 * s], T.K23[:, :, u_], ALU.is_gt, ["pb3", "K23"], ["kept"])
+            cp(T.Vg[:, 16 * a2:3072], T.Vw[:].indirect(T.cU[:, a2:192]), VK + ["cU"], ["Vg2"])
+            tt(T.dl[:, :, u_], T.dl[:, :, u_], T.kept[:, 0:12, u_], ALU.mult, ["dl", "kept"], ["dl"])
+            tt(T.St[:, :, u_], T.St[:, :, u_], T.kept[:, :, u_], ALU.mult, ["St", "kept"], ["St"])
+            tt(T.ko[:, :, u_], T.dl[:, :, u_], T.DUM[:, :, u_], ALU.add, ["dl", "DUMk"], ["ko"])
+            cp(T.koU[:, 0:12 * s], T.ko[:, :, u_], ["ko"], ["koU"])
+            if not lastr:
+                cp(T.pvU[:], T.ko[:, :, 3], ["ko"], ["pvU"])
+            cp(T.Tw[:].indirect(T.koU[:, 0:12 * s]), T.kv[:, 0:n_], ["koU", "kv0", "kv1"], ["Tw"])
+            for lo, hi, kx in ((0, a1, "Vg0"), (a2, A, "Vg2"), (a1, a2, "Vg1")):
+                for p in range(16):
+                    last = kx == "Vg1" and p == 15
+                    mm(T.pS[:, lo:hi], T.E1[:, 15 - p:143 - p], T.Vg[:, 16 * lo + p:16 * hi:16], False, last,
+                       ["E1", kx], ["pS"], last)
+            if lastr:
+                for k in range(3):
+                    aff(T.yB[:, 12 * k:12 * k + 12], T.kept[:, 0:12, 3 - k], 1.0, -1.0, ["kept"], ["yB%d" % k])
+        else:
+            nl = T.aK[:]
+            S2, S1, k2, k1 = T.CA[:, 960:960 + A], T.CA[:, 1920:1920 + A], "CA2", "CA1"
+        tt(T.sc[:, 0:192], S2, T.pS[:, 0:192], ALU.min, [k2, "pS"], ["sc2"])
+        tt(T.sc[:, 192:384], S1, T.pS[:, 0:192], ALU.min, [k1, "pS"], ["sc1"])
+        op("v", lambda: V.transpose(T.sT[:], T.sc[:]), ["sc1", "sc2"], ["sT"])
+        op("v", lambda: V.tensor_tensor_scan(T.rm[:], T.RS[:], T.sT[:], 2.0 ** 24, ALU.min, ALU.max),
+           ["sT", "RS", "RSa", "RSb"], ["rm"])
+        ts(T.Hh[:], T.rm[:, 15:384:16], M64, ALU.add, ["rm"], ["Hh"], M64, ALU.subtract)
+        ts(T.UT[:, 12:192:16], T.rm[:, 207:384:16], M32K, ALU.add, ["rm", "UT"], ["U12"], M32K, ALU.subtract)
+        tt(T.xx[:], T.rm[:, 15:384:16], T.Hh[:], ALU.subtract, ["rm", "Hh"], ["xx"])
+        ts(T.GT[:], T.rm[:, 207:384:16], M2K, ALU.add, ["rm"], ["GT"], M2K, ALU.subtract)
+        for u in range(2):
+            for h in range(2):
+                o_ = 160 * u + 16 - 16 * (h - u)
+                mm(T.pS[:, 192 + u:204:2], T.Z[:, o_:o_ + 128], T.xx[:, h:12:2], h == 0, False, ["Z0", "Z1", "xx"], ["pS"])
+                mm(T.pS[:, 192 + u:204:2], T.Z[:, 320 + o_:320 + o_ + 128], T.xx[:, 12 + h:24:2], False, h == 1,
+                   ["Z2", "xx"], ["pS"], u == 1 and h == 1)
+        tt(T.UT[:, 13:192:16], T.GT[:], T.UT[:, 12:192:16], ALU.subtract, ["GT", "U12"], ["U13"])
+        ts(T.ctU[:], T.pS[:, 192:204], 2047.5, ALU.add, ["pS"], ["ctU"])
+        op("v", lambda: V.transpose(T.H[:], T.UT[:]), ["U12", "U13", "UTs", "UT"], ["H"])
+        for u in range(2):
+            for h in range(2):
+                o_ = 160 * u + 16 - 16 * (h - u)
+                for j in (12, 13):
+                    mm(T.pP[:, u:12:2], T.Z[:, o_:o_ + 128], T.UT[:, 16 * h + j:192:32], h == 0 and j == 12,
+                       h == 1 and j == 13, ["U12", "U13"], ["pP"], u == 1 and h == 1 and j == 13)
+        cp(T.Bt[:], T.BW[:].indirect(T.ctU[:]), ["BW", "ctU"], ["Bt"])
+        act(T.nb1[:], T.pP[:, 0:12], ["pP"], ["nb1"], scale=-512.0)
+        aff(T.ck[:, 0:12], T.pS[:, 192:204], 1.0, 2047.5, ["pS"], ["ctF"])
+        wk, wkk = (T.WK2, "WK2") if lastr else (T.WK1, "WK1")
+        mm(T.pS[:, 256:448], wk[:], T.H[:], True, True, [wkk, "H"], ["pS"], True)
+        for gq in range(NMV, 8):
+            act(T.Abd[:, :, gq, :], T.Bt[:], ["Bt", "MC"], ["A%d" % gq], func=AF.Identity, scale=T.MC[:, gq:gq + 1])
+        tt(T.B[:], T.Bt[:], T.H[:], ALU.mult, ["Bt", "H"], ["B"])
+        for gq in range(NMV):
+            ts(T.Abd[:, :, gq, :], T.Bt[:], T.MC[:, gq:gq + 1], ALU.mult, ["Bt", "MC"], ["A%d" % gq])
+        tt(T.nbb[:], T.nb1[:], T.nbS[:], ALU.add, ["nb1", "nbS"], ["nbb"])
+        act(T.ktR[:], T.pS[:, 256:448], ["pS"], ["ktR"])
+        if lastr:
+            ts(T.lw[:], T.ck[:, 0:12], 1.0, ALU.add, ["ctF"], ["lw"])
+            for k in range(3):
+                y_ = slice(12 * k, 12 * k + 12)
+                tt(T.yE[:, y_], nl, T.K2[:, 0:12, 3 - k], ALU.is_equal, ["rs", "K2"], ["yE%d" % k])
+        AK = ["A%d" % j for j in range(8)] + ["B"]
+        for b in (3, 0, 4, 1, 5, 2):
+            for j in range(2):
+                mm(banks[b][:, 192 * j:192 * j + 192], T.Abd[:, 2 * b + j, :, :], T.B[:], True, True, AK, ["pb%d" % b], j == 1)
+            for j in range(2):
+                m = 2 * b + j
+                src = banks[b][:, 192 * j:192 * j + 192]
+                if b < 3:
+                    op("v", lambda: V.tensor_reduce(T.Wr[:, m:m + 1], src, AxisListType.X, ALU.max), ["pb%d" % b], ["W%d" % m])
+                else:
+                    act(T.junk[:, A * (m - 6):A * (m - 5)], src, ["pb%d" % b, "nbb"], ["W%d" % m], func=AF.Relu,
+                        bias=T.nbb[:, m:m + 1], accum_out=T.Wr[:, m:m + 1])
+        if 2 <= t < RO:
+            act(T.Mn[:], T.Fw[:].indirect(T.pvU[:]), FK + ["pvU"], ["Mn"])
+        WD = ["W%d" % m for m in range(6)]
+        tt(T.Wr[:, 0:6], T.Wr[:, 0:6], T.nbb[:, 0:6], ALU.add, WD + ["nbb"], WD)
+        tt(T.t12[:], T.Wr[:], T.ck[:, 0:12], ALU.max, ["ctF"] + ["W%d" % m for m in range(12)], ["t12"])
+        if lastr:
+            for k in range(3):
+                y_ = slice(12 * k, 12 * k + 12)
+                ts(T.yW[:, y_], T.t12[:], float(W), ALU.is_lt, ["t12"], ["yW%d" % k])
+                tt(T.yE[:, y_], T.yE[:, y_], T.lw[:], ALU.mult, ["yE%d" % k, "lw"], ["yE%d" % k])
+                tt(T.yB[:, y_], T.yB[:, y_], T.St[:, 0:12, 3 - k], ALU.add, ["yB%d" % k, "St"], ["yB%d" % k])
+            tt(T.yW[:], T.yW[:], T.yE[:], ALU.mult, ["yW0", "yW1", "yW2", "yE0", "yE1", "yE2"], ["yW"])
+        tt(T.oF[:], T.t12[:], T.dumB[:], ALU.min, ["t12", "dumB"], ["oF"])
+        if lastr:
+            tt(T.yL[:], T.yW[:], T.yB[:], ALU.add, ["yW", "yB0", "yB1", "yB2"], ["yL"])
+        cp(T.oU[:], T.oF[:], ["oF"], ["oU"])
+        cp(T.Tw[:].indirect(T.oU[:]), T.ktR[:], ["oU", "ktR", "Tw"], ["Tw"])
+
+        if lastr:
+            dma("s", T.yt[:], T.Tw[0:128:16, 0:W], ["Tw"], ["yt"])
+            for q in range(16):
+                mm(T.pb0[0:8, q:384:16], T.I1[:, q:128:16], T.yL[:, 0:24], True, True, ["yL"], ["pb0"], q == 15)
+            for q in range(16):
+                mm(T.pb1[0:8, q:192:16], T.I1[:, q:128:16], T.yL[:, 24:36], True, True, ["yL"], ["pb1"], q == 15)
+            act(T.yo[0:8, 0:384], T.pb0[0:8, 0:384], ["pb0"], ["yo0"])
+            cp(T.yo[0:8, 384:576], T.pb1[0:8, 0:192], ["pb1"], ["yo1"])
+            dma("a", T.yb[:], T.yo[0:8, :], ["yo0", "yo1"], ["yb"])
+            break
+
+        x = slice(240 * (t - 1), 240 * t)
+        tc = "Tc%d" % t
+        dma("s", T.Tc[:, x], T.Tw[0:128:16, 0:W], ["Tw"], [tc])
+        cl, cr = cores[left], cores[right]
+        el, er = topo.engines(core, cl), topo.engines(core, cr)
+        if len(el) <= len(er):
+            el = el[:len(off)]
+            er = [e for e in er if e not in el]
+        else:
+            el = [e for e in el if e not in er]
+        send([([cl], T.Tc[:, x], T.NR[:, x], "aR%d" % (t - 1), el), ([cr], T.Tc[:, x], T.NL[:, x], "aL%d" % (t - 1), er)], [tc])
+        mark(("aL%d" % (t - 1), len(off)), [], ["NL"])
+        mark(("aR%d" % (t - 1), len(off)), [], ["NR"])
+        dma("s", T.Tw[0:128:16, 0:W], (T.ZER if t == RO - 1 else T.FLO)[:], ["FLO", "ZER"], ["Tw"])
+        (n1, k1_), (n2, k2_) = ((T.NL, "NL"), (T.NR, "NR")) if left in mine else ((T.NR, "NR"), (T.NL, "NL"))
+
+        def near(_):
+            tt(T.pb5[:, 0:240], T.Tc[:, x], n1[:, x], ALU.min, [tc, k1_], ["pb5"])
+
+        def tables(_):
+            tt(T.Vc[:], T.pb5[:, 0:240], n2[:, x], ALU.min, ["pb5", k2_], ["Vc"])
+            ts(T.pb5[:, 256:496], T.Vc[:], MV, ALU.add, ["Vc"], ["pb5"], MV, ALU.subtract)
+            act(T.Pc[:, 0:240], T.Vc[:], ["Vc"], ["P0"])
+            dma("a", T.Vw[0:128:16, :], T.Pc[:, 0:240], ["P0"], ["V0"])
+            tt(T.Pc[:, 480:720], T.Vc[:], T.pb5[:, 256:496], ALU.subtract, ["pb5", "Vc"], ["P2"])
+            tt(T.Pc[:, 240:480], T.pb5[:, 256:496], T.Pc[:, 0:240], ALU.subtract, ["pb5", "P0"], ["P1"])
+            dma("s", T.Vw[2:128:16, :], T.Pc[:, 480:720], ["P2"], ["V2"])
+            dma("a", T.Vw[1:128:16, :], T.Pc[:, 240:480], ["P1"], ["V1"])
+
+        def append1(_):
+            ts(T.lw[:], T.oF[:], float(W), ALU.is_ge, ["oF"], ["lw"], 65536.0, ALU.mult)
+            tt(T.ck[:, 12:24], T.pP[:, 0:12], T.idl1[:], ALU.add, ["pP", "idl1"], ["ktF"])
+            tt(T.nlw[:], nl, T.lw[:], ALU.add, ["rs", "aK", "lw"], ["nlw"])
+            for j in range(2 * s1):
+                b0 = 128 + 12 * s1 * (j // s1)
+                mm(T.pP[:, b0 + j % s1:b0 + 12 * s1:s1], T.I23[:], T.nlw[:], True, True, ["nlw"], ["pP"])
+            for j in range(s1):
+                mm(T.pP[:, 256 + j:256 + 24 * s1:s1], T.I1[:], T.ck[:], True, True, ["ctF", "ktF", "I1"], ["pP"], j == s1 - 1)
+            if t >= 2:
+                tt(T.t12[:], T.nlw[:], T.dmpK[:], ALU.min, ["nlw", "dmpK"], ["t12"])
+                tt(T.no[:], T.t12[:], T.mK1[:], ALU.add, ["t12", "mK1"], ["no"])
+                cp(T.woU[:], T.no[:], ["no"], ["woU"])
+
+        def append2(_):
+            v_ = slice(4 - s1, 4)
+            tt(T.ee[:, 0:24 * s1], T.pP[:, 128:128 + 24 * s1], T.K23[:, :, v_], ALU.is_equal, ["pP", "K23"], ["ee"])
+            tt(T.ee[:, 0:24 * s1], T.ee[:, 0:24 * s1], T.pP[:, 256:256 + 24 * s1], ALU.mult, ["ee", "pP"], ["ee"])
+            tt(T.St[:, :, v_], T.St[:, :, v_], T.ee[:, 0:24 * s1], ALU.add, ["St", "ee"], ["St"])
+            cp(T.btU[:, 0:12 * s1], T.St[:, 0:12, v_], ["St"], ["btU"])
+            tt(T.dl[:, :, v_], T.St[:, 0:12, v_], T.DUM[:, :, v_], ALU.subtract, ["St", "DUMk"], ["dl"])
+
+        cp(T.cG[:], T.Cw[:].indirect(T.ctU[:]), CK + ["ctU"], ["cG"])
+        if t == 1:
+            cp(T.Mw[:], T.Fw[:].indirect(T.ctU[:]), FK + ["ctU"], ["Mw"])
+        else:
+            tt(T.Mw[:], T.Fw[:].indirect(T.ctU[:]), T.Mn[:], ALU.max, FK + ["ctU", "Mn"], ["Mw"])
+
+        def gat(ch):
+            gather(GENG[ch], T.Fg[:, 1024 * ch:1024 * ch + 1024], T.Fw[:], T.cG[:, 64 * ch:64 * ch + 64], FK + ["cG"], ["Fg%d" % ch])
+
+        def sub(ch):
+            for p in range(16):
+                b = 1 + (2 * ch + p // 8) % 4
+                o = banks[b][:, 64 * (p % 8):64 * (p % 8) + 64]
+                mm(o, T.Nb[:], T.Mw[:, 64 * ch:64 * ch + 64], True, False, ["Nb", "Mw"], ["pb%d" % b])
+                mm(o, T.Ib[:], T.Fg[:, 1024 * ch + p:1024 * ch + 1024:16], False, True, ["Ib", "Fg%d" % ch], ["pb%d" % b], p % 8 == 7)
+
+        def clip(ch):
+            for h in range(2):
+                b = 1 + (2 * ch + h) % 4
+                o = T.X[:, 1024 * ch + 512 * h:1024 * ch + 512 * h + 512]
+                xk = ["X%d" % (2 * ch + h)]
+                if RENG[2 * ch + h] == "a":
+                    act(o, banks[b][:], ["pb%d" % b], xk, func=AF.Relu)
+                else:
+                    ts(o, banks[b][:], 0.0, ALU.max, ["pb%d" % b], xk)
+
+        def tot(ch):
+            for p in range(16):
+                last = ch == 2 and p == 15
+                mm(T.pb0[:, 64 * ch:64 * ch + 64], T.E2[:, 15 - p:143 - p], T.X[:, 1024 * ch + 64 * p:1024 * ch + 64 * p + 64],
+                   False, last, ["E2", "X%d" % (2 * ch + p // 8)], ["pb0"], last)
+
+        steps = {"g": gat, "s": sub, "c": clip, "t": tot, "A": append1, "B": append2, "N": near, "T": tables,
+                 "P": lambda _: parts(t, T.ctU[:], "ctU"), "S": lambda _: scores(t),
+                 "I": lambda _: mm(T.pb0[:, 0:192], T.I23[:], T.PST[:], True, False, ["I23", "PST"], ["pb0"])}
+        for st in ORDER.split():
+            steps[st[0]](int(st[1:] or 0))
+
+    total["sent"] = sent[0]
+    for s_, v_ in total.items():
+        wait("g", (s_, v_))

@@ -3,41 +3,58 @@ from concourse.mybir import AluOpType as ALU, AxisListType, ActivationFunctionTy
 
 N, Q, A, RO = 6, 640, 192, 5
 W = N * Q
-U23 = float(2 ** 23)
-M64 = 1.5 * 2.0 ** 29
-M2K = 1.5 * 2.0 ** 34
-M32K = 1.5 * 2.0 ** 38
-MV = 1.5 * 2.0 ** 54
-FW, CW, TW = 4224, 4032, 4608
-RELAY = True
-GENG = "aav"
-RENG = "aaaaaa"
-ORDER = "g0 g1 A I s0 P g2 B c0 s1 c1 s2 t0 c2 t1 t2 N T S"
+U24 = float(2 ** 24)
+BIG = 65536.0
+M16 = 1.5 * 2.0 ** 27
+M256 = 1.5 * 2.0 ** 31
+M1K = 1.5 * 2.0 ** 33
+SAME = 12.0 * BIG
+VW, TW = 4096, 4032
+SPLIT = 528
+ORDER = "B a0:64 M v64:104 I a104:128 a128:192 A x0:128 t0:128 r128:192 N T z128:192 S C Y"
+LISTS = False
+FKEEP = "aaa"
+FBID = "v"
 NMV = 4
-CSPLIT = {1: 6, 2: 12, 3: 18}
-VSPLIT = {1: (64, 128), 2: (76, 152), 3: (86, 172)}
+CSPLIT = {1: 12, 2: 18, 3: 24, 4: 30}
+VP0 = "a0:32 v32:64 m0:64 a64:96 v96:128 m64:128 a128:160 v160:192 M128:192 C"
+VP1 = "a0:40 P v40:64 m0:64 a64:96 v96:128 m64:128 a128:164 v164:192 M128:192 K k0"
+VP2 = "a0:40 P v40:64 m0:64 a64:96 v96:128 m64:128 a128:164 v164:192 M128:192 K k0 k1"
+VP3 = "a0:40 P v40:64 m0:64 a64:96 v96:128 m64:128 K a128:176 v176:192 M128:192 k0 k1 k2"
+VP4 = "a0:40 P v40:64 m0:64 a64:96 v96:128 m64:128 K a128:192 M128:192 e0 k1 k2 k3 Y"
+VPLAN = (VP0, VP1, VP2, VP3, VP4)
+EARLY = False
+
+
+def spans(plan_):
+    return [(w_[0], int(w_[1:].split(":")[0] or 0), int(w_[1:].split(":")[-1] or 0)) for w_ in plan_.split()]
+
+
+def over(name, plan_, lo, hi):
+    return [name + str(a) for e, a, b in spans(plan_) if e in "av" and a < hi and b > lo]
+
 
 f32, bf, i32, u16 = "float32", "bfloat16", "int32", "uint16"
 SB = {
-    bf: dict(Fw=FW, Vw=W, BW=4096, E1=144, E2=144, Z=640, BLK=128, BLV=128, Ib=128, Nb=128, WK1=128, WK2=128, UT=192,
-             Vs=576, Vg=3072, xx=24, H=192, Bt=192, B=192, junk=1152, Mn=192, Mw=192, Fg=3072, X=3072, Pc=720),
-    u16: dict(Cu=W, hU=12, btU=36, koU=36, pvU=12, noU=12, cU=192, ctU=12, oU=12, woU=12, cG=192),
-    i32: dict(Cw=CW, hI=12, pI=4, cI=192, chl=384),
-    f32: dict(Tw=TW, CA=2880, col=16, AR=192, JG=128, XP=160, I23=128, I1=128, MC=8, FL=12, OH=16, io2=24, IDL=192, PST=192,
-              RS=384, aL=12, aT=12, aK=12, mK=12, mK1=12, no=12, t12=12, KS=72, KT=72, M1=36, dumB=12, dmpK=12, idl1=12,
-              nbS=12, FLO=240, ZER=240, rs=36, kv=576, S12=384, G=192, sc=384, sT=384, rm=384, Hh=24, GT=12, ck=24, nb1=12,
-              nbb=12, Wr=12, oF=12, ktR=192, lw=12, nlw=12, ee=72, Sn=384, Tc=960, NL=960, NR=960, Vc=240,
-              yL=36, yB=36, yE=36, yW=36, yo=576),
+    bf: dict(Fw=W, Vw=VW, E1=160, ES=152, EG=160, EV=160, E16=160, EW=160, Z=320, BLK=128, Ib=128, Nb=128, WK=128, UT=192,
+             PST=192, MCb=8, MKb=8, SL=480, Vs=960, Vg=3072, xx=12, H=192, Bt=192, B=192, junk=1152, Mn=192, CM=1152,
+             Fg=3072, X=3072, Pc=720, NB16=128, UF=192, HF=192, WF=128),
+    u16: dict(Cu=W, hU=12, btU=60, koU=240, koF=192, noU=12, cU=192, ctU=12, oU=80, oF=64, poU=12, cG=192),
+    i32: dict(Cw=W, hI=12, pI=8, CC=1152),
+    f32: dict(Tw=TW, Tf=TW, KF=768, CS=1152, KR=960, col=24, AR=192, JG=128, XG=160, XP=160, I24=128, MC=8, FL=12, EQ=12, RJ=12, P2=12, OH=16,
+              CD=192, RS=192, R5=180, PC=60, aL=12, aT=12, aLt=48, C16=12, CG=12, CT=12, CK=12, t12=12, ZER=240, rs=60,
+              S1=192, sc=192, sT=192, rm=192, Hh=12, ck=12, nbb=12, nob=12, Wr=12, x1=12, x2=12, x3=12, AL=60, nn=60, Sr=80,
+              Tc=960, NL=960, NR=960, Vc=240, X1=60, YQ=180, YS=180, yL=36, yB=36, yE=36, yW=36, yo=576),
 }
 SCRATCH = {n_: ("sbuf", [128, c_], d_) for d_, t_ in SB.items() for n_, c_ in t_.items()}
-SCRATCH.update({n_: ("sbuf", [128, 24, 4], f32) for n_ in ("K2", "K23", "St", "kept")})
-SCRATCH.update({n_: ("sbuf", [128, 12, 4], f32) for n_ in ("DUM", "dl", "ko")})
+SCRATCH.update({n_: ("sbuf", [128, 12, 5], f32) for n_ in ("ST", "PW", "KW", "DUM", "Zk", "NS")})
 SCRATCH["Abd"] = ("sbuf", [128, 12, 8, 16], bf)
 BANKS = ["pb0", "pb1", "pb2", "pb3", "pb4", "pb5", "pS", "pP"]
 SCRATCH.update({n_: ("psum", [128, 512], f32) for n_ in BANKS})
-NDS = 32
-SEMAPHORES = (["qv", "qa", "qp", "qg", "sent"] + ["aF%d" % j for j in range(N)] + ["aC%d" % j for j in range(N)]
-              + ["aL%d" % t for t in range(4)] + ["aR%d" % t for t in range(4)] + ["d%d" % i for i in range(NDS)])
+NDS = 48
+SEMAPHORES = (["qv", "qa", "qp", "qg", "sent"] + ["a%s%d%d" % (k_, j, h) for k_ in "FC" for j in range(N) for h in range(2)]
+              + ["aS%d" % j for j in range(N)]
+              + ["a%s%d" % (k_, t) for k_ in "LRGKO" for t in range(4)] + ["d%d" % i for i in range(NDS)])
 
 
 def bits(es):
@@ -52,9 +69,13 @@ def plan(T, topo):
     place = [(topo.host(c), topo.chip(c)) for c in cores]
     big = [r for r in range(N) if place[r] == place[0]]
     small = [r for r in range(N) if place[r] != place[0]]
-    helpers = [c for c in topo.cores_of(cores[0]) if c not in cores and topo.die(c) != topo.die(cores[0])
-               and all(topo.may_write(c, cores[r]) for r in small)]
-    return cores, big, small, helpers
+    helper = {}
+    for mine, other in ((big, small), (small, big)):
+        c0 = cores[mine[0]]
+        free = [c for c in topo.cores_of(c0) if c not in cores and topo.die(c) != topo.die(c0)
+                and all(topo.may_write(c, cores[r]) for r in other)]
+        helper.update(zip(mine, free))
+    return cores, big, small, helper
 
 
 def xfer(topo, src_core, dst_cores, src, dst, sem, engines):
@@ -65,25 +86,41 @@ def xfer(topo, src_core, dst_cores, src, dst, sem, engines):
     return RemoteDMATransfer(dst_ids=ids, dma_engine_mask=bits(engines), remote_sem=sem, srcs=[src], dsts=[dst] * len(ids))
 
 
-def helper_program(g, core, T, topo, cores, big, small, helpers):
-    i = helpers.index(core)
-    if i >= len(big) or not RELAY:
-        return
-    r = big[i]
-    dst = cores[small[(i + 1) % 2]]
-    off = topo.engines(core, dst)
-    ap = T.Fw[:, r * Q:(r + 1) * Q]
-    g.wait_ge(T.sem["aF%d" % r], len(off))
-    g.remote_dma_fused([xfer(topo, core, [dst], ap, ap, T.sem["aF%d" % r], off)], local_sem=T.sem.sent)
-    g.wait_ge(T.sem.sent, len(off))
+def span(big, kind, r, h):
+    mid = SPLIT if kind == "C" and r in big else Q // 2
+    return slice(r * Q + mid * h, r * Q + (Q if h else mid))
+
+
+def piece(T, big, kind, r, h):
+    return (T.Fw if kind == "F" else T.Cu)[:, span(big, kind, r, h)]
+
+
+def helper_program(g, core, T, topo, cores, big, small, r):
+    far = [cores[j] for j in (small if r in big else big)]
+    off = topo.engines(core, far[0])
+    n4 = len(off) // 2
+    ap = T.SL[:, 80 * r:80 * r + 80]
+    sem = T.sem["aS%d" % r]
+    g.wait_ge(sem, n4)
+    g.remote_dma_fused([xfer(topo, core, far[h::2], ap, ap, sem, off[h::2]) for h in range(2)], local_sem=T.sem.sent)
+    sent = 2 * n4
+    if r in big:
+        for kind, dst, es in (("C", far, off[0::2]), ("F", [far[(big.index(r) + 1) % 2]], off[1::2])):
+            ap = piece(T, big, kind, r, 1)
+            sem = T.sem["a%s%d1" % (kind, r)]
+            g.wait_ge(sem, n4)
+            g.remote_dma_fused([xfer(topo, core, dst, ap, ap, sem, es)], local_sem=T.sem.sent)
+            sent += n4
+    g.wait_ge(T.sem.sent, sent)
 
 
 def rank_program(g, core, T, topo):
-    cores, big, small, helpers = plan(T, topo)
+    cores, big, small, helper = plan(T, topo)
     rank = T.rank_of(core)
     if rank is None:
-        if core in helpers:
-            helper_program(g, core, T, topo, cores, big, small, helpers)
+        for r, c in helper.items():
+            if c == core:
+                helper_program(g, core, T, topo, cores, big, small, r)
         return
 
     V, S, P = g.vector, g.scalar, g.tensor
@@ -150,6 +187,12 @@ def rank_program(g, core, T, topo):
     def ms(ap, val, w):
         op("v", lambda: V.memset(ap, val), [], w)
 
+    def scan(out, d0, d1, init, op0, op1, r, w):
+        op("v", lambda: V.tensor_tensor_scan(out, d0, d1, init, op0, op1), r, w)
+
+    def rnd(out, in_, m, r, w):
+        ts(out, in_, m, ALU.add, r, w, m, ALU.subtract)
+
     def act(out, in_, r, w, func=AF.Copy, **kw):
         op("a", lambda: S.activation(out, in_, func, **kw), r, w)
 
@@ -168,25 +211,33 @@ def rank_program(g, core, T, topo):
         else:
             act(out, win.indirect(off_), r, w)
 
+    def put(e, win, off_, in_, r, wk):
+        if e == "a":
+            act(win[:].indirect(off_), in_, r, [wk], func=AF.Silu)
+        else:
+            cp(win[:].indirect(off_), in_, r, [wk])
+
     def send(trs, r):
         deps("g", r, [])
         g.remote_dma_fused([xfer(topo, core, d, a, b, T.sem[s_], es) for d, a, b, s_, es in trs], local_sem=T.sem.sent)
         sent[0] += sum(len(t_[4]) for t_ in trs)
 
-    FK = ["F%d" % j for j in range(N)] + ["Fpad"]
-    CK = ["C%d" % j for j in range(N)] + ["Cpad"]
+    def row(E, q):
+        return E[:, 23 - q:151 - q]
+
+    FK = ["F%d%d" % (j, h) for j in range(N) for h in range(2)]
+    CK = ["C%d%d" % (j, h) for j in range(N) for h in range(2)]
     VK = ["V0", "V1", "V2"]
     me = slice(rank * Q, (rank + 1) * Q)
-    fme = "F%d" % rank
+    fme = "F%d0" % rank
 
     dma("s", T.Fw[:, me], T.feat[:], [], [fme])
-    dma("a", T.Cw[:, me], T.nb[:], [], ["C%d" % rank])
-    dma("s", T.hI[:], T.home[:], [], ["hI"])
+    dma("s", T.Cw[:, me], T.nb[:], [], ["C%d0" % rank])
+    dma("a", T.hI[:], T.home[:], [], ["hI"])
     op("g", lambda: g.iota(T.pI[:, 0:1], [[0, 1]], 0, 1), [], ["pI"])
+    iota(T.RJ[:], [[4, 4], [1, 3]], 1, ["RJ"])
     iota(T.AR[:], [[1, 192]], 0, ["AR"])
     iota(T.JG[:], [[1, 8], [0, 16]], 0, ["JG"])
-    iota(T.io2[:, 0:12], [[-256, 3], [-96, 2], [-64, 2]], 1536, ["ioa"])
-    iota(T.io2[:, 12:24], [[-255, 3], [-128, 2], [-64, 2]], 828, ["iob"])
 
     mine, other = (big, small) if rank in big else (small, big)
     i = mine.index(rank)
@@ -194,259 +245,305 @@ def rank_program(g, core, T, topo):
     on = topo.engines(core, peers[0])
     off = topo.engines(core, cores[other[0]])
     up = [e for e in on if e not in off]
+    offC, offS = off[0::2], off[1::2]
+    upA, upB = up[0::2], up[1::2]
+    n4 = len(offC)
+    left, right = (rank - 1) % N, (rank + 1) % N
+    close = [j for j in (left, right) if j in mine]
+    far = ([j for j in (left, right) if j in other] + [None])[0]
+    if not LISTS:
+        close, far = sorted((left, right), key=lambda j: j in other), None
+    key = lambda kind, j, h: "%s%d%d" % ("F" if kind == "F" else "U", j, h)
     if rank in big:
-        dF = helpers[i] if RELAY else cores[small[(i + 1) % 2]]
-        dC = cores[small[i % 2]]
-        fwd = [("F" if i % 2 == 0 else "C", small[i // 2])]
+        fwd = [(kind, small[i // 2], i % 2) for kind in "CF"]
     else:
-        dF, dC = cores[big[2 * i]], cores[big[2 * i + 1]]
-        fwd = [("C", r) for j, r in enumerate(big) if j % 2 == i] + [("F", r) for j, r in enumerate(big) if (j + 1) % 2 == i]
+        fwd = [("C", r, 0) for r in big[i::2]] + [("F", r, 0) for r in big[i::2]] + [("F", r, 1) for r in big[1 - i::2]]
     for j in range(N):
         if j != rank:
+            mark(("aS%d" % j, n4), [], ["SL%d" % j])
             for kind in "FC":
-                n_ = len(up) if j in mine else (len(off) if (kind, j) in fwd else len(on))
-                mark(("a%s%d" % (kind, j), n_), [], [("F%d" if kind == "F" else "U%d") % j])
-    a_ = T.Fw[:, me]
-    send([([dF], a_, a_, "aF%d" % rank, off), (peers, a_, a_, "aF%d" % rank, up)], [fme])
+                for h in range(2):
+                    if j in mine and rank in big:
+                        mark(("a%s%d0" % (kind, j), len(up)), [], [key(kind, j, h)])
+                        continue
+                    n_ = n4
+                    if j in other and rank in big and (kind, j, h) in fwd:
+                        n_ = n4 // 2
+                    elif j in other and rank in small and kind == "C" and h == 0 and (kind, j, h) not in fwd:
+                        n_ = len(up)
+                    mark(("a%s%d%d" % (kind, j, h), n_), [], [key(kind, j, h)])
 
     c_ = lambda j: T.col[:, j:j + 1]
-    ts(T.pI[:, 1:2], T.pI[:, 0:1], 15, ALU.bitwise_and, ["pI"], ["pI1"])
-    ts(T.pI[:, 2:3], T.pI[:, 0:1], 4, ALU.arith_shift_right, ["pI"], ["pI2"])
-    ts(T.pI[:, 3:4], T.pI[:, 0:1], 31, ALU.bitwise_and, ["pI"], ["pI3"])
-    ms(T.Fw[:, W:FW], 0.0, ["Fpad"])
-    ms(T.Cw[:, W:CW], 0, ["Cpad"])
-    cp(T.col[:, 0:3], T.pI[:, 0:3], ["pI", "pI1", "pI2"], ["c0"])
-    cp(c_(4), T.pI[:, 3:4], ["pI3"], ["c4"])
-    ms(T.FLO[:], -2047.0 * U23, ["FLO"])
-    ms(T.RS[:], 2.0 ** 24, ["RS"])
-    cp(T.Cu[:, me], T.Cw[:, me], ["C%d" % rank], ["U%d" % rank])
-    a_ = T.Cu[:, me]
-    send([([dC], a_, a_, "aC%d" % rank, off), (peers, a_, a_, "aC%d" % rank, up)], ["U%d" % rank])
-    for kind, j in fwd:
-        a_ = (T.Fw if kind == "F" else T.Cu)[:, j * Q:(j + 1) * Q]
-        send([(peers, a_, a_, "a%s%d" % (kind, j), on)], [("F%d" if kind == "F" else "U%d") % j])
+    o_ = lambda j: T.OH[:, j:j + 1]
+    for j, (v_, o) in enumerate(((15, ALU.bitwise_and), (4, ALU.arith_shift_right), (31, ALU.bitwise_and), (3, ALU.bitwise_and))):
+        ts(T.pI[:, j + 1:j + 2], T.pI[:, 0:1], v_, o, ["pI"], ["pI%d" % j])
+    cp(T.col[:, 0:5], T.pI[:, 0:5], ["pI", "pI0", "pI1", "pI2", "pI3"], ["c0"])
+    ms(T.ZER[:], 0.0, ["ZER"])
+    ts(T.EQ[:], T.RJ[:], c_(1), ALU.is_equal, ["RJ", "c0"], ["EQ"])
+    ts(c_(6), c_(4), 0.0, ALU.not_equal, ["c0"], ["c6"])
+    ts(c_(5), c_(2), 16.0, ALU.mult, ["c0"], ["c5"])
+    ts(T.FL[:], T.EQ[:], -2.0, ALU.mult, ["EQ"], ["FL"], 1.0, ALU.add)
+    cp(T.Vw[:, 0:1], c_(6), ["c6"], VK)
+    ts(T.E1[:], T.AR[:, 0:160], c_(5), ALU.subtract, ["AR", "c5"], ["E1"], 23.0, ALU.is_equal)
 
-    others = [j for j in mine if j != rank] + [j for k_, j in fwd if k_ == "C"]
-    others += [j for j in other if j not in others]
+    def double(j0, j1):
+        for j in range(j0, j1):
+            ts(T.Vw[:, 2 ** j:2 ** (j + 1)], T.Vw[:, 0:2 ** j], T.FL[:, j:j + 1], ALU.mult, VK + ["FL"], VK)
 
-    def widen(n_):
-        for _ in range(n_):
-            if others:
-                j = others.pop(0)
-                cp(T.Cw[:, j * Q:(j + 1) * Q], T.Cu[:, j * Q:(j + 1) * Q], ["U%d" % j], ["C%d" % j])
+    double(0, 1)
+    tt(T.ES[:], T.E1[:, 0:152], T.E1[:, 8:160], ALU.add, ["E1"], ["ES"])
+    double(1, 9)
+    dma("s", T.Tw[0:128:16, 0:W], T.ZER[:], ["ZER"], ["Tw"])
 
-    dma("s", T.Tw[0:128:16, 0:W], T.FLO[:], ["FLO"], ["Tw"])
-    ts(T.mK[:], T.AR[:, 0:12], 1024.0, ALU.mult, ["AR"], ["mK"], 4096.0, ALU.add)
-    ts(T.aL[:], T.AR[:, 0:192:16], c_(1), ALU.add, ["AR", "c0"], ["aL"])
-    ts(c_(3), c_(2), 16.0, ALU.mult, ["c0"], ["c3"])
-    ts(c_(5), c_(4), 16.0, ALU.is_lt, ["c4"], ["c5"])
-    ts(c_(6), c_(4), 16.0, ALU.is_ge, ["c4"], ["c6"])
-    ts(c_(7), c_(1), 12.0, ALU.is_lt, ["c0"], ["c7"], 1023.0, ALU.mult)
-    ts(c_(8), c_(1), -64.0 / U23, ALU.mult, ["c0"], ["c8"], 480.5 / U23, ALU.add)
-    tt(T.aK[:], T.aL[:], T.mK[:], ALU.subtract, ["aL", "mK"], ["aK"])
-    ts(T.XP[:], T.AR[:, 0:160], c_(0), ALU.subtract, ["AR", "c0"], ["XP"])
+    sl = slice(80 * rank, 80 * rank + 80)
+    for E, b in ((T.ES, "pb0"), (T.E1, "pb1")):
+        for h in range(8):
+            mm(T[b][:, 0:80], E[:, 15 - h:143 - h], T.Fw[:, rank * Q + 80 * h:rank * Q + 80 * h + 80], h == 0, h == 7,
+               ["ES", "E1", fme], [b], h == 7)
+    rnd(T.Sr[:], T.pb0[:, 0:80], M16, ["pb0"], ["Sr"])
+    tt(T.SL[:, sl], T.Sr[:], T.pb1[:, 0:80], ALU.subtract, ["Sr", "pb1"], ["SL%d" % rank])
+    cp(T.Cu[:, me], T.Cw[:, me], ["C%d0" % rank], ["U"])
+    a_ = T.SL[:, sl]
+    send([([helper[rank]], a_, a_, "aS%d" % rank, offS), (peers, a_, a_, "aS%d" % rank, upA)], ["SL%d" % rank])
+
+    def part(dst, kind, j, h, es):
+        a_ = piece(T, big, kind, j, h)
+        return (dst, a_, a_, "a%s%d%d" % (kind, j, h), es)
+
+    def whole(kind):
+        a_ = (T.Fw if kind == "F" else T.Cu)[:, me]
+        send([(peers, a_, a_, "a%s%d0" % (kind, rank), up)], [fme, "U"])
+
+    if rank in big:
+        near_, far_ = [helper[rank]], [cores[small[i % 2]]]
+        send([part(near_, "C", rank, 1, upB)], ["U"])
+        send([part(far_, "C", rank, 0, offC)], ["U"])
+        whole("C")
+        send([part(far_, "F", rank, 0, offC), part(near_, "F", rank, 1, offS)], [fme])
+        for kind, j, h in fwd:
+            send([part([d], kind, j, h, es) for d, es in zip(peers, (upA, upB, offS))], [key(kind, j, h)])
+            if kind == "C":
+                whole("F")
+    else:
+        for kind in "CF":
+            send([part([cores[big[2 * i + h]]], kind, rank, h, offC[2 * h:2 * h + 2]) for h in range(2)]
+                 + [part(peers, kind, rank, h, (upA, upB)[h]) for h in range(2)], [fme, "U"])
+        for c in fwd[0:2]:
+            send([part(peers, *c, up)], [key(*c)])
+        for cs in (fwd[2:4], fwd[4:6]):
+            send([part(peers, *c, es) for c, es in zip(cs, (upA, upB))], [key(*c) for c in cs])
+    double(9, 12)
+    for j in [rank] + [j for j in mine if j != rank] + other:
+        dma("s", T.Vw[0:128:8, j * Q:(j + 1) * Q], T.SL[:, 80 * j:80 * j + 80], ["SL%d" % j, "V0"], ["S%d" % j])
+    SK = ["S%d" % j for j in range(N)]
+
+    parts = [("C", j, h) for j in mine if j != rank for h in range(2)] + [c for c in fwd if c[0] == "C"]
+    parts += [("C", j, h) for h in (1, 0) for j in other if ("C", j, h) not in parts]
+
+    def widen():
+        for c in parts:
+            cp(T.Cw[:, span(big, *c)], T.Cu[:, span(big, *c)], [key(*c)], ["C%d%d" % c[1:]])
+
     ts(T.OH[:], T.AR[:, 0:16], c_(1), ALU.is_equal, ["AR", "c0"], ["OH"])
-    ts(T.BLK[:], T.JG[:], c_(2), ALU.is_equal, ["JG", "c0"], ["BLK"])
-    ts(T.E1[:], T.AR[:, 0:144], c_(3), ALU.subtract, ["AR", "c3"], ["E1"], 15.0, ALU.is_equal)
-    ts(T.BW[:, 0:1], c_(7), 1.0, ALU.add, ["c7"], ["BW"])
-    ts(T.FL[:], T.OH[:, 0:12], -2.0, ALU.mult, ["OH"], ["FL"], 1.0, ALU.add)
-    ts(T.I1[:], T.XP[:, 0:128], 0.0, ALU.is_equal, ["XP"], ["I1"])
-    ts(T.Z[:, 0:160], T.XP[:], 16.0, ALU.is_equal, ["XP", "c5"], ["Z0"], c_(5), ALU.mult)
-    ts(T.Z[:, 160:320], T.XP[:], 16.0, ALU.is_equal, ["XP", "c6"], ["Z1"], c_(6), ALU.mult)
-    tt(c_(11), T.OH[:, 12:13], T.OH[:, 13:14], ALU.add, ["OH"], ["c11"])
+    ts(T.aL[:], T.AR[:, 0:192:16], c_(1), ALU.add, ["AR", "c0"], ["aL"])
+    ts(T.XP[:], T.AR[:, 0:160], c_(0), ALU.subtract, ["AR", "c0"], ["XP"])
+    ts(c_(7), c_(3), 16.0, ALU.is_lt, ["c0"], ["c7"])
+    ts(c_(8), c_(3), 16.0, ALU.is_ge, ["c0"], ["c8"])
+    tt(c_(9), o_(0), o_(8), ALU.add, ["OH"], ["c9"])
+    ts(c_(10), o_(4), 4096.0, ALU.mult, ["OH"], ["c10"])
+    ts(c_(11), o_(0), o_(8), ALU.subtract, ["OH"], ["c11"], 16.0, ALU.mult)
+    ts(c_(16), c_(1), -1.0, ALU.mult, ["c0"], ["c16"], 7.5, ALU.add)
+    ts(c_(17), c_(1), (1087.0 - A * rank) / 128.0, ALU.add, ["c0"], ["c17"])
+    ms(T.X1[:, 0:12], 2.0, ["X1"])
     cp(T.hU[:], T.hI[:], ["hI"], ["hU"])
-    ms(T.UT[:], 1.0, ["UT"])
-    ts(c_(12), c_(11), -3584.0, ALU.mult, ["c11"], ["c12"], 4096.0, ALU.add)
-    ts(c_(13), T.OH[:, 0:1], float(1856 - A * rank), ALU.mult, ["OH", "c11"], ["c13"], c_(11), ALU.add)
-    ts(T.RS[:, 0:192:16], T.io2[:, 0:12], c_(4), ALU.add, ["ioa", "c4", "RS"], ["RSa"], 31.5, ALU.subtract)
-    ts(c_(9), T.OH[:, 15:16], -4096.0, ALU.mult, ["OH", "c12"], ["c9"], c_(12), ALU.add)
-    tt(c_(10), c_(13), T.OH[:, 14:15], ALU.add, ["OH", "c13"], ["c10"])
-    ts(T.RS[:, 192:384:16], T.io2[:, 12:24], 31.5, ALU.subtract, ["iob", "RS"], ["RSb"])
-    ts(T.MC[:], T.AR[:, 0:8], c_(2), ALU.is_equal, ["AR", "c0", "c9"], ["MC"], c_(9), ALU.mult)
-    ts(T.WK1[:], T.BLK[:], c_(10), ALU.mult, ["BLK", "c10"], ["WK1"], -U23, ALU.mult)
-    widen(len(mine) - 1)
-    fill = [lambda: ms(T.St[:], 0.0, ["St"]), lambda: ms(T.M1[:], -1.0, ["M1"]), lambda: ms(T.DUM[:], 0.0, ["DUM"]),
-            lambda: ms(T.ZER[:], 0.0, ["ZER"]), lambda: ms(T.KT[:], 0.0, ["KT0"])]
-    for j in range(12):
-        ts(T.BW[:, 2 ** j:2 ** (j + 1)], T.BW[:, 0:2 ** j], T.FL[:, j:j + 1], ALU.mult, ["BW", "FL"], ["BW"])
-        if j < len(fill):
-            fill[j]()
-    widen(N)
+    ts(c_(12), c_(9), BIG, ALU.mult, ["c9", "c10"], ["c12"], c_(10), ALU.add)
+    ts(c_(13), c_(9), 128.0, ALU.mult, ["c9", "OH"], ["c13"], o_(4), ALU.add)
+    ts(c_(14), c_(9), o_(4), ALU.add, ["c9", "OH"], ["c14"], -2.0 * BIG, ALU.mult)
+    scan(T.P2[:], T.X1[:, 0:12], T.ZER[:, 0:12], -0.25, ALU.mult, ALU.add, ["X1", "ZER"], ["P2"])
+    ts(T.I24[:], T.XP[:, 0:128], 0.0, ALU.is_equal, ["XP"], ["I24"], U24, ALU.mult)
+    ts(T.BLK[:], T.JG[:], c_(2), ALU.is_equal, ["JG", "c0"], ["BLK"])
+    ts(T.Z[:, 0:160], T.XP[:], 16.0, ALU.is_equal, ["XP", "c7"], ["Z0"], c_(7), ALU.mult)
+    ts(T.Z[:, 160:320], T.XP[:], 16.0, ALU.is_equal, ["XP", "c8"], ["Z1"], c_(8), ALU.mult)
+    tt(T.P2[:], T.P2[:], T.EQ[:], ALU.mult, ["P2", "EQ"], ["P2"])
+    ts(c_(15), o_(12), float(1856 - A * rank), ALU.mult, ["OH", "c13"], ["c15"], c_(13), ALU.add)
+    ts(T.MC[:], T.AR[:, 0:8], c_(2), ALU.is_equal, ["AR", "c0"], ["MC"], BIG * BIG, ALU.mult)
+    ts(T.MKb[:], T.AR[:, 0:8], c_(2), ALU.is_equal, ["AR", "c0", "c12"], ["MKb"], c_(12), ALU.mult)
+    op("v", lambda: V.tensor_reduce(c_(18), T.P2[:], AxisListType.X, ALU.add), ["P2"], ["c18"])
+    ms(T.UT[:], 0.0, ["UT"])
+    if far is not None:
+        ts(c_(19), o_(12), float(1856 - A * far), ALU.mult, ["OH", "c13"], ["c19"], c_(13), ALU.add)
+        dma("s", T.Tf[0:128:16, 0:W], T.ZER[:], ["ZER"], ["Tf"])
+    ms(T.RS[:], U24, ["RS"])
+    ms(T.R5[:], 1.0, ["R5"])
+    ms(T.KW[:], -1.0, ["KW"])
+    ms(T.PW[:], 0.0, ["PW"])
+    ms(T.NS[:], 0.0, ["NS"])
+    ms(T.CC[:, 4 * A:6 * A], 0, ["CC4", "CC5"])
+    widen()
 
-    aff(T.IDL[:], T.AR[:], -1.0, float(2047 - A * rank), ["AR"], ["IDL"])
-    CZ = ["CAz%d" % j for j in range(5)]
-    for j in range(5):
-        n_ = min(Q, 2880 - Q * j)
-        act(T.CA[:, Q * j:Q * j + n_], T.Fw[:, rank * Q:rank * Q + n_], [fme], [CZ[j]], scale=0.0)
-    aff(T.PST[:], T.AR[:], 0.0, c_(8), ["AR", "c8"], ["PST"])
-    act(T.I23[:], T.I1[:], ["I1"], ["I23"], scale=U23)
-    act(T.E2[:], T.E1[:], ["E1"], ["E2"], scale=2048.0)
-    act(T.Z[:, 320:640], T.Z[:, 0:320], ["Z0", "Z1"], ["Z2"], scale=64.0)
+    zero = T.AR[:, 0:12]
+    act(T.E16[:], T.E1[:], ["E1", "c11"], ["E16"], func=AF.Identity, scale=c_(11))
+    aff(T.PST[:], T.AR[:], 0.0, c_(16), ["AR", "c16"], ["PST"])
+    act(T.Ib[:], T.I24[:], ["I24"], ["Ib"], scale=1.0 / U24)
+    act(T.Nb[:], T.I24[:], ["I24"], ["Nb"], scale=-1.0 / U24)
+    act(T.MCb[:], T.MC[:], ["MC"], ["MCb"])
+    aff(T.RS[:, 0:192:16], zero, 0.0, 7.5, ["AR", "RS"], ["RS"])
+    aff(T.R5[:, 0:180:5], T.AR[:, 0:36], 0.0, 0.0, ["AR", "R5"], ["R5"])
     for h in range(2):
-        aff(T.aT[:, h:12:2], T.AR[:, 0:192:32], 1.0, c_(4), ["AR", "c4"], ["aT%d" % h])
-    aff(T.dumB[:], T.aL[:], 1.0, float(W), ["aL"], ["dumB"])
-    aff(T.dmpK[:], T.aK[:], 1.0, float(2 * A), ["aK"], ["dmpK"])
-    aff(T.idl1[:], T.aL[:], -1.0, float(2048 - A * rank), ["aL"], ["idl1"])
-    aff(T.nbS[:], T.aL[:], 4096.0, -4096.0 * (12 * 2 ** 20 + 191), ["aL"], ["nbS"])
-    aff(T.UT[:, 14:192:16], T.aT[:], -1.0, 191.0, ["aT0", "aT1", "UT"], ["UTs"])
-    aff(T.mK1[:], T.mK[:], 1.0, float(A), ["mK"], ["mK1"])
-    for kk in range(4):
-        for h in range(2):
-            aff(T.K2[:, 12 * h:12 * h + 12, kk], T.aK[:], 1.0, float((4, 2, 1, 0)[kk] * A), ["aK"], ["K2"])
-    act(T.K23[:], T.K2[:], ["K2"], ["K23"], scale=U23)
-    act(T.Ib[:], T.I1[:], ["I1"], ["Ib"])
-    act(T.Nb[:], T.I1[:], ["I1"], ["Nb"], scale=-1.0)
-    for kk in range(1, 4):
-        aff(T.DUM[:, :, kk], T.aL[:], 1.0, float(W + A + (3 - kk) * A), ["aL", "DUM"], ["DUMk"])
-    for s in (1, 2, 3):
-        o_ = 6 * s * (s - 1)
-        act(T.KS[:, o_:o_ + 12 * s], T.K2[:, 0:12, 4 - s:4], ["K2"], ["KS"])
-        act(T.KT[:, o_:o_ + 12 * s:s], T.K2[:, 0:12, 3 - s], ["K2", "KT0"], ["KT"], scale=1.0 / U23)
-    act(T.BLV[:], T.BLK[:], ["BLK"], ["BLV"], scale=-1.0 / U23)
-    act(T.WK2[:], T.WK1[:], ["WK1"], ["WK2"], scale=-1.0 / U23)
-    for j in range(N):
-        act(T.Vw[:, Q * j:Q * j + Q], T.Fw[:, me], [fme], VK, scale=0.0)
+        aff(T.aT[:, h:12:2], T.AR[:, 0:192:32], 1.0, c_(3), ["AR", "c0"], ["aT%d" % h])
+    aff(T.UT[:, 4:192:16], T.aT[:], -1.0, 191.0, ["aT0", "aT1", "UT"], ["UTs"])
+    aff(T.UT[:, 12:192:16], zero, 0.0, 1.0, ["AR", "UT"], ["UTo"])
+    aff(T.C16[:], T.aL[:], 16.0 / U24, 7.5 / U24, ["aL"], ["C16"])
+    aff(T.CG[:], T.aL[:], -1.0 / 16.0 / U24, (SAME + 191.0 / 16.0) / U24, ["aL"], ["CG"])
+    aff(T.CT[:], zero, 0.0, 2047.5 / U24, ["AR"], ["CT"])
+    aff(T.CK[:], T.aL[:], 7.0 / 128.0, (2047.5 - A * rank - 8 * 191) / 128.0, ["aL"], ["CK"])
+    for k in range(5):
+        aff(T.DUM[:, :, k], T.aL[:], 1.0, float(W), ["aL"], ["DUM"])
+    for k in range(4):
+        act(T.aLt[:, 12 * k:12 * k + 12], T.aL[:], ["aL"], ["aLt"], func=AF.Silu, bias=float(A * k + A))
+    if far is not None:
+        act(T.UF[:], T.UT[:], ["UT", "UTs", "UTo"], ["UF"])
+        act(T.WF[:], T.BLK[:], ["BLK", "c19"], ["WF"], func=AF.Identity, scale=c_(19))
+    act(T.ST[:], T.DUM[:], ["DUM"], ["ST"])
+    act(T.Zk[:], T.DUM[:], ["DUM"], ["Zk"], scale=0.0)
+    act(T.EW[:], T.E1[:], ["E1", "c18"], ["EW"], func=AF.Identity, scale=c_(18))
+    act(T.WK[:], T.BLK[:], ["BLK", "c15"], ["WK"], func=AF.Identity, scale=c_(15))
+    act(T.EG[:], T.E1[:], ["E1"], ["EG"], scale=16.0)
+    act(T.NB16[:], T.BLK[:], ["BLK"], ["NB16"], scale=-16.0)
+    act(T.EV[:], T.E1[:], ["E1", "c14"], ["EV"], func=AF.Identity, scale=c_(14))
+    aff(T.CD[:], T.AR[:], -1.0 / 128.0, c_(17), ["AR", "c17"], ["CD"])
+    for t in (4, 5):
+        aff(T.CS[:, A * t:A * t + A], T.AR[:], 0.0, -8.0, ["AR"], ["CS%d" % t])
+    for t in (0, 4, 5):
+        act(T.CM[:, A * t:A * t + A], T.AR[:], ["AR"], ["CM%d" % t], scale=0.0)
 
-    CAc, CA2, CA1 = T.CA[:, 0:960], T.CA[:, 960:1920], T.CA[:, 1920:2880]
+    def count():
+        ts(T.AL[:], T.ST[:], float(W), ALU.is_lt, ["ST"], ["AL"])
+        scan(T.nn[:], T.R5[:, 0:60], T.AL[:], 0.0, ALU.mult, ALU.add, ["R5", "AL"], ["nn"])
+
     banks = [T.pb0, T.pb1, T.pb2, T.pb3, T.pb4, T.pb5]
-
-    def parts(t, lst, lk):
-        cp(T.cI[:], T.Cw[:].indirect(lst), CK + [lk], ["cI"])
-        ts(T.chl[:, 0:192], T.cI[:], 63, ALU.bitwise_and, ["cI"], ["clo"])
-        ts(T.chl[:, 192:384], T.cI[:], 6, ALU.arith_shift_right, ["cI"], ["chi"])
-        if t < 2:
-            cp(T.CA[:, t * A:t * A + A], T.cI[:], ["cI"] + CZ, ["CAc"])
-        else:
-            cp(CAc.indirect(T.woU[:]), T.cI[:], ["cI", "woU"], ["CAc"])
-
-    def scores(t):
-        if t < 2:
-            tt(T.CA[:, 960 + t * A:960 + t * A + A], T.pb0[:, 0:192], T.chl[:, 0:192], ALU.add, ["pb0", "clo"] + CZ, ["CA2"])
-            tt(T.CA[:, 1920 + t * A:1920 + t * A + A], T.pb0[:, 0:192], T.chl[:, 192:384], ALU.add, ["pb0", "chi"] + CZ, ["CA1"])
-        else:
-            tt(T.Sn[:, 192:384], T.pb0[:, 0:192], T.chl[:, 192:384], ALU.add, ["pb0", "chi"], ["Sn1"])
-            tt(T.Sn[:, 0:192], T.pb0[:, 0:192], T.chl[:, 0:192], ALU.add, ["pb0", "clo"], ["Sn2"])
-            cp(CA1.indirect(T.woU[:]), T.Sn[:, 192:384], ["Sn1", "woU"], ["CA1"])
-            cp(CA2.indirect(T.woU[:]), T.Sn[:, 0:192], ["Sn2", "woU"], ["CA2"])
-
-    cp(T.cG[:], T.Cw[:].indirect(T.hU[:]), CK + ["hU"], ["cG"])
-    mm(T.pb0[:, 0:192], T.I23[:], T.PST[:], True, False, ["I23", "PST"], ["pb0"])
-    for ch, (lo, hi) in enumerate(((0, 38), (38, 96), (96, 132), (132, 192))):
-        if ch == 2:
-            parts(0, T.hU[:], "hU")
-        gather("va"[ch % 2], T.X[:, 16 * lo:16 * hi], T.Fw[:], T.cG[:, lo:hi], FK + ["cG"], ["X%d" % ch])
-        if ch % 2:
-            a0 = 48 * (ch - 1)
-            for p in range(16):
-                last = ch == 3 and p == 15
-                mm(T.pb0[:, a0:a0 + 96], T.E2[:, 15 - p:143 - p], T.X[:, 16 * a0 + p:16 * a0 + 1536:16], False, last,
-                   ["E2", "X%d" % (ch - 1), "X%d" % ch], ["pb0"], last)
-    aff(T.pS[:, 0:192], T.pb0[:, 0:192], 4.0, -2176.0, ["pb0"], ["pS"])
-    scores(0)
-
-    left, right = (rank - 1) % N, (rank + 1) % N
     for t in range(1, RO + 1):
-        s = min(t - 1, 3)
-        s1 = min(s, 2) + 1
+        s = t - 1
         lastr = t == RO
+        nblk = t if t < 4 else 6
+        keys = lambda n_: ["%s%d" % (n_, j) for j in range(nblk)]
+        vk = VK if s else VK + SK
+        todo = []
         if s:
-            n_ = A * s
-            o_ = 6 * s * (s - 1)
-            nl = T.rs[:, s - 1:12 * s:s]
             hk = CSPLIT[s]
             cp(T.Vs[:, 0:16 * hk], T.Vw[:].indirect(T.btU[:, 0:hk]), VK + ["btU"], ["Vs0"])
-            act(T.Vs[:, 16 * hk:n_], T.Vw[:].indirect(T.btU[:, hk:12 * s]), VK + ["btU"], ["Vs1"])
-            mm(T.pP[:, 0:12 * s], T.I23[:], T.St[:, 12:24, 4 - s:4], True, False, ["I23", "St"], ["pP"])
-            mm(T.pP[:, 0:12 * s], T.I23[:], T.M1[:, 0:12 * s], False, False, ["M1"], ["pP"])
+            act(T.Vs[:, 16 * hk:A * t], T.Vw[:].indirect(T.btU[:, hk:12 * t]), VK + ["btU"], ["Vs1"])
+            mm(T.pS[:, 0:192], T.I24[:], T.CD[:], True, False, ["I24", "CD"], ["pS"])
+            mm(T.pP[:, 0:12 * t], T.I24[:], T.KW[:, :, 5 - t:5], True, False, ["I24", "KW"], ["pP"])
             for q in range(16):
-                mm(T.pP[:, 0:12 * s], T.E1[:, 15 - q:143 - q], T.Vs[:, q:n_:16], False, False, ["E1", "Vs0", "Vs1"], ["pP"])
-            mm(T.pP[:, 0:12 * s], T.I23[:], T.KT[:, o_:o_ + 12 * s], False, True, ["KT"], ["pP"], True)
-            wv, wk_ = (T.BLV, "BLV") if lastr else (T.BLK, "BLK")
-            n1 = min(n_, 384)
-            mm(T.pb1[:, 0:n1], wv[:], T.Vs[:, 0:n1], True, True, [wk_, "Vs0", "Vs1"], ["pb1"], True)
-            act(T.kv[:, 0:n1], T.pb1[:, 0:n1], ["pb1"], ["kv0"])
-            if n1 < n_:
-                mm(T.pb2[:, 0:n_ - n1], wv[:], T.Vs[:, n1:n_], True, True, [wk_, "Vs0", "Vs1"], ["pb2"], True)
-                act(T.kv[:, n1:n_], T.pb2[:, 0:n_ - n1], ["pb2"], ["kv1"])
-            op("v", lambda: V.tensor_tensor_scan(T.rs[:, 0:12 * s], T.pP[:, 0:12 * s], T.KS[:, o_:o_ + 12 * s], 0.0, ALU.min, ALU.max),
-               ["pP", "KS"], ["rs"])
-            tt(T.no[:], nl, T.mK[:], ALU.add, ["rs", "mK"], ["no"])
-            cp(T.noU[:], T.no[:], ["no"], ["noU"])
-            cp(T.cU[:], CAc.indirect(T.noU[:]), ["CAc", "noU"], ["cU"])
-            a1, a2 = VSPLIT[s]
-            act(T.Vg[:, 0:16 * a1], T.Vw[:].indirect(T.cU[:, 0:a1]), VK + ["cU"], ["Vg0"])
-            act(T.Vg[:, 16 * a1:16 * a2], T.Vw[:].indirect(T.cU[:, a1:a2]), VK + ["cU"], ["Vg1"])
-            for j in range(2 * s):
-                b0 = 12 * s * (j // s)
-                mm(T.pb3[:, b0 + j % s:b0 + 12 * s:s], T.I23[:], nl, True, True, ["rs"], ["pb3"], j == 2 * s - 1)
-            cp(T.S12[:, 192:384], CA1.indirect(T.noU[:]), ["CA1", "noU"], ["S1"])
-            cp(T.S12[:, 0:192], CA2.indirect(T.noU[:]), ["CA2", "noU"], ["S2"])
-            S2, S1, k2, k1 = T.S12[:, 0:192], T.S12[:, 192:384], "S2", "S1"
-            mm(T.pS[:, 0:192], T.I23[:], T.IDL[:], True, False, ["I23", "IDL"], ["pS"])
-            ts(T.G[:], S1, M2K, ALU.add, [k1], ["G"], M2K, ALU.subtract)
-            mm(T.pS[:, 0:192], T.I23[:], T.G[:], False, False, ["G"], ["pS"])
-            u_ = slice(4 - s, 4)
-            tt(T.kept[:, :, u_], T.pb3[:, 0:24 * s], T.K23[:, :, u_], ALU.is_gt, ["pb3", "K23"], ["kept"])
-            cp(T.Vg[:, 16 * a2:3072], T.Vw[:].indirect(T.cU[:, a2:192]), VK + ["cU"], ["Vg2"])
-            tt(T.dl[:, :, u_], T.dl[:, :, u_], T.kept[:, 0:12, u_], ALU.mult, ["dl", "kept"], ["dl"])
-            tt(T.St[:, :, u_], T.St[:, :, u_], T.kept[:, :, u_], ALU.mult, ["St", "kept"], ["St"])
-            tt(T.ko[:, :, u_], T.dl[:, :, u_], T.DUM[:, :, u_], ALU.add, ["dl", "DUMk"], ["ko"])
-            cp(T.koU[:, 0:12 * s], T.ko[:, :, u_], ["ko"], ["koU"])
-            if not lastr:
-                cp(T.pvU[:], T.ko[:, :, 3], ["ko"], ["pvU"])
-            cp(T.Tw[:].indirect(T.koU[:, 0:12 * s]), T.kv[:, 0:n_], ["koU", "kv0", "kv1"], ["Tw"])
-            for lo, hi, kx in ((0, a1, "Vg0"), (a2, A, "Vg2"), (a1, a2, "Vg1")):
-                for p in range(16):
-                    last = kx == "Vg1" and p == 15
-                    mm(T.pS[:, lo:hi], T.E1[:, 15 - p:143 - p], T.Vg[:, 16 * lo + p:16 * hi:16], False, last,
-                       ["E1", kx], ["pS"], last)
-            if lastr:
+                mm(T.pP[:, 0:12 * t], row(T.EV, q), T.Vs[:, q:A * t:16], False, q == 15, ["EV", "Vs0", "Vs1"], ["pP"], q == 15)
+            scan(T.rs[:, 0:12 * t], T.pP[:, 0:12 * t], T.PC[:, 0:12 * t], 0.0, ALU.min, ALU.max, ["pP", "PC"], ["rs"])
+            nl = T.rs[:, s:12 * t:t]
+            cp(T.noU[:], nl, ["rs"], ["noU"])
+            cp(T.cU[:], T.CC[:, 0:A * nblk].indirect(T.noU[:]), keys("CC") + ["noU"], ["cU"])
+
+            def pick(_):
+                cp(T.S1[:], T.CS[:, 0:A * nblk].indirect(T.noU[:]), keys("CS") + ["noU"], ["S1"])
+                mm(T.pS[:, 0:192], T.I24[:], T.S1[:], False, False, ["S1"], ["pS"])
+
+            def kill(_):
+                for k in range(s):
+                    ts(T.Zk[:, :, 4 - k], nl, float(A * k + A), ALU.is_lt, ["rs"], ["Zk%d" % k], BIG, ALU.mult)
+                tt(T.ST[:], T.ST[:], T.Zk[:], ALU.max, ["ST", "Zk"] + ["Zk%d" % k for k in range(s)], ["ST"])
+                tt(T.ST[:], T.ST[:], T.DUM[:], ALU.min, ["ST", "DUM"], ["ST"])
+                for k in range(s):
+                    cp(T.koU[:, 48 * s + 12 * k:48 * s + 12 * k + 12], T.ST[:, :, 4 - k], ["ST", "koU"], ["koU%d" % k])
+
+            def keep(e, k):
+                put(e, T.Tw, T.koU[:, 48 * s + 12 * k:48 * s + 12 * k + 12], T.KR[:, A * k:A * k + A],
+                    ["koU%d" % k, "KR%d" % k], "Tw")
+
+            def bundle(_):
+                count()
+                ts(T.X1[:], T.ST[:], 1.0, ALU.add, ["ST"], ["X1"])
+                tt(T.X1[:], T.X1[:], T.AL[:], ALU.mult, ["X1", "AL"], ["X1"])
                 for k in range(3):
-                    aff(T.yB[:, 12 * k:12 * k + 12], T.kept[:, 0:12, 3 - k], 1.0, -1.0, ["kept"], ["yB%d" % k])
+                    ts(T.yE[:, 12 * k:12 * k + 12], T.nn[:, 4:60:5], float(k), ALU.is_equal, ["nn"], ["yE%d" % k])
+                for k in range(3):
+                    y_ = T.YQ[:, 60 * k:60 * k + 60]
+                    tt(y_, y_, T.X1[:], ALU.mult, ["YQ%d" % k, "X1"], ["YQ%d" % k])
+                scan(T.YS[:], T.R5[:], T.YQ[:], 0.0, ALU.mult, ALU.add, ["R5", "YQ0", "YQ1", "YQ2"], ["YS"])
+                ts(T.yB[:], T.YS[:, 4:180:5], 1.0, ALU.subtract, ["YS"], ["yB"])
+
+            todo = {"P": pick, "K": kill, "Y": bundle, "k": lambda k: keep("a", k), "e": lambda k: keep("v", k)}
         else:
-            nl = T.aK[:]
-            S2, S1, k2, k1 = T.CA[:, 960:960 + A], T.CA[:, 1920:1920 + A], "CA2", "CA1"
-        tt(T.sc[:, 0:192], S2, T.pS[:, 0:192], ALU.min, [k2, "pS"], ["sc2"])
-        tt(T.sc[:, 192:384], S1, T.pS[:, 0:192], ALU.min, [k1, "pS"], ["sc1"])
-        op("v", lambda: V.transpose(T.sT[:], T.sc[:]), ["sc1", "sc2"], ["sT"])
-        op("v", lambda: V.tensor_tensor_scan(T.rm[:], T.RS[:], T.sT[:], 2.0 ** 24, ALU.min, ALU.max),
-           ["sT", "RS", "RSa", "RSb"], ["rm"])
-        ts(T.Hh[:], T.rm[:, 15:384:16], M64, ALU.add, ["rm"], ["Hh"], M64, ALU.subtract)
-        ts(T.UT[:, 12:192:16], T.rm[:, 207:384:16], M32K, ALU.add, ["rm", "UT"], ["U12"], M32K, ALU.subtract)
-        tt(T.xx[:], T.rm[:, 15:384:16], T.Hh[:], ALU.subtract, ["rm", "Hh"], ["xx"])
-        ts(T.GT[:], T.rm[:, 207:384:16], M2K, ALU.add, ["rm"], ["GT"], M2K, ALU.subtract)
-        for u in range(2):
-            for h in range(2):
-                o_ = 160 * u + 16 - 16 * (h - u)
-                mm(T.pS[:, 192 + u:204:2], T.Z[:, o_:o_ + 128], T.xx[:, h:12:2], h == 0, False, ["Z0", "Z1", "xx"], ["pS"])
-                mm(T.pS[:, 192 + u:204:2], T.Z[:, 320 + o_:320 + o_ + 128], T.xx[:, 12 + h:24:2], False, h == 1,
-                   ["Z2", "xx"], ["pS"], u == 1 and h == 1)
-        tt(T.UT[:, 13:192:16], T.GT[:], T.UT[:, 12:192:16], ALU.subtract, ["GT", "U12"], ["U13"])
-        ts(T.ctU[:], T.pS[:, 192:204], 2047.5, ALU.add, ["pS"], ["ctU"])
-        op("v", lambda: V.transpose(T.H[:], T.UT[:]), ["U12", "U13", "UTs", "UT"], ["H"])
-        for u in range(2):
-            for h in range(2):
-                o_ = 160 * u + 16 - 16 * (h - u)
-                for j in (12, 13):
-                    mm(T.pP[:, u:12:2], T.Z[:, o_:o_ + 128], T.UT[:, 16 * h + j:192:32], h == 0 and j == 12,
-                       h == 1 and j == 13, ["U12", "U13"], ["pP"], u == 1 and h == 1 and j == 13)
-        cp(T.Bt[:], T.BW[:].indirect(T.ctU[:]), ["BW", "ctU"], ["Bt"])
-        act(T.nb1[:], T.pP[:, 0:12], ["pP"], ["nb1"], scale=-512.0)
-        aff(T.ck[:, 0:12], T.pS[:, 192:204], 1.0, 2047.5, ["pS"], ["ctF"])
-        wk, wkk = (T.WK2, "WK2") if lastr else (T.WK1, "WK1")
-        mm(T.pS[:, 256:448], wk[:], T.H[:], True, True, [wkk, "H"], ["pS"], True)
+            nl = T.aL[:]
+            cp(T.cU[:], T.Cw[:].indirect(T.hU[:]), CK + ["hU"], ["cU"])
+            mm(T.pS[:, 0:192], T.Ib[:], T.PST[:], True, False, ["Ib", "PST"], ["pS"])
+            todo = {"C": lambda _: cp(T.CC[:, 0:A], T.cU[:], ["cU"], ["CC0"])}
+        GK = []
+        for e, lo, hi in spans(VPLAN[s]):
+            if e in "av":
+                GK.append("Vg%d" % lo)
+                gather(e, T.Vg[:, 16 * lo:16 * hi], T.Vw[:], T.cU[:, lo:hi], vk + ["cU"], GK[-1:])
+            elif e in "mM":
+                for p in range(16):
+                    last = e == "M" and p == 15
+                    mm(T.pS[:, lo:hi], row(T.EV if s else T.E16, p), T.Vg[:, 16 * lo + p:16 * hi:16], False, last,
+                       ["EV", "E16"] + over("Vg", VPLAN[s], lo, hi), ["pS"], last)
+            else:
+                todo[e](lo)
+        mm(T.pb0[:, 0:12], T.I24[:], T.C16[:], True, False, ["C16"], ["pb0"])
+        mm(T.pb1[:, 0:12], T.I24[:], T.CG[:], True, False, ["CG"], ["pb1"])
+        mm(T.pP[:, 0:12], T.I24[:], T.CT[:], True, False, ["CT"], ["pP"])
+
+        if s:
+            tt(T.sc[:], T.S1[:], T.pS[:, 0:192], ALU.min, ["S1", "pS"], ["sc"])
+            op("v", lambda: V.transpose(T.sT[:], T.sc[:]), ["sc"], ["sT"])
+        else:
+            op("v", lambda: V.transpose(T.sT[:], T.pS[:, 0:192]), ["pS"], ["sT"])
+            act(T.CS[:, 0:A], T.pS[:, 0:192], ["pS"], ["CS0"])
+        scan(T.rm[:], T.RS[:], T.sT[:], U24, ALU.min, ALU.max, ["sT", "RS"], ["rm"])
+        best = T.rm[:, 15:192:16]
+        rnd(T.Hh[:], best, M16, ["rm"], ["Hh"])
+        rnd(T.UT[:, 0:192:16], best, M1K, ["rm", "UT"], ["U0"])
+        tt(T.xx[:], T.Hh[:], best, ALU.subtract, ["rm", "Hh"], ["xx"])
+        tt(T.UT[:, 8:192:16], T.Hh[:], T.UT[:, 0:192:16], ALU.subtract, ["Hh", "U0"], ["U8"])
+        uh = [(u, h) for u in range(2) for h in range(2)]
+        zm = lambda u, h: T.Z[:, 160 * u + 16 - 16 * (h - u):160 * u + 144 - 16 * (h - u)]
+        for u, h in uh:
+            mm(T.pb0[:, u:12:2], zm(u, h), T.xx[:, h:12:2], False, u + h == 2, ["Z0", "Z1", "xx"], ["pb0"], u + h == 2)
+        op("v", lambda: V.transpose(T.H[:], T.UT[:]), ["U0", "U8", "UTs", "UTo", "UT"], ["H"])
+        cp(T.poU[:], T.pb0[:, 0:12], ["pb0"], ["poU"])
+        ts(T.Bt[:], T.Vg[:].indirect(T.poU[:]), c_(6), ALU.mult, GK + ["poU", "c6"], ["Bt"])
+        tell = far is not None and not lastr
+        if tell:
+            z = slice(48 * s, 48 * s + 12 * t)
+            ts(T.koU[:, 48 * s + 12 * s:48 * s + 12 * t], T.Hh[:], 1.0 / 16.0, ALU.mult, ["Hh"], ["gU"])
+            send([([cores[far]], T.koU[:, z], T.koF[:, z], "aK%d" % s, off)], ["gU"] + ["koU%d" % k for k in range(s)])
+            mark(("aK%d" % s, len(off)), [], ["koF"])
+        for u, h in uh:
+            for j in (0, 8):
+                last = u + h == 2 and j == 8
+                mm(T.pb1[:, u:12:2], zm(u, h), T.UT[:, 16 * h + j:192:32], False, last, ["U0", "U8"], ["pb1"], last)
+        act(T.nbb[:], T.pb1[:, 0:12], ["pb1"], ["nbb"], scale=-BIG)
+        mm(T.pS[:, 256:448], T.WK[:], T.H[:], True, True, ["WK", "H"], ["pS"], True)
+        for q in range(16):
+            mm(T.pP[:, 0:12], row(T.EW, q), T.Bt[:, q:192:16], False, q == 15, ["EW", "Bt"], ["pP"], q == 15)
         for gq in range(NMV, 8):
-            act(T.Abd[:, :, gq, :], T.Bt[:], ["Bt", "MC"], ["A%d" % gq], func=AF.Identity, scale=T.MC[:, gq:gq + 1])
-        tt(T.B[:], T.Bt[:], T.H[:], ALU.mult, ["Bt", "H"], ["B"])
+            aff(T.Abd[:, :, gq, :], T.Bt[:], T.MC[:, gq:gq + 1], T.MKb[:, gq:gq + 1], ["Bt", "MC", "MKb"], ["A%d" % gq])
+        tt(T.B[:], T.Bt[:], T.H[:], ALU.add, ["Bt", "H"], ["B"])
         for gq in range(NMV):
-            ts(T.Abd[:, :, gq, :], T.Bt[:], T.MC[:, gq:gq + 1], ALU.mult, ["Bt", "MC"], ["A%d" % gq])
-        tt(T.nbb[:], T.nb1[:], T.nbS[:], ALU.add, ["nb1", "nbS"], ["nbb"])
-        act(T.ktR[:], T.pS[:, 256:448], ["pS"], ["ktR"])
-        if lastr:
-            ts(T.lw[:], T.ck[:, 0:12], 1.0, ALU.add, ["ctF"], ["lw"])
+            ts(T.Abd[:, :, gq, :], T.Bt[:], T.MCb[:, gq:gq + 1], ALU.mult, ["Bt", "MCb", "MKb"], ["A%d" % gq],
+               T.MKb[:, gq:gq + 1], ALU.add)
+        ts(T.nob[:], T.nbb[:], -BIG * (SAME + 13.0), ALU.is_gt, ["nbb"], ["nob"], 8192.0, ALU.mult)
+        tt(T.ck[:], T.pP[:, 0:12], T.nob[:], ALU.max, ["pP", "nob"], ["ck"])
+        if not lastr:
+            cp(T.ctU[:], T.pP[:, 0:12], ["pP"], ["ctU"])
+            if EARLY:
+                cp(T.cG[:], T.Cw[:].indirect(T.ctU[:]), CK + ["ctU"], ["cG"])
+        else:
+            ts(T.x2[:], T.ck[:], 1.0, ALU.add, ["ck"], ["x2"])
             for k in range(3):
-                y_ = slice(12 * k, 12 * k + 12)
-                tt(T.yE[:, y_], nl, T.K2[:, 0:12, 3 - k], ALU.is_equal, ["rs", "K2"], ["yE%d" % k])
+                y_ = T.yE[:, 12 * k:12 * k + 12]
+                tt(y_, y_, T.x2[:], ALU.mult, ["yE%d" % k, "x2"], ["yE%d" % k])
+        kr = T.KR[:, A * s:A * t]
+        act(kr, T.pS[:, 256:448], ["pS"], ["KR%d" % s])
         AK = ["A%d" % j for j in range(8)] + ["B"]
         for b in (3, 0, 4, 1, 5, 2):
             for j in range(2):
@@ -459,123 +556,153 @@ def rank_program(g, core, T, topo):
                 else:
                     act(T.junk[:, A * (m - 6):A * (m - 5)], src, ["pb%d" % b, "nbb"], ["W%d" % m], func=AF.Relu,
                         bias=T.nbb[:, m:m + 1], accum_out=T.Wr[:, m:m + 1])
-        if 2 <= t < RO:
-            act(T.Mn[:], T.Fw[:].indirect(T.pvU[:]), FK + ["pvU"], ["Mn"])
         WD = ["W%d" % m for m in range(6)]
         tt(T.Wr[:, 0:6], T.Wr[:, 0:6], T.nbb[:, 0:6], ALU.add, WD + ["nbb"], WD)
-        tt(T.t12[:], T.Wr[:], T.ck[:, 0:12], ALU.max, ["ctF"] + ["W%d" % m for m in range(12)], ["t12"])
+        tt(T.t12[:], T.Wr[:], T.ck[:], ALU.max, ["ck"] + ["W%d" % m for m in range(12)], ["t12"])
         if lastr:
             for k in range(3):
-                y_ = slice(12 * k, 12 * k + 12)
-                ts(T.yW[:, y_], T.t12[:], float(W), ALU.is_lt, ["t12"], ["yW%d" % k])
-                tt(T.yE[:, y_], T.yE[:, y_], T.lw[:], ALU.mult, ["yE%d" % k, "lw"], ["yE%d" % k])
-                tt(T.yB[:, y_], T.yB[:, y_], T.St[:, 0:12, 3 - k], ALU.add, ["yB%d" % k, "St"], ["yB%d" % k])
+                ts(T.yW[:, 12 * k:12 * k + 12], T.t12[:], float(W), ALU.is_lt, ["t12"], ["yW%d" % k])
             tt(T.yW[:], T.yW[:], T.yE[:], ALU.mult, ["yW0", "yW1", "yW2", "yE0", "yE1", "yE2"], ["yW"])
-        tt(T.oF[:], T.t12[:], T.dumB[:], ALU.min, ["t12", "dumB"], ["oF"])
+        new = T.x1[:] if lastr else T.ST[:, :, 4 - s]
+        tt(new, T.t12[:], T.DUM[:, :, 0], ALU.min, ["t12", "DUM", "ST"], ["x1" if lastr else "ST"])
         if lastr:
-            tt(T.yL[:], T.yW[:], T.yB[:], ALU.add, ["yW", "yB0", "yB1", "yB2"], ["yL"])
-        cp(T.oU[:], T.oF[:], ["oF"], ["oU"])
-        cp(T.Tw[:].indirect(T.oU[:]), T.ktR[:], ["oU", "ktR", "Tw"], ["Tw"])
+            tt(T.yL[:], T.yW[:], T.yB[:], ALU.add, ["yW", "yB"], ["yL"])
+        ou = T.oU[:, 16 * s:16 * s + 12]
+        cp(ou, new, ["ST", "x1"], ["oU"])
+        if tell:
+            send([([cores[far]], ou, T.oF[:, 16 * s:16 * s + 12], "aO%d" % s, off)], ["oU"])
+            mark(("aO%d" % s, len(off)), [], ["oF"])
+        put("v", T.Tw, ou, kr, ["oU", "KR%d" % s], "Tw")
 
         if lastr:
             dma("s", T.yt[:], T.Tw[0:128:16, 0:W], ["Tw"], ["yt"])
             for q in range(16):
-                mm(T.pb0[0:8, q:384:16], T.I1[:, q:128:16], T.yL[:, 0:24], True, True, ["yL"], ["pb0"], q == 15)
+                mm(T.pb0[0:8, q:384:16], T.I24[:, q:128:16], T.yL[:, 0:24], True, True, ["yL"], ["pb0"], q == 15)
             for q in range(16):
-                mm(T.pb1[0:8, q:192:16], T.I1[:, q:128:16], T.yL[:, 24:36], True, True, ["yL"], ["pb1"], q == 15)
-            act(T.yo[0:8, 0:384], T.pb0[0:8, 0:384], ["pb0"], ["yo0"])
-            cp(T.yo[0:8, 384:576], T.pb1[0:8, 0:192], ["pb1"], ["yo1"])
+                mm(T.pb1[0:8, q:192:16], T.I24[:, q:128:16], T.yL[:, 24:36], True, True, ["yL"], ["pb1"], q == 15)
+            act(T.yo[0:8, 0:384], T.pb0[0:8, 0:384], ["pb0"], ["yo0"], scale=1.0 / U24)
+            ts(T.yo[0:8, 384:576], T.pb1[0:8, 0:192], 1.0 / U24, ALU.mult, ["pb1"], ["yo1"])
             dma("a", T.yb[:], T.yo[0:8, :], ["yo0", "yo1"], ["yb"])
             break
 
-        x = slice(240 * (t - 1), 240 * t)
+        x = slice(240 * s, 240 * t)
         tc = "Tc%d" % t
         dma("s", T.Tc[:, x], T.Tw[0:128:16, 0:W], ["Tw"], [tc])
-        cl, cr = cores[left], cores[right]
-        el, er = topo.engines(core, cl), topo.engines(core, cr)
-        if len(el) <= len(er):
-            el = el[:len(off)]
-            er = [e for e in er if e not in el]
-        else:
-            el = [e for e in el if e not in er]
-        send([([cl], T.Tc[:, x], T.NR[:, x], "aR%d" % (t - 1), el), ([cr], T.Tc[:, x], T.NL[:, x], "aL%d" % (t - 1), er)], [tc])
-        mark(("aL%d" % (t - 1), len(off)), [], ["NL"])
-        mark(("aR%d" % (t - 1), len(off)), [], ["NR"])
-        dma("s", T.Tw[0:128:16, 0:W], (T.ZER if t == RO - 1 else T.FLO)[:], ["FLO", "ZER"], ["Tw"])
+        send([([cores[j]], T.Tc[:, x], T["N" + "RL"[j == right]][:, x], "a%s%d" % ("RL"[j == right], s), es)
+              for j, es in zip(close, (up, off) if far is None else (on,))], [tc])
+        for j in close:
+            alone = LISTS and (j + j - rank) % N not in mine
+            mark(("a%s%d" % ("LR"[j == right], s), len(on if alone else up)), [], ["N" + "LR"[j == right]])
         (n1, k1_), (n2, k2_) = ((T.NL, "NL"), (T.NR, "NR")) if left in mine else ((T.NR, "NR"), (T.NL, "NL"))
 
+        def farkeys(_):
+            if far is not None:
+                ts(T.x3[:], T.koF[:, 48 * s + 12 * s:48 * s + 12 * t], 16.0, ALU.mult, ["koF"], ["x3"])
+                rnd(T.UF[:, 0:192:16], T.x3[:], M1K, ["x3", "UF"], ["UF0"])
+                tt(T.UF[:, 8:192:16], T.x3[:], T.UF[:, 0:192:16], ALU.subtract, ["x3", "UF0"], ["UF1"])
+                op("v", lambda: V.transpose(T.HF[:], T.UF[:]), ["UF", "UF0", "UF1"], ["HF"])
+                mm(T.pS[:, 256:448], T.WF[:], T.HF[:], True, True, ["WF", "HF"], ["pS"], True)
+                act(T.KF[:, A * s:A * t], T.pS[:, 256:448], ["pS"], ["KF%d" % s])
+
+        def farkeep(e):
+            if far is not None:
+                for k in range(s):
+                    put(FKEEP[k], T.Tf, T.koF[:, 48 * s + 12 * k:48 * s + 12 * k + 12], T.KF[:, A * k:A * k + A], ["koF", "KF%d" % k], "Tf")
+
+        def farbids(_):
+            if far is not None:
+                put(FBID, T.Tf, T.oF[:, 16 * s:16 * s + 12], T.KF[:, A * s:A * t], ["oF", "KF%d" % s], "Tf")
+                dma("s", n2[:, x], T.Tf[0:128:16, 0:W], ["Tf"], [k2_])
+            dma("s", T.Tw[0:128:16, 0:W], T.ZER[:], ["ZER"], ["Tw"])
+            if far is not None and t < RO - 1:
+                dma("s", T.Tf[0:128:16, 0:W], T.ZER[:], ["ZER"], ["Tf"])
+
         def near(_):
-            tt(T.pb5[:, 0:240], T.Tc[:, x], n1[:, x], ALU.min, [tc, k1_], ["pb5"])
+            tt(T.pb5[:, 0:240], T.Tc[:, x], n1[:, x], ALU.max, [tc, k1_], ["pb5"])
 
         def tables(_):
-            tt(T.Vc[:], T.pb5[:, 0:240], n2[:, x], ALU.min, ["pb5", k2_], ["Vc"])
-            ts(T.pb5[:, 256:496], T.Vc[:], MV, ALU.add, ["Vc"], ["pb5"], MV, ALU.subtract)
-            act(T.Pc[:, 0:240], T.Vc[:], ["Vc"], ["P0"])
-            dma("a", T.Vw[0:128:16, :], T.Pc[:, 0:240], ["P0"], ["V0"])
+            tt(T.Vc[:], T.pb5[:, 0:240], n2[:, x], ALU.max, ["pb5", k2_], ["Vc"])
+            rnd(T.pb5[:, 256:496], T.Vc[:], M256, ["Vc"], ["pb5"])
+            cp(T.Pc[:, 0:240], T.Vc[:], ["Vc"], ["P0"])
+            dma("s", T.Vw[0:128:16, 0:W], T.Pc[:, 0:240], ["P0"], ["V0"] + SK)
             tt(T.Pc[:, 480:720], T.Vc[:], T.pb5[:, 256:496], ALU.subtract, ["pb5", "Vc"], ["P2"])
+            dma("s", T.Vw[4:128:16, 0:W], T.Pc[:, 480:720], ["P2"], ["V2"])
             tt(T.Pc[:, 240:480], T.pb5[:, 256:496], T.Pc[:, 0:240], ALU.subtract, ["pb5", "P0"], ["P1"])
-            dma("s", T.Vw[2:128:16, :], T.Pc[:, 480:720], ["P2"], ["V2"])
-            dma("a", T.Vw[1:128:16, :], T.Pc[:, 240:480], ["P1"], ["V1"])
+            dma("s", T.Vw[8:128:16, 0:W], T.Pc[:, 240:480], ["P1"], ["V1"])
 
-        def append1(_):
-            ts(T.lw[:], T.oF[:], float(W), ALU.is_ge, ["oF"], ["lw"], 65536.0, ALU.mult)
-            tt(T.ck[:, 12:24], T.pP[:, 0:12], T.idl1[:], ALU.add, ["pP", "idl1"], ["ktF"])
-            tt(T.nlw[:], nl, T.lw[:], ALU.add, ["rs", "aK", "lw"], ["nlw"])
-            for j in range(2 * s1):
-                b0 = 128 + 12 * s1 * (j // s1)
-                mm(T.pP[:, b0 + j % s1:b0 + 12 * s1:s1], T.I23[:], T.nlw[:], True, True, ["nlw"], ["pP"])
-            for j in range(s1):
-                mm(T.pP[:, 256 + j:256 + 24 * s1:s1], T.I1[:], T.ck[:], True, True, ["ctF", "ktF", "I1"], ["pP"], j == s1 - 1)
-            if t >= 2:
-                tt(T.t12[:], T.nlw[:], T.dmpK[:], ALU.min, ["nlw", "dmpK"], ["t12"])
-                tt(T.no[:], T.t12[:], T.mK1[:], ALU.add, ["t12", "mK1"], ["no"])
-                cp(T.woU[:], T.no[:], ["no"], ["woU"])
+        def append(_):
+            count()
+            ts(T.x2[:], T.nbb[:], -1.0 / BIG, ALU.mult, ["nbb"], ["x2"], SAME, ALU.subtract)
+            tt(T.x1[:], T.AL[:, 4 - s:60:5], T.aLt[:, 12 * s:12 * t], ALU.mult, ["AL", "aLt"], ["x1"])
+            cp(T.PW[:, :, 4 - s], nl, ["rs", "aL"], ["PW"])
+            tt(T.KW[:, :, 4 - s], T.x2[:], T.CK[:], ALU.add, ["x2", "CK"], ["KW"])
+            cp(T.btU[:, 0:12 * t + 12], T.ST[:, :, 4 - t:5], ["ST"], ["btU"])
+            tt(T.PW[:], T.PW[:], T.AL[:], ALU.mult, ["PW", "AL"], ["PW"])
+            if t >= 3:
+                ts(T.x2[:], T.nn[:, 4:60:5], 3.0, ALU.is_ge, ["nn"], ["x2"], float(A * (RO - t)), ALU.mult)
+                tt(T.x1[:], T.x1[:], T.x2[:], ALU.add, ["x1", "x2"], ["x1"])
+            tt(T.PW[:, :, 4 - t], T.x1[:], nl, ALU.max, ["x1", "rs", "aL", "PW"], ["PW"])
+            if s:
+                ts(T.NS[:, :, 4 - s], T.nn[:, 4:60:5], 1.0, ALU.subtract, ["nn", "NS"], ["NS%d" % s])
+            cp(T.PC[:, 0:12 * t + 12], T.PW[:, :, 4 - t:5], ["PW"], ["PC"])
 
-        def append2(_):
-            v_ = slice(4 - s1, 4)
-            tt(T.ee[:, 0:24 * s1], T.pP[:, 128:128 + 24 * s1], T.K23[:, :, v_], ALU.is_equal, ["pP", "K23"], ["ee"])
-            tt(T.ee[:, 0:24 * s1], T.ee[:, 0:24 * s1], T.pP[:, 256:256 + 24 * s1], ALU.mult, ["ee", "pP"], ["ee"])
-            tt(T.St[:, :, v_], T.St[:, :, v_], T.ee[:, 0:24 * s1], ALU.add, ["St", "ee"], ["St"])
-            cp(T.btU[:, 0:12 * s1], T.St[:, 0:12, v_], ["St"], ["btU"])
-            tt(T.dl[:, :, v_], T.St[:, 0:12, v_], T.DUM[:, :, v_], ALU.subtract, ["St", "DUMk"], ["dl"])
+        def slots(_):
+            if t == RO - 1:
+                for k in range(3):
+                    ts(T.YQ[:, 60 * k:60 * k + 60], T.NS[:], float(k), ALU.is_equal, ["NS", "NS1", "NS2", "NS3"], ["YQ%d" % k])
 
-        cp(T.cG[:], T.Cw[:].indirect(T.ctU[:]), CK + ["ctU"], ["cG"])
-        if t == 1:
-            cp(T.Mw[:], T.Fw[:].indirect(T.ctU[:]), FK + ["ctU"], ["Mw"])
-        else:
-            tt(T.Mw[:], T.Fw[:].indirect(T.ctU[:]), T.Mn[:], ALU.max, FK + ["ctU", "Mn"], ["Mw"])
+        if s:
+            act(T.Mn[:], T.CM[:, 0:A * nblk].indirect(T.noU[:]), keys("CM") + ["noU"], ["Mn"])
+        if not EARLY:
+            cp(T.cG[:], T.Cw[:].indirect(T.ctU[:]), CK + ["ctU"], ["cG"])
+        Mw = T.CM[:, A * t:A * t + A]
+        mk = "CM%d" % t
 
-        def gat(ch):
-            gather(GENG[ch], T.Fg[:, 1024 * ch:1024 * ch + 1024], T.Fw[:], T.cG[:, 64 * ch:64 * ch + 64], FK + ["cG"], ["Fg%d" % ch])
+        def most(_):
+            if s:
+                tt(Mw, T.Fw[:].indirect(T.ctU[:]), T.Mn[:], ALU.max, FK + ["ctU", "Mn"], [mk])
+            else:
+                cp(Mw, T.Fw[:].indirect(T.ctU[:]), FK + ["ctU"], [mk])
 
-        def sub(ch):
+        def start(_):
+            mm(T.pb1[:, 0:192], T.Ib[:], Mw, True, True, ["Ib", mk], ["pb1"], True)
+            mm(T.pb0[:, 0:192], T.Ib[:], T.PST[:], True, False, ["Ib", "PST"], ["pb0"])
+
+        xs = lambda lo, hi, p: T.X[:, 16 * lo + (hi - lo) * p:16 * lo + (hi - lo) * (p + 1)]
+        fs = lambda lo, hi, p: T.Fg[:, 16 * lo + p:16 * hi:16]
+
+        def top(lo, hi):
+            mm(T.pb0[:, lo:hi], T.NB16[:], T.CM[:, A * t + lo:A * t + hi], False, False, ["NB16", mk], ["pb0"])
             for p in range(16):
-                b = 1 + (2 * ch + p // 8) % 4
-                o = banks[b][:, 64 * (p % 8):64 * (p % 8) + 64]
-                mm(o, T.Nb[:], T.Mw[:, 64 * ch:64 * ch + 64], True, False, ["Nb", "Mw"], ["pb%d" % b])
-                mm(o, T.Ib[:], T.Fg[:, 1024 * ch + p:1024 * ch + 1024:16], False, True, ["Ib", "Fg%d" % ch], ["pb%d" % b], p % 8 == 7)
+                tt(xs(lo, hi, p), fs(lo, hi, p), T.pb1[:, lo:hi], ALU.max, over("Fg", ORDER, lo, hi) + ["pb1"], ["X%d_%d" % (lo, p)])
 
-        def clip(ch):
+        def sub(lo, hi):
+            for p in range(16):
+                b = 2 + p // 8
+                o = banks[b][:, 64 * (p % 8):64 * (p % 8) + hi - lo]
+                mm(o, T.Nb[:], T.CM[:, A * t + lo:A * t + hi], True, False, ["Nb", mk], ["pb%d" % b])
+                mm(o, T.Ib[:], fs(lo, hi, p), False, True, ["Ib"] + over("Fg", ORDER, lo, hi), ["pb%d" % b], p % 8 == 7)
             for h in range(2):
-                b = 1 + (2 * ch + h) % 4
-                o = T.X[:, 1024 * ch + 512 * h:1024 * ch + 512 * h + 512]
-                xk = ["X%d" % (2 * ch + h)]
-                if RENG[2 * ch + h] == "a":
-                    act(o, banks[b][:], ["pb%d" % b], xk, func=AF.Relu)
-                else:
-                    ts(o, banks[b][:], 0.0, ALU.max, ["pb%d" % b], xk)
+                act(T.X[:, 16 * lo + 512 * h:16 * lo + 512 * h + 512], banks[2 + h][:], ["pb%d" % (2 + h)],
+                    ["X%d_%d" % (lo, p) for p in range(8 * h, 8 * h + 8)], func=AF.Relu)
 
-        def tot(ch):
+        def tot(lo, hi, end):
             for p in range(16):
-                last = ch == 2 and p == 15
-                mm(T.pb0[:, 64 * ch:64 * ch + 64], T.E2[:, 15 - p:143 - p], T.X[:, 1024 * ch + 64 * p:1024 * ch + 64 * p + 64],
-                   False, last, ["E2", "X%d" % (2 * ch + p // 8)], ["pb0"], last)
+                last = end and p == 15
+                mm(T.pb0[:, lo:hi], row(T.EG, p), xs(lo, hi, p), False, last, ["EG", "X%d_%d" % (lo, p)], ["pb0"], last)
 
-        steps = {"g": gat, "s": sub, "c": clip, "t": tot, "A": append1, "B": append2, "N": near, "T": tables,
-                 "P": lambda _: parts(t, T.ctU[:], "ctU"), "S": lambda _: scores(t),
-                 "I": lambda _: mm(T.pb0[:, 0:192], T.I23[:], T.PST[:], True, False, ["I23", "PST"], ["pb0"])}
-        for st in ORDER.split():
-            steps[st[0]](int(st[1:] or 0))
+        steps = {"A": append, "N": near, "T": tables, "Y": slots, "M": most, "U": farkeys, "K": farkeep, "B": farbids, "I": start,
+                 "S": lambda _: act(T.CS[:, A * t:A * t + A], T.pb0[:, 0:192], ["pb0"], ["CS%d" % t]),
+                 "C": lambda _: cp(T.CC[:, A * t:A * t + A], T.cG[:], ["cG"], ["CC%d" % t])}
+        for e, lo, hi in spans(ORDER):
+            if e in "av":
+                gather(e, T.Fg[:, 16 * lo:16 * hi], T.Fw[:], T.cG[:, lo:hi], FK + ["cG"], ["Fg%d" % lo])
+            elif e in "tz":
+                tot(lo, hi, e == "z")
+            elif e in "xr":
+                (top if e == "x" else sub)(lo, hi)
+            else:
+                steps[e](lo)
 
     total["sent"] = sent[0]
     for s_, v_ in total.items():

@@ -5,25 +5,25 @@ N, Q, A, RO = 6, 640, 192, 5
 W = N * Q
 U24 = float(2 ** 24)
 BIG = 65536.0
+M1 = 1.5 * 2.0 ** 23
 M16 = 1.5 * 2.0 ** 27
 M256 = 1.5 * 2.0 ** 31
 M1K = 1.5 * 2.0 ** 33
 SAME = 12.0 * BIG
-VW, TW = 4096, 4032
+VW, FO = 4096, 256
 SPLIT = 528
-ORDER = "B a0:64 M v64:104 I a104:128 a128:192 A x0:128 t0:128 r128:192 N T z128:192 S C Y"
-LISTS = False
-FKEEP = "aaa"
-FBID = "v"
 NMV = 4
-CSPLIT = {1: 12, 2: 18, 3: 24, 4: 30}
+NRED = 6
+P0A = True
+EARLY = True
+ORDER = "H a0:64 a64:112 M v112:192 I r0:64 O L A r64:128 N T"
+AFTER = "D2 t0:64 r128:192 D0 G D1 t64:128 z128:192 C S Y"
 VP0 = "a0:32 v32:64 m0:64 a64:96 v96:128 m64:128 a128:160 v160:192 M128:192 C"
-VP1 = "a0:40 P v40:64 m0:64 a64:96 v96:128 m64:128 a128:164 v164:192 M128:192 K k0"
-VP2 = "a0:40 P v40:64 m0:64 a64:96 v96:128 m64:128 a128:164 v164:192 M128:192 K k0 k1"
-VP3 = "a0:40 P v40:64 m0:64 a64:96 v96:128 m64:128 K a128:176 v176:192 M128:192 k0 k1 k2"
-VP4 = "a0:40 P v40:64 m0:64 a64:96 v96:128 m64:128 K a128:192 M128:192 e0 k1 k2 k3 Y"
+VP1 = "P K a0:36 v36:64 m0:64 a64:96 v96:128 m64:128 a128:160 v160:192 M128:192 k0"
+VP2 = "P K a0:36 v36:64 m0:64 a64:96 v96:128 m64:128 a128:160 v160:192 M128:192 k0 k1"
+VP3 = "P K a0:36 v36:64 m0:64 a64:96 v96:128 m64:128 a128:160 v160:192 M128:192 k0 k1 k2"
+VP4 = "P K a0:40 v40:64 m0:64 a64:112 e0 v112:128 m64:128 a128:168 v168:192 Y0 M128:192 Y1 k1 k2 R k3"
 VPLAN = (VP0, VP1, VP2, VP3, VP4)
-EARLY = False
 
 
 def spans(plan_):
@@ -36,25 +36,26 @@ def over(name, plan_, lo, hi):
 
 f32, bf, i32, u16 = "float32", "bfloat16", "int32", "uint16"
 SB = {
-    bf: dict(Fw=W, Vw=VW, E1=160, ES=152, EG=160, EV=160, E16=160, EW=160, Z=320, BLK=128, Ib=128, Nb=128, WK=128, UT=192,
-             PST=192, MCb=8, MKb=8, SL=480, Vs=960, Vg=3072, xx=12, H=192, Bt=192, B=192, junk=1152, Mn=192, CM=1152,
-             Fg=3072, X=3072, Pc=720, NB16=128, UF=192, HF=192, WF=128),
-    u16: dict(Cu=W, hU=12, btU=60, koU=240, koF=192, noU=12, cU=192, ctU=12, oU=80, oF=64, poU=12, cG=192),
-    i32: dict(Cw=W, hI=12, pI=8, CC=1152),
-    f32: dict(Tw=TW, Tf=TW, KF=768, CS=1152, KR=960, col=24, AR=192, JG=128, XG=160, XP=160, I24=128, MC=8, FL=12, EQ=12, RJ=12, P2=12, OH=16,
-              CD=192, RS=192, R5=180, PC=60, aL=12, aT=12, aLt=48, C16=12, CG=12, CT=12, CK=12, t12=12, ZER=240, rs=60,
-              S1=192, sc=192, sT=192, rm=192, Hh=12, ck=12, nbb=12, nob=12, Wr=12, x1=12, x2=12, x3=12, AL=60, nn=60, Sr=80,
-              Tc=960, NL=960, NR=960, Vc=240, X1=60, YQ=180, YS=180, yL=36, yB=36, yE=36, yW=36, yo=576),
+    bf: dict(Fw=W, Vw=VW, WM=128, NO=128, E1=160, ES=152, EG=160, EV=160, E16=160, EW=160, EL=160, EF=160, Z=320, BLK=128, Ib=128, Nb=128,
+             WK=128, WT=128, UT=192, PST=192, MCb=8, MKb=8, SL=480, LO=768, Vg=3072, xx=12, H=192, Bt=192, B=192,
+             junk=1536, Mn=192, CM=1152, Fg=3072, X=3072, Pc=3 * FO),
+    u16: dict(Cu=W, hU=12, sgU=8, lU=48, koU=48, noU=12, cU=192, ctU=12, oU=12, poU=12, cG=192),
+    i32: dict(Ci=Q, hI=12, pI=8),
+    f32: dict(Cw=W, Tw=VW, CC=1152, CS=1152, KR=960, KM=768, col=24, AR=192, JG=128, XP=160, I24=128, NI=128, MC=8, FL=12, EQ=12,
+              RJ=12, P2=12, OH=16, G8=8, CD=192, RS=192, aL=12, aT=12, aLt=48, C16=12, CG=12, CT=12, ZC=48, Y2=72, ZER=FO,
+              ST=48, PW=48, DUM=48, NS=48, IN=48, X1=48, U=60, rs=12, S1=192, sc=192, sT=192, rm=192, Hh=12, ck=12, nbb=12,
+              nob=12, Wr=12, t12=12, x1=12, x2=24, x3=12, fr=12, Sr=80, Tc=4 * FO, NL=4 * FO, NR=4 * FO, Vc=FO,
+              yB=36, yE=24, y8=576, yo=768),
 }
 SCRATCH = {n_: ("sbuf", [128, c_], d_) for d_, t_ in SB.items() for n_, c_ in t_.items()}
-SCRATCH.update({n_: ("sbuf", [128, 12, 5], f32) for n_ in ("ST", "PW", "KW", "DUM", "Zk", "NS")})
+SCRATCH["YQ"] = ("sbuf", [128, 4, 3, 12], f32)
 SCRATCH["Abd"] = ("sbuf", [128, 12, 8, 16], bf)
 BANKS = ["pb0", "pb1", "pb2", "pb3", "pb4", "pb5", "pS", "pP"]
 SCRATCH.update({n_: ("psum", [128, 512], f32) for n_ in BANKS})
-NDS = 48
+NDS = 40
 SEMAPHORES = (["qv", "qa", "qp", "qg", "sent"] + ["a%s%d%d" % (k_, j, h) for k_ in "FC" for j in range(N) for h in range(2)]
               + ["aS%d" % j for j in range(N)]
-              + ["a%s%d" % (k_, t) for k_ in "LRGKO" for t in range(4)] + ["d%d" % i for i in range(NDS)])
+              + ["a%s%d" % (k_, t) for k_ in "LR" for t in range(4)] + ["d%d" % i for i in range(NDS)])
 
 
 def bits(es):
@@ -105,11 +106,11 @@ def helper_program(g, core, T, topo, cores, big, small, r):
     g.remote_dma_fused([xfer(topo, core, far[h::2], ap, ap, sem, off[h::2]) for h in range(2)], local_sem=T.sem.sent)
     sent = 2 * n4
     if r in big:
-        for kind, dst, es in (("C", far, off[0::2]), ("F", [far[(big.index(r) + 1) % 2]], off[1::2])):
+        for kind, es in (("C", off[0::2]), ("F", off[1::2])):
             ap = piece(T, big, kind, r, 1)
             sem = T.sem["a%s%d1" % (kind, r)]
             g.wait_ge(sem, n4)
-            g.remote_dma_fused([xfer(topo, core, dst, ap, ap, sem, es)], local_sem=T.sem.sent)
+            g.remote_dma_fused([xfer(topo, core, far, ap, ap, sem, es)], local_sem=T.sem.sent)
             sent += n4
     g.wait_ge(T.sem.sent, sent)
 
@@ -225,14 +226,20 @@ def rank_program(g, core, T, topo):
     def row(E, q):
         return E[:, 23 - q:151 - q]
 
+    def wrap(out, E, src, n_, first, r, w):
+        for q in range(16):
+            mm(out, row(E, q), src[:, q:n_:16], first and q == 0, q == 15, r, w, q == 15)
+
     FK = ["F%d%d" % (j, h) for j in range(N) for h in range(2)]
     CK = ["C%d%d" % (j, h) for j in range(N) for h in range(2)]
     VK = ["V0", "V1", "V2"]
+    SK = ["S%d" % j for j in range(N)]
     me = slice(rank * Q, (rank + 1) * Q)
     fme = "F%d0" % rank
+    blk = lambda X, k, n_=12: X[:, n_ * k:n_ * k + n_]
 
     dma("s", T.Fw[:, me], T.feat[:], [], [fme])
-    dma("s", T.Cw[:, me], T.nb[:], [], ["C%d0" % rank])
+    dma("s", T.Ci[:], T.nb[:], [], ["Ci"])
     dma("a", T.hI[:], T.home[:], [], ["hI"])
     op("g", lambda: g.iota(T.pI[:, 0:1], [[0, 1]], 0, 1), [], ["pI"])
     iota(T.RJ[:], [[4, 4], [1, 3]], 1, ["RJ"])
@@ -249,22 +256,19 @@ def rank_program(g, core, T, topo):
     upA, upB = up[0::2], up[1::2]
     n4 = len(offC)
     left, right = (rank - 1) % N, (rank + 1) % N
-    close = [j for j in (left, right) if j in mine]
-    far = ([j for j in (left, right) if j in other] + [None])[0]
-    if not LISTS:
-        close, far = sorted((left, right), key=lambda j: j in other), None
+    ring = sorted((left, right), key=lambda j: j in other)
     key = lambda kind, j, h: "%s%d%d" % ("F" if kind == "F" else "U", j, h)
     if rank in big:
         fwd = [(kind, small[i // 2], i % 2) for kind in "CF"]
     else:
-        fwd = [("C", r, 0) for r in big[i::2]] + [("F", r, 0) for r in big[i::2]] + [("F", r, 1) for r in big[1 - i::2]]
+        fwd = [(kind, r, 0) for kind in "CF" for r in big[i::2]]
     for j in range(N):
         if j != rank:
             mark(("aS%d" % j, n4), [], ["SL%d" % j])
             for kind in "FC":
                 for h in range(2):
                     if j in mine and rank in big:
-                        mark(("a%s%d0" % (kind, j), len(up)), [], [key(kind, j, h)])
+                        mark(("a%s%d%d" % (kind, j, h * (kind == "C")), len(up)), [], [key(kind, j, h)])
                         continue
                     n_ = n4
                     if j in other and rank in big and (kind, j, h) in fwd:
@@ -292,103 +296,95 @@ def rank_program(g, core, T, topo):
 
     double(0, 1)
     tt(T.ES[:], T.E1[:, 0:152], T.E1[:, 8:160], ALU.add, ["E1"], ["ES"])
-    double(1, 9)
-    dma("s", T.Tw[0:128:16, 0:W], T.ZER[:], ["ZER"], ["Tw"])
+    double(1, 3)
+    dma("s", T.Tw[0:128:16, :], T.ZER[:], ["ZER"], ["Tw"])
 
-    sl = slice(80 * rank, 80 * rank + 80)
     for E, b in ((T.ES, "pb0"), (T.E1, "pb1")):
         for h in range(8):
             mm(T[b][:, 0:80], E[:, 15 - h:143 - h], T.Fw[:, rank * Q + 80 * h:rank * Q + 80 * h + 80], h == 0, h == 7,
                ["ES", "E1", fme], [b], h == 7)
+    a_ = blk(T.SL, rank, 80)
     rnd(T.Sr[:], T.pb0[:, 0:80], M16, ["pb0"], ["Sr"])
-    tt(T.SL[:, sl], T.Sr[:], T.pb1[:, 0:80], ALU.subtract, ["Sr", "pb1"], ["SL%d" % rank])
-    cp(T.Cu[:, me], T.Cw[:, me], ["C%d0" % rank], ["U"])
-    a_ = T.SL[:, sl]
+    tt(a_, T.Sr[:], T.pb1[:, 0:80], ALU.subtract, ["Sr", "pb1"], ["SL%d" % rank])
+    cp(T.Cu[:, me], T.Ci[:], ["Ci"], ["U"])
     send([([helper[rank]], a_, a_, "aS%d" % rank, offS), (peers, a_, a_, "aS%d" % rank, upA)], ["SL%d" % rank])
 
     def part(dst, kind, j, h, es):
         a_ = piece(T, big, kind, j, h)
         return (dst, a_, a_, "a%s%d%d" % (kind, j, h), es)
 
-    def whole(kind):
-        a_ = (T.Fw if kind == "F" else T.Cu)[:, me]
-        send([(peers, a_, a_, "a%s%d0" % (kind, rank), up)], [fme, "U"])
-
     if rank in big:
         near_, far_ = [helper[rank]], [cores[small[i % 2]]]
-        send([part(near_, "C", rank, 1, upB)], ["U"])
-        send([part(far_, "C", rank, 0, offC)], ["U"])
-        whole("C")
+        for h in range(2):
+            send([part((far_, near_)[h], "C", rank, h, (offC, offS)[h]), part(peers, "C", rank, h, up)], ["U"])
         send([part(far_, "F", rank, 0, offC), part(near_, "F", rank, 1, offS)], [fme])
         for kind, j, h in fwd:
             send([part([d], kind, j, h, es) for d, es in zip(peers, (upA, upB, offS))], [key(kind, j, h)])
             if kind == "C":
-                whole("F")
+                send([(peers, T.Fw[:, me], T.Fw[:, me], "aF%d0" % rank, up)], [fme])
     else:
         for kind in "CF":
             send([part([cores[big[2 * i + h]]], kind, rank, h, offC[2 * h:2 * h + 2]) for h in range(2)]
                  + [part(peers, kind, rank, h, (upA, upB)[h]) for h in range(2)], [fme, "U"])
         for c in fwd[0:2]:
             send([part(peers, *c, up)], [key(*c)])
-        for cs in (fwd[2:4], fwd[4:6]):
-            send([part(peers, *c, es) for c, es in zip(cs, (upA, upB))], [key(*c) for c in cs])
-    double(9, 12)
+        send([part(peers, *c, es) for c, es in zip(fwd[2:4], (upA, upB))], [key(*c) for c in fwd[2:4]])
+
+    aff(T.aL[:], T.AR[:, 0:192:16], 1.0, c_(1), ["AR", "c0"], ["aL"])
+    aff(T.XP[:], T.AR[:, 0:160], -1.0, c_(0), ["AR", "c0"], ["XP"])
+    aff(c_(16), c_(1), -1.0, 7.5, ["c0"], ["c16"])
+    aff(c_(17), c_(1), 1.0, (1087.0 - A * rank) / 128.0, ["c0"], ["c17"])
+    aff(T.X1[:, 0:12], T.AR[:, 0:12], 0.0, 2.0, ["AR"], ["X1"])
+    act(T.UT[:], T.AR[:], ["AR"], ["UT"], scale=0.0)
+    between = [
+        lambda: ts(T.OH[:], T.AR[:, 0:16], c_(1), ALU.is_equal, ["AR", "c0"], ["OH"]),
+        lambda: ts(T.G8[:], T.AR[:, 0:8], c_(2), ALU.is_equal, ["AR", "c0"], ["G8"]),
+        lambda: scan(T.P2[:], T.X1[:, 0:12], T.ZER[:, 0:12], -0.25, ALU.mult, ALU.add, ["X1", "ZER"], ["P2"]),
+        lambda: ts(c_(7), c_(3), 16.0, ALU.is_lt, ["c0"], ["c7"]),
+        lambda: tt(T.P2[:], T.P2[:], T.EQ[:], ALU.mult, ["P2", "EQ"], ["P2"]),
+        lambda: cp(T.hU[:], T.hI[:], ["hI"], ["hU"]),
+        lambda: ts(T.BLK[:], T.JG[:], c_(2), ALU.is_equal, ["JG", "c0"], ["BLK"])]
+    for j, f in enumerate(between):
+        double(3 + j, 4 + j)
+        f()
+    aff(c_(9), o_(0), 1.0, o_(8), ["OH"], ["c9"])
+    act(c_(10), o_(4), ["OH"], ["c10"], scale=4096.0)
+    act(c_(22), o_(8), ["OH"], ["c22"], scale=-16.0)
+    act(c_(21), o_(12), ["OH"], ["c21"], scale=U24)
+    act(c_(23), o_(4), ["OH"], ["c23"], scale=-2.0 * BIG)
+    aff(c_(8), c_(7), -1.0, 1.0, ["c7"], ["c8"])
+    aff(c_(11), o_(0), 16.0, c_(22), ["OH", "c22"], ["c11"])
+    aff(c_(12), c_(9), BIG, c_(10), ["c9", "c10"], ["c12"])
+    aff(c_(13), c_(9), 128.0, o_(4), ["c9", "OH"], ["c13"])
+    aff(c_(14), c_(9), -2.0 * BIG, c_(23), ["c9", "c23"], ["c14"])
+    aff(c_(15), o_(12), float(1856 - A * rank), c_(13), ["OH", "c13"], ["c15"])
+    act(T.MC[:], T.G8[:], ["G8"], ["MC"], scale=BIG * BIG)
+    act(T.MKb[:], T.G8[:], ["G8", "c12"], ["MKb"], func=AF.Identity, scale=c_(12))
+    for j in (10, 11):
+        act(T.Vw[:, 2 ** j:2 ** (j + 1)], T.Vw[:, 0:2 ** j], VK + ["FL"], VK, func=AF.Identity, scale=T.FL[:, j:j + 1])
+    ts(T.sgU[:], T.ZER[:, 0:8], c_(1), ALU.add, ["c0", "ZER"], ["sgU"], float(FO), ALU.mult)
     for j in [rank] + [j for j in mine if j != rank] + other:
-        dma("s", T.Vw[0:128:8, j * Q:(j + 1) * Q], T.SL[:, 80 * j:80 * j + 80], ["SL%d" % j, "V0"], ["S%d" % j])
-    SK = ["S%d" % j for j in range(N)]
-
-    parts = [("C", j, h) for j in mine if j != rank for h in range(2)] + [c for c in fwd if c[0] == "C"]
-    parts += [("C", j, h) for h in (1, 0) for j in other if ("C", j, h) not in parts]
-
-    def widen():
-        for c in parts:
-            cp(T.Cw[:, span(big, *c)], T.Cu[:, span(big, *c)], [key(*c)], ["C%d%d" % c[1:]])
-
-    ts(T.OH[:], T.AR[:, 0:16], c_(1), ALU.is_equal, ["AR", "c0"], ["OH"])
-    ts(T.aL[:], T.AR[:, 0:192:16], c_(1), ALU.add, ["AR", "c0"], ["aL"])
-    ts(T.XP[:], T.AR[:, 0:160], c_(0), ALU.subtract, ["AR", "c0"], ["XP"])
-    ts(c_(7), c_(3), 16.0, ALU.is_lt, ["c0"], ["c7"])
-    ts(c_(8), c_(3), 16.0, ALU.is_ge, ["c0"], ["c8"])
-    tt(c_(9), o_(0), o_(8), ALU.add, ["OH"], ["c9"])
-    ts(c_(10), o_(4), 4096.0, ALU.mult, ["OH"], ["c10"])
-    ts(c_(11), o_(0), o_(8), ALU.subtract, ["OH"], ["c11"], 16.0, ALU.mult)
-    ts(c_(16), c_(1), -1.0, ALU.mult, ["c0"], ["c16"], 7.5, ALU.add)
-    ts(c_(17), c_(1), (1087.0 - A * rank) / 128.0, ALU.add, ["c0"], ["c17"])
-    ms(T.X1[:, 0:12], 2.0, ["X1"])
-    cp(T.hU[:], T.hI[:], ["hI"], ["hU"])
-    ts(c_(12), c_(9), BIG, ALU.mult, ["c9", "c10"], ["c12"], c_(10), ALU.add)
-    ts(c_(13), c_(9), 128.0, ALU.mult, ["c9", "OH"], ["c13"], o_(4), ALU.add)
-    ts(c_(14), c_(9), o_(4), ALU.add, ["c9", "OH"], ["c14"], -2.0 * BIG, ALU.mult)
-    scan(T.P2[:], T.X1[:, 0:12], T.ZER[:, 0:12], -0.25, ALU.mult, ALU.add, ["X1", "ZER"], ["P2"])
-    ts(T.I24[:], T.XP[:, 0:128], 0.0, ALU.is_equal, ["XP"], ["I24"], U24, ALU.mult)
-    ts(T.BLK[:], T.JG[:], c_(2), ALU.is_equal, ["JG", "c0"], ["BLK"])
-    ts(T.Z[:, 0:160], T.XP[:], 16.0, ALU.is_equal, ["XP", "c7"], ["Z0"], c_(7), ALU.mult)
-    ts(T.Z[:, 160:320], T.XP[:], 16.0, ALU.is_equal, ["XP", "c8"], ["Z1"], c_(8), ALU.mult)
-    tt(T.P2[:], T.P2[:], T.EQ[:], ALU.mult, ["P2", "EQ"], ["P2"])
-    ts(c_(15), o_(12), float(1856 - A * rank), ALU.mult, ["OH", "c13"], ["c15"], c_(13), ALU.add)
-    ts(T.MC[:], T.AR[:, 0:8], c_(2), ALU.is_equal, ["AR", "c0"], ["MC"], BIG * BIG, ALU.mult)
-    ts(T.MKb[:], T.AR[:, 0:8], c_(2), ALU.is_equal, ["AR", "c0", "c12"], ["MKb"], c_(12), ALU.mult)
+        dma("s", T.Vw[0:128:8, j * Q:(j + 1) * Q], blk(T.SL, j, 80), ["SL%d" % j, "V0"], ["S%d" % j])
     op("v", lambda: V.tensor_reduce(c_(18), T.P2[:], AxisListType.X, ALU.add), ["P2"], ["c18"])
-    ms(T.UT[:], 0.0, ["UT"])
-    if far is not None:
-        ts(c_(19), o_(12), float(1856 - A * far), ALU.mult, ["OH", "c13"], ["c19"], c_(13), ALU.add)
-        dma("s", T.Tf[0:128:16, 0:W], T.ZER[:], ["ZER"], ["Tf"])
-    ms(T.RS[:], U24, ["RS"])
-    ms(T.R5[:], 1.0, ["R5"])
-    ms(T.KW[:], -1.0, ["KW"])
-    ms(T.PW[:], 0.0, ["PW"])
-    ms(T.NS[:], 0.0, ["NS"])
-    ms(T.CC[:, 4 * A:6 * A], 0, ["CC4", "CC5"])
-    widen()
+    op("v", lambda: V.tensor_reduce(c_(19), T.P2[:, 0:8], AxisListType.X, ALU.add), ["P2"], ["c19"])
+    ts(T.I24[:], T.XP[:, 0:128], 0.0, ALU.is_equal, ["XP"], ["I24"], U24, ALU.mult)
+    ts(c_(20), c_(18), c_(19), ALU.not_equal, ["c18", "c19"], ["c20"], -U24 / 4, ALU.mult)
+    ts(T.Z[:, 0:160], T.XP[:], -16.0, ALU.is_equal, ["XP", "c7"], ["Z0"], c_(7), ALU.mult)
+    ts(T.Z[:, 160:320], T.XP[:], -16.0, ALU.is_equal, ["XP", "c8"], ["Z1"], c_(8), ALU.mult)
+    cp(T.Cw[:, me], T.Ci[:], ["Ci"], ["C%d0" % rank])
+    parts = [("C", j, h) for h in range(2) for j in mine if j != rank] + [c for c in fwd if c[0] == "C"]
+    parts += [("C", j, h) for h in (1, 0) for j in other if ("C", j, h) not in parts]
+    for c in parts:
+        cp(T.Cw[:, span(big, *c)], T.Cu[:, span(big, *c)], [key(*c)], ["C%d%d" % c[1:]])
 
     zero = T.AR[:, 0:12]
-    act(T.E16[:], T.E1[:], ["E1", "c11"], ["E16"], func=AF.Identity, scale=c_(11))
+    weigh = lambda out, in_, j, r, w: act(out[:], in_[:], r + ["c%d" % j], w, func=AF.Identity, scale=c_(j))
+    weigh(T.E16, T.E1, 11, ["E1"], ["E16"])
     aff(T.PST[:], T.AR[:], 0.0, c_(16), ["AR", "c16"], ["PST"])
     act(T.Ib[:], T.I24[:], ["I24"], ["Ib"], scale=1.0 / U24)
-    act(T.Nb[:], T.I24[:], ["I24"], ["Nb"], scale=-1.0 / U24)
     act(T.MCb[:], T.MC[:], ["MC"], ["MCb"])
+    aff(T.RS[:], T.AR[:], 0.0, U24, ["AR"], ["RS"])
     aff(T.RS[:, 0:192:16], zero, 0.0, 7.5, ["AR", "RS"], ["RS"])
-    aff(T.R5[:, 0:180:5], T.AR[:, 0:36], 0.0, 0.0, ["AR", "R5"], ["R5"])
     for h in range(2):
         aff(T.aT[:, h:12:2], T.AR[:, 0:192:32], 1.0, c_(3), ["AR", "c0"], ["aT%d" % h])
     aff(T.UT[:, 4:192:16], T.aT[:], -1.0, 191.0, ["aT0", "aT1", "UT"], ["UTs"])
@@ -396,30 +392,40 @@ def rank_program(g, core, T, topo):
     aff(T.C16[:], T.aL[:], 16.0 / U24, 7.5 / U24, ["aL"], ["C16"])
     aff(T.CG[:], T.aL[:], -1.0 / 16.0 / U24, (SAME + 191.0 / 16.0) / U24, ["aL"], ["CG"])
     aff(T.CT[:], zero, 0.0, 2047.5 / U24, ["AR"], ["CT"])
-    aff(T.CK[:], T.aL[:], 7.0 / 128.0, (2047.5 - A * rank - 8 * 191) / 128.0, ["aL"], ["CK"])
-    for k in range(5):
-        aff(T.DUM[:, :, k], T.aL[:], 1.0, float(W), ["aL"], ["DUM"])
+    DK = ["DUM%d" % k for k in range(4)]
     for k in range(4):
-        act(T.aLt[:, 12 * k:12 * k + 12], T.aL[:], ["aL"], ["aLt"], func=AF.Silu, bias=float(A * k + A))
-    if far is not None:
-        act(T.UF[:], T.UT[:], ["UT", "UTs", "UTo"], ["UF"])
-        act(T.WF[:], T.BLK[:], ["BLK", "c19"], ["WF"], func=AF.Identity, scale=c_(19))
-    act(T.ST[:], T.DUM[:], ["DUM"], ["ST"])
-    act(T.Zk[:], T.DUM[:], ["DUM"], ["Zk"], scale=0.0)
-    act(T.EW[:], T.E1[:], ["E1", "c18"], ["EW"], func=AF.Identity, scale=c_(18))
-    act(T.WK[:], T.BLK[:], ["BLK", "c15"], ["WK"], func=AF.Identity, scale=c_(15))
-    act(T.EG[:], T.E1[:], ["E1"], ["EG"], scale=16.0)
-    act(T.NB16[:], T.BLK[:], ["BLK"], ["NB16"], scale=-16.0)
-    act(T.EV[:], T.E1[:], ["E1", "c14"], ["EV"], func=AF.Identity, scale=c_(14))
-    aff(T.CD[:], T.AR[:], -1.0 / 128.0, c_(17), ["AR", "c17"], ["CD"])
-    for t in (4, 5):
-        aff(T.CS[:, A * t:A * t + A], T.AR[:], 0.0, -8.0, ["AR"], ["CS%d" % t])
-    for t in (0, 4, 5):
-        act(T.CM[:, A * t:A * t + A], T.AR[:], ["AR"], ["CM%d" % t], scale=0.0)
+        act(blk(T.DUM, k), T.aL[:], ["aL"], [DK[k]], func=AF.Silu, bias=float(W))
+    act(T.ST[:], T.DUM[:], DK, ["ST"])
+    weigh(T.EW, T.E1, 18, ["E1"], ["EW"])
+    weigh(T.WK, T.BLK, 15, ["BLK"], ["WK"])
 
-    def count():
-        ts(T.AL[:], T.ST[:], float(W), ALU.is_lt, ["ST"], ["AL"])
-        scan(T.nn[:], T.R5[:, 0:60], T.AL[:], 0.0, ALU.mult, ALU.add, ["R5", "AL"], ["nn"])
+    def later(k):
+        if k == 2:
+            for n_ in ("CM", "CC"):
+                act(T[n_][:, 4 * A:6 * A], T.Cw[:, 0:2 * A], CK, [n_ + "4", n_ + "5"], scale=0.0)
+            return
+        if k == 0:
+            act(T.Nb[:], T.I24[:], ["I24"], ["Nb"], scale=-1.0 / U24)
+            act(T.EG[:], T.E1[:], ["E1"], ["EG"], scale=16.0)
+            weigh(T.EV, T.E1, 14, ["E1"], ["EV"])
+            weigh(T.EL, T.E1, 19, ["E1"], ["EL"])
+            act(T.EF[:], T.E1[:], ["E1"], ["EF"], scale=-2.0 * BIG)
+            act(T.NI[:], T.I24[:], ["I24"], ["NI"], scale=-BIG / U24)
+            aff(T.CD[:], T.AR[:], -1.0 / 128.0, c_(17), ["AR", "c17"], ["CD"])
+        else:
+            act(blk(T.CM, 0, A), T.AR[:], ["AR"], ["CM0"], scale=0.0)
+            act(T.NS[:], T.AR[:, 0:48], ["AR"], ["NS"], scale=0.0)
+        for j in ((0,), (1, 2, 3))[k]:
+            aff(blk(T.aLt, j), T.aL[:], 1.0, A * j + A + 0.125, ["aL"], ["aLt%d" % j])
+            aff(blk(T.ZC, j), zero, 0.0, (A * j + A - 0.5) * BIG / U24, ["AR"], ["ZC%d" % j])
+        if k == 1:
+            aff(T.CS[:, 4 * A:6 * A], T.Cw[:, 0:2 * A], 0.0, -8.0, CK, ["CS4", "CS5"])
+            weigh(T.WT, T.BLK, 18, ["BLK"], ["WT"])
+            aff(T.yE[:, 12:24], T.aL[:], 1.0, 3.0 * A, ["aL"], ["yD"])
+
+    def level(nl):
+        rnd(T.fr[:], nl, M1, ["rs"], ["fr"])
+        tt(T.fr[:], nl, T.fr[:], ALU.subtract, ["rs", "fr"], ["fr"])
 
     banks = [T.pb0, T.pb1, T.pb2, T.pb3, T.pb4, T.pb5]
     for t in range(1, RO + 1):
@@ -428,18 +434,22 @@ def rank_program(g, core, T, topo):
         nblk = t if t < 4 else 6
         keys = lambda n_: ["%s%d" % (n_, j) for j in range(nblk)]
         vk = VK if s else VK + SK
-        todo = []
         if s:
-            hk = CSPLIT[s]
-            cp(T.Vs[:, 0:16 * hk], T.Vw[:].indirect(T.btU[:, 0:hk]), VK + ["btU"], ["Vs0"])
-            act(T.Vs[:, 16 * hk:A * t], T.Vw[:].indirect(T.btU[:, hk:12 * t]), VK + ["btU"], ["Vs1"])
+            nl = T.rs[:]
             mm(T.pS[:, 0:192], T.I24[:], T.CD[:], True, False, ["I24", "CD"], ["pS"])
-            mm(T.pP[:, 0:12 * t], T.I24[:], T.KW[:, :, 5 - t:5], True, False, ["I24", "KW"], ["pP"])
-            for q in range(16):
-                mm(T.pP[:, 0:12 * t], row(T.EV, q), T.Vs[:, q:A * t:16], False, q == 15, ["EV", "Vs0", "Vs1"], ["pP"], q == 15)
-            scan(T.rs[:, 0:12 * t], T.pP[:, 0:12 * t], T.PC[:, 0:12 * t], 0.0, ALU.min, ALU.max, ["pP", "PC"], ["rs"])
-            nl = T.rs[:, s:12 * t:t]
+            mm(T.pb2[:, 0:12 * s], T.I24[:], T.ZC[:, 0:12 * s], True, False, ["I24"] + ["ZC%d" % k for k in range(s)], ["pb2"])
+            mm(T.pP[:, 0:12 * s], T.I24[:], T.IN[:, 0:12 * s], True, False, ["I24", "IN"], ["pP"])
+            wrap(T.pP[:, 0:12 * s], T.EF, T.LO, A * s, False, ["EF", "LO"], ["pP"])
+            tt(T.U[:, 12:12 * t], T.pP[:, 0:12 * s], T.PW[:, 0:12 * s], ALU.max, ["pP"] + ["PW%d" % k for k in range(s)], ["U"])
+            if s >= 3:
+                tt(T.x2[:], T.U[:, 12 * s - 36:12 * s - 12], T.U[:, 12 * s - 12:12 * s + 12], ALU.min, ["U", "Ut"], ["x2"])
+            pair = (T.x2[:, 0:12], T.x2[:, 12:24]) if s >= 3 else (blk(T.U, s - 1), blk(T.U, s))
+            tt(T.x1[:] if s % 2 == 0 else nl, pair[0], pair[1], ALU.min, ["U", "Ut", "x2"], ["x1" if s % 2 == 0 else "rs"])
+            if s % 2 == 0:
+                tt(nl, T.x1[:], blk(T.U, 0), ALU.min, ["x1", "Ut"], ["rs"])
             cp(T.noU[:], nl, ["rs"], ["noU"])
+            for k in range(s):
+                mm(blk(T.pb2, k), T.NI[:], nl, False, k == s - 1, ["NI", "rs"], ["pb2"], k == s - 1)
             cp(T.cU[:], T.CC[:, 0:A * nblk].indirect(T.noU[:]), keys("CC") + ["noU"], ["cU"])
 
             def pick(_):
@@ -447,35 +457,42 @@ def rank_program(g, core, T, topo):
                 mm(T.pS[:, 0:192], T.I24[:], T.S1[:], False, False, ["S1"], ["pS"])
 
             def kill(_):
-                for k in range(s):
-                    ts(T.Zk[:, :, 4 - k], nl, float(A * k + A), ALU.is_lt, ["rs"], ["Zk%d" % k], BIG, ALU.mult)
-                tt(T.ST[:], T.ST[:], T.Zk[:], ALU.max, ["ST", "Zk"] + ["Zk%d" % k for k in range(s)], ["ST"])
-                tt(T.ST[:], T.ST[:], T.DUM[:], ALU.min, ["ST", "DUM"], ["ST"])
-                for k in range(s):
-                    cp(T.koU[:, 48 * s + 12 * k:48 * s + 12 * k + 12], T.ST[:, :, 4 - k], ["ST", "koU"], ["koU%d" % k])
+                st = T.ST[:, 0:12 * s]
+                tt(st, T.pb2[:, 0:12 * s], st, ALU.max, ["ST", "pb2"], ["ST"])
+                tt(st, st, T.DUM[:, 0:12 * s], ALU.min, ["ST"] + DK, ["ST"])
+                cp(T.koU[:, 0:12 * s], st, ["ST"], ["koU"])
 
             def keep(e, k):
-                put(e, T.Tw, T.koU[:, 48 * s + 12 * k:48 * s + 12 * k + 12], T.KR[:, A * k:A * k + A],
-                    ["koU%d" % k, "KR%d" % k], "Tw")
+                put(e, T.Tw, blk(T.koU, k), blk(T.KR, k, A), ["koU", "KR%d" % k], "Tw")
 
             def bundle(_):
-                count()
-                ts(T.X1[:], T.ST[:], 1.0, ALU.add, ["ST"], ["X1"])
-                tt(T.X1[:], T.X1[:], T.AL[:], ALU.mult, ["X1", "AL"], ["X1"])
-                for k in range(3):
-                    ts(T.yE[:, 12 * k:12 * k + 12], T.nn[:, 4:60:5], float(k), ALU.is_equal, ["nn"], ["yE%d" % k])
-                for k in range(3):
-                    y_ = T.YQ[:, 60 * k:60 * k + 60]
-                    tt(y_, y_, T.X1[:], ALU.mult, ["YQ%d" % k, "X1"], ["YQ%d" % k])
-                scan(T.YS[:], T.R5[:], T.YQ[:], 0.0, ALU.mult, ALU.add, ["R5", "YQ0", "YQ1", "YQ2"], ["YS"])
-                ts(T.yB[:], T.YS[:, 4:180:5], 1.0, ALU.subtract, ["YS"], ["yB"])
+                if _ == 0:
+                    ts(T.X1[:], T.ST[:], -BIG, ALU.mult, ["ST"], ["X1"], BIG * (W - 0.5), ALU.add)
+                    rnd(T.fr[:], nl, M1, ["rs"], ["fr"])
+                    tt(T.X1[:], T.X1[:], T.ST[:], ALU.min, ["X1", "ST"], ["X1"])
+                    tt(T.fr[:], nl, T.fr[:], ALU.subtract, ["rs", "fr"], ["fr"])
+                    for k in range(3):
+                        tt(T.YQ[:, :, k, :], T.YQ[:, :, k, :], T.X1[:], ALU.add, ["YQ%d" % k, "X1"], ["YQ%d" % k])
+                    ts(T.x3[:], T.fr[:], 8.0 * A, ALU.mult, ["fr"], ["x3"])
+                else:
+                    tt(T.Y2[:], T.YQ[:, 0:2, :, :], T.YQ[:, 2:4, :, :], ALU.max, ["YQ0", "YQ1", "YQ2"], ["Y2"])
+                    tt(T.yE[:, 0:12], T.x3[:], T.aL[:], ALU.add, ["x3", "aL"], ["yE"])
+                    tt(T.yB[:], T.Y2[:, 0:36], T.Y2[:, 36:72], ALU.max, ["Y2"], ["yB"])
+                    ts(T.yB[:], T.yB[:], -1.0, ALU.max, ["yB"], ["yB"])
 
-            todo = {"P": pick, "K": kill, "Y": bundle, "k": lambda k: keep("a", k), "e": lambda k: keep("v", k)}
+            def rows(_):
+                for b, lo, hi in (("pb4", 0, 24), ("pb5", 24, 36)):
+                    for q in range(16):
+                        mm(T[b][0:8, q:16 * (hi - lo):16], T.I24[:, q:128:16], T.yB[:, lo:hi], True, True, ["yB"], [b], q == 15)
+                    act(T.y8[0:8, 16 * lo:16 * hi], T[b][0:8, 0:16 * (hi - lo)], [b], ["y8" + b], scale=1.0 / U24)
+                dma("s", T.yo[0:128:16, 0:576], T.y8[0:8, :], ["y8pb4", "y8pb5"], ["yo"])
+
+            todo = {"P": pick, "K": kill, "Y": bundle, "R": rows, "k": lambda k: keep("a", k), "e": lambda k: keep("v", k)}
         else:
             nl = T.aL[:]
             cp(T.cU[:], T.Cw[:].indirect(T.hU[:]), CK + ["hU"], ["cU"])
             mm(T.pS[:, 0:192], T.Ib[:], T.PST[:], True, False, ["Ib", "PST"], ["pS"])
-            todo = {"C": lambda _: cp(T.CC[:, 0:A], T.cU[:], ["cU"], ["CC0"])}
+            todo = {"C": lambda _: act(T.CC[:, 0:A], T.Cw[:].indirect(T.hU[:]), CK + ["hU"], ["CC0"])}
         GK = []
         for e, lo, hi in spans(VPLAN[s]):
             if e in "av":
@@ -488,6 +505,11 @@ def rank_program(g, core, T, topo):
                        ["EV", "E16"] + over("Vg", VPLAN[s], lo, hi), ["pS"], last)
             else:
                 todo[e](lo)
+        if s < 3:
+            later(s)
+        if s == 0:
+            ts(T.NO[:], T.Vw[:].indirect(T.sgU[:]), c_(20), ALU.mult, vk + ["sgU", "c20", "c21"], ["NO"], c_(21), ALU.add)
+            tt(T.WM[:], T.NO[:], T.BLK[:], ALU.mult, ["NO", "BLK"], ["WM"])
         mm(T.pb0[:, 0:12], T.I24[:], T.C16[:], True, False, ["C16"], ["pb0"])
         mm(T.pb1[:, 0:12], T.I24[:], T.CG[:], True, False, ["CG"], ["pb1"])
         mm(T.pP[:, 0:12], T.I24[:], T.CT[:], True, False, ["CT"], ["pP"])
@@ -511,38 +533,28 @@ def rank_program(g, core, T, topo):
         op("v", lambda: V.transpose(T.H[:], T.UT[:]), ["U0", "U8", "UTs", "UTo", "UT"], ["H"])
         cp(T.poU[:], T.pb0[:, 0:12], ["pb0"], ["poU"])
         ts(T.Bt[:], T.Vg[:].indirect(T.poU[:]), c_(6), ALU.mult, GK + ["poU", "c6"], ["Bt"])
-        tell = far is not None and not lastr
-        if tell:
-            z = slice(48 * s, 48 * s + 12 * t)
-            ts(T.koU[:, 48 * s + 12 * s:48 * s + 12 * t], T.Hh[:], 1.0 / 16.0, ALU.mult, ["Hh"], ["gU"])
-            send([([cores[far]], T.koU[:, z], T.koF[:, z], "aK%d" % s, off)], ["gU"] + ["koU%d" % k for k in range(s)])
-            mark(("aK%d" % s, len(off)), [], ["koF"])
         for u, h in uh:
             for j in (0, 8):
                 last = u + h == 2 and j == 8
                 mm(T.pb1[:, u:12:2], zm(u, h), T.UT[:, 16 * h + j:192:32], False, last, ["U0", "U8"], ["pb1"], last)
         act(T.nbb[:], T.pb1[:, 0:12], ["pb1"], ["nbb"], scale=-BIG)
+        act(T.nob[:], T.pb1[:, 0:12], ["pb1"], ["nob"], func=AF.Relu, scale=-2048.0, bias=2048.0 * (SAME + 14.0))
         mm(T.pS[:, 256:448], T.WK[:], T.H[:], True, True, ["WK", "H"], ["pS"], True)
-        for q in range(16):
-            mm(T.pP[:, 0:12], row(T.EW, q), T.Bt[:, q:192:16], False, q == 15, ["EW", "Bt"], ["pP"], q == 15)
+        wrap(T.pP[:, 0:12], T.EW, T.Bt, A, False, ["EW", "Bt"], ["pP"])
         for gq in range(NMV, 8):
             aff(T.Abd[:, :, gq, :], T.Bt[:], T.MC[:, gq:gq + 1], T.MKb[:, gq:gq + 1], ["Bt", "MC", "MKb"], ["A%d" % gq])
         tt(T.B[:], T.Bt[:], T.H[:], ALU.add, ["Bt", "H"], ["B"])
         for gq in range(NMV):
             ts(T.Abd[:, :, gq, :], T.Bt[:], T.MCb[:, gq:gq + 1], ALU.mult, ["Bt", "MCb", "MKb"], ["A%d" % gq],
                T.MKb[:, gq:gq + 1], ALU.add)
-        ts(T.nob[:], T.nbb[:], -BIG * (SAME + 13.0), ALU.is_gt, ["nbb"], ["nob"], 8192.0, ALU.mult)
         tt(T.ck[:], T.pP[:, 0:12], T.nob[:], ALU.max, ["pP", "nob"], ["ck"])
         if not lastr:
             cp(T.ctU[:], T.pP[:, 0:12], ["pP"], ["ctU"])
             if EARLY:
                 cp(T.cG[:], T.Cw[:].indirect(T.ctU[:]), CK + ["ctU"], ["cG"])
         else:
-            ts(T.x2[:], T.ck[:], 1.0, ALU.add, ["ck"], ["x2"])
-            for k in range(3):
-                y_ = T.yE[:, 12 * k:12 * k + 12]
-                tt(y_, y_, T.x2[:], ALU.mult, ["yE%d" % k, "x2"], ["yE%d" % k])
-        kr = T.KR[:, A * s:A * t]
+            tt(T.yE[:, 0:12], T.yE[:, 0:12], T.nob[:], ALU.add, ["yE", "nob"], ["yE"])
+        kr = blk(T.KR, s, A)
         act(kr, T.pS[:, 256:448], ["pS"], ["KR%d" % s])
         AK = ["A%d" % j for j in range(8)] + ["B"]
         for b in (3, 0, 4, 1, 5, 2):
@@ -551,112 +563,102 @@ def rank_program(g, core, T, topo):
             for j in range(2):
                 m = 2 * b + j
                 src = banks[b][:, 192 * j:192 * j + 192]
-                if b < 3:
+                if m < NRED:
                     op("v", lambda: V.tensor_reduce(T.Wr[:, m:m + 1], src, AxisListType.X, ALU.max), ["pb%d" % b], ["W%d" % m])
                 else:
-                    act(T.junk[:, A * (m - 6):A * (m - 5)], src, ["pb%d" % b, "nbb"], ["W%d" % m], func=AF.Relu,
+                    act(blk(T.junk, m - NRED, A), src, ["pb%d" % b, "nbb"], ["W%d" % m], func=AF.Relu,
                         bias=T.nbb[:, m:m + 1], accum_out=T.Wr[:, m:m + 1])
-        WD = ["W%d" % m for m in range(6)]
-        tt(T.Wr[:, 0:6], T.Wr[:, 0:6], T.nbb[:, 0:6], ALU.add, WD + ["nbb"], WD)
+        if lastr:
+            mm(T.pS[:, 0:192], T.WT[:], T.Bt[:], True, True, ["WT", "Bt"], ["pS"], True)
+        WD = ["W%d" % m for m in range(NRED)]
+        tt(T.Wr[:, 0:NRED], T.Wr[:, 0:NRED], T.nbb[:, 0:NRED], ALU.add, WD + ["nbb"], WD)
         tt(T.t12[:], T.Wr[:], T.ck[:], ALU.max, ["ck"] + ["W%d" % m for m in range(12)], ["t12"])
+        new = T.x1[:] if lastr else blk(T.ST, s)
         if lastr:
-            for k in range(3):
-                ts(T.yW[:, 12 * k:12 * k + 12], T.t12[:], float(W), ALU.is_lt, ["t12"], ["yW%d" % k])
-            tt(T.yW[:], T.yW[:], T.yE[:], ALU.mult, ["yW0", "yW1", "yW2", "yE0", "yE1", "yE2"], ["yW"])
-        new = T.x1[:] if lastr else T.ST[:, :, 4 - s]
-        tt(new, T.t12[:], T.DUM[:, :, 0], ALU.min, ["t12", "DUM", "ST"], ["x1" if lastr else "ST"])
+            tt(T.yE[:, 0:12], T.Wr[:], T.yE[:, 0:12], ALU.add, ["yE"] + ["W%d" % m for m in range(12)], ["yE"])
+            aff(T.S1[:], T.pS[:, 0:192], 1.0, 2047.5, ["pS"], ["S1"])
+        tt(new, T.t12[:], blk(T.DUM, 0), ALU.min, ["t12", "DUM0", "ST"], ["x1" if lastr else "ST"])
         if lastr:
-            tt(T.yL[:], T.yW[:], T.yB[:], ALU.add, ["yW", "yB"], ["yL"])
-        ou = T.oU[:, 16 * s:16 * s + 12]
-        cp(ou, new, ["ST", "x1"], ["oU"])
-        if tell:
-            send([([cores[far]], ou, T.oF[:, 16 * s:16 * s + 12], "aO%d" % s, off)], ["oU"])
-            mark(("aO%d" % s, len(off)), [], ["oF"])
-        put("v", T.Tw, ou, kr, ["oU", "KR%d" % s], "Tw")
+            tt(T.yE[:, 0:12], T.yE[:, 0:12], T.yE[:, 12:24], ALU.min, ["yE", "yD"], ["yE"])
+        cp(T.oU[:], new, ["ST", "x1"], ["oU"])
+        put("a" if lastr else "v", T.Tw, T.oU[:], kr, ["oU", "KR%d" % s], "Tw")
 
         if lastr:
-            dma("s", T.yt[:], T.Tw[0:128:16, 0:W], ["Tw"], ["yt"])
-            for q in range(16):
-                mm(T.pb0[0:8, q:384:16], T.I24[:, q:128:16], T.yL[:, 0:24], True, True, ["yL"], ["pb0"], q == 15)
-            for q in range(16):
-                mm(T.pb1[0:8, q:192:16], T.I24[:, q:128:16], T.yL[:, 24:36], True, True, ["yL"], ["pb1"], q == 15)
-            act(T.yo[0:8, 0:384], T.pb0[0:8, 0:384], ["pb0"], ["yo0"], scale=1.0 / U24)
-            ts(T.yo[0:8, 384:576], T.pb1[0:8, 0:192], 1.0 / U24, ALU.mult, ["pb1"], ["yo1"])
-            dma("a", T.yb[:], T.yo[0:8, :], ["yo0", "yo1"], ["yb"])
+            cp(T.noU[:], T.yE[:, 0:12], ["yE"], ["noU"])
+            put("v", T.yo, T.noU[:], T.S1[:], ["noU", "S1"], "yo")
+            dma("a", T.yt[:], T.Tw[0:128:16, 0:W], ["Tw"], ["yt"])
+            dma("s", T.yb[:], T.yo[0:128:16, 0:576], ["yo"], ["yb"])
             break
 
-        x = slice(240 * s, 240 * t)
-        tc = "Tc%d" % t
-        dma("s", T.Tc[:, x], T.Tw[0:128:16, 0:W], ["Tw"], [tc])
-        send([([cores[j]], T.Tc[:, x], T["N" + "RL"[j == right]][:, x], "a%s%d" % ("RL"[j == right], s), es)
-              for j, es in zip(close, (up, off) if far is None else (on,))], [tc])
-        for j in close:
-            alone = LISTS and (j + j - rank) % N not in mine
-            mark(("a%s%d" % ("LR"[j == right], s), len(on if alone else up)), [], ["N" + "LR"[j == right]])
-        (n1, k1_), (n2, k2_) = ((T.NL, "NL"), (T.NR, "NR")) if left in mine else ((T.NR, "NR"), (T.NL, "NL"))
-
-        def farkeys(_):
-            if far is not None:
-                ts(T.x3[:], T.koF[:, 48 * s + 12 * s:48 * s + 12 * t], 16.0, ALU.mult, ["koF"], ["x3"])
-                rnd(T.UF[:, 0:192:16], T.x3[:], M1K, ["x3", "UF"], ["UF0"])
-                tt(T.UF[:, 8:192:16], T.x3[:], T.UF[:, 0:192:16], ALU.subtract, ["x3", "UF0"], ["UF1"])
-                op("v", lambda: V.transpose(T.HF[:], T.UF[:]), ["UF", "UF0", "UF1"], ["HF"])
-                mm(T.pS[:, 256:448], T.WF[:], T.HF[:], True, True, ["WF", "HF"], ["pS"], True)
-                act(T.KF[:, A * s:A * t], T.pS[:, 256:448], ["pS"], ["KF%d" % s])
-
-        def farkeep(e):
-            if far is not None:
-                for k in range(s):
-                    put(FKEEP[k], T.Tf, T.koF[:, 48 * s + 12 * k:48 * s + 12 * k + 12], T.KF[:, A * k:A * k + A], ["koF", "KF%d" % k], "Tf")
-
-        def farbids(_):
-            if far is not None:
-                put(FBID, T.Tf, T.oF[:, 16 * s:16 * s + 12], T.KF[:, A * s:A * t], ["oF", "KF%d" % s], "Tf")
-                dma("s", n2[:, x], T.Tf[0:128:16, 0:W], ["Tf"], [k2_])
-            dma("s", T.Tw[0:128:16, 0:W], T.ZER[:], ["ZER"], ["Tw"])
-            if far is not None and t < RO - 1:
-                dma("s", T.Tf[0:128:16, 0:W], T.ZER[:], ["ZER"], ["Tf"])
+        tc, own = "Tc%d" % t, blk(T.Tc, s, FO)
+        dma("s", own, T.Tw[0:128:16, :], ["Tw"], [tc])
+        send([([cores[j]], own, blk(T["N" + "RL"[j == right]], s, FO), "a%s%d" % ("RL"[j == right], s), es)
+              for j, es in zip(ring, (up, off))], [tc])
+        for j in ring:
+            mark(("a%s%d" % ("LR"[j == right], s), len(up)), [], ["N" + "LR"[j == right]])
+        dma("s", T.Tw[0:128:16, :], T.ZER[:], ["ZER"], ["Tw"])
+        k1_, k2_ = ["N" + "LR"[j == right] for j in ring]
 
         def near(_):
-            tt(T.pb5[:, 0:240], T.Tc[:, x], n1[:, x], ALU.max, [tc, k1_], ["pb5"])
+            tt(T.pb5[:, 0:FO], T.pb4[:, 0:FO], blk(T[k1_], s, FO), ALU.max, ["pb4", k1_], ["pb5"])
 
         def tables(_):
-            tt(T.Vc[:], T.pb5[:, 0:240], n2[:, x], ALU.max, ["pb5", k2_], ["Vc"])
-            rnd(T.pb5[:, 256:496], T.Vc[:], M256, ["Vc"], ["pb5"])
-            cp(T.Pc[:, 0:240], T.Vc[:], ["Vc"], ["P0"])
-            dma("s", T.Vw[0:128:16, 0:W], T.Pc[:, 0:240], ["P0"], ["V0"] + SK)
-            tt(T.Pc[:, 480:720], T.Vc[:], T.pb5[:, 256:496], ALU.subtract, ["pb5", "Vc"], ["P2"])
-            dma("s", T.Vw[4:128:16, 0:W], T.Pc[:, 480:720], ["P2"], ["V2"])
-            tt(T.Pc[:, 240:480], T.pb5[:, 256:496], T.Pc[:, 0:240], ALU.subtract, ["pb5", "P0"], ["P1"])
-            dma("s", T.Vw[8:128:16, 0:W], T.Pc[:, 240:480], ["P1"], ["V1"])
+            tt(T.Vc[:], T.pb5[:, 0:FO], blk(T[k2_], s, FO), ALU.max, ["pb5", k2_], ["Vc"])
+
+        def lost(_):
+            tt(T.LO[:, 0:A * t], T.Vc[:].indirect(T.lU[:, 0:12 * t]), T.KM[:, 0:A * t], ALU.is_gt,
+               ["Vc"] + ["lU%d" % k for k in range(t)] + ["KM%d" % k for k in range(t)], ["LO"])
+
+        def pieces(_):
+            r_ = T.pb5[:, FO:2 * FO]
+            if _ == 2:
+                rnd(r_, T.Vc[:], M256, ["Vc"], ["pb5"])
+                tt(blk(T.Pc, 2, FO), T.Vc[:], r_, ALU.subtract, ["pb5", "Vc"], ["P2"])
+                dma("s", T.Vw[4:128:16, :], blk(T.Pc, 2, FO), ["P2"], ["V2"])
+            elif _ == 0:
+                (act if P0A else cp)(blk(T.Pc, 0, FO), T.Vc[:], ["Vc"], ["P0"])
+                dma("a" if P0A else "s", T.Vw[0:128:16, :], blk(T.Pc, 0, FO), ["P0"], ["V0"] + SK)
+            else:
+                tt(blk(T.Pc, 1, FO), r_, blk(T.Pc, 0, FO), ALU.subtract, ["pb5", "P0"], ["P1"])
+                dma("s", T.Vw[8:128:16, :], blk(T.Pc, 1, FO), ["P1"], ["V1"])
+
+        def place(_):
+            wrap(T.pb5[:, 0:12], T.EL, T.Bt, A, True, ["EL", "Bt"], ["pb5"])
+            mm(T.pS[:, 0:192], T.WM[:], T.B[:], True, False, ["WM", "B"], ["pS"])
+            mm(T.pS[:, 0:192], T.WK[:], T.H[:], False, True, ["WK", "H"], ["pS"], True)
+            act(blk(T.KM, s, A), T.pS[:, 0:192], ["pS"], ["KM%d" % s])
+            ts(blk(T.lU, s), T.pb5[:, 0:12], 127.5, ALU.add, ["pb5"], ["lU%d" % s])
 
         def append(_):
-            count()
-            ts(T.x2[:], T.nbb[:], -1.0 / BIG, ALU.mult, ["nbb"], ["x2"], SAME, ALU.subtract)
-            tt(T.x1[:], T.AL[:, 4 - s:60:5], T.aLt[:, 12 * s:12 * t], ALU.mult, ["AL", "aLt"], ["x1"])
-            cp(T.PW[:, :, 4 - s], nl, ["rs", "aL"], ["PW"])
-            tt(T.KW[:, :, 4 - s], T.x2[:], T.CK[:], ALU.add, ["x2", "CK"], ["KW"])
-            cp(T.btU[:, 0:12 * t + 12], T.ST[:, :, 4 - t:5], ["ST"], ["btU"])
-            tt(T.PW[:], T.PW[:], T.AL[:], ALU.mult, ["PW", "AL"], ["PW"])
-            if t >= 3:
-                ts(T.x2[:], T.nn[:, 4:60:5], 3.0, ALU.is_ge, ["nn"], ["x2"], float(A * (RO - t)), ALU.mult)
-                tt(T.x1[:], T.x1[:], T.x2[:], ALU.add, ["x1", "x2"], ["x1"])
-            tt(T.PW[:, :, 4 - t], T.x1[:], nl, ALU.max, ["x1", "rs", "aL", "PW"], ["PW"])
+            aff(T.X1[:], T.ST[:], -BIG, BIG * (W - 0.5), ["ST"], ["X1"])
+            act(blk(T.PW, s), nl, ["rs", "aL"], ["PW%d" % s])
+            ts(T.IN[:], T.ST[:], W - 0.5, ALU.subtract, ["ST"], ["IN"], BIG / U24, ALU.max)
+            up_ = blk(T.aLt, s)
             if s:
-                ts(T.NS[:, :, 4 - s], T.nn[:, 4:60:5], 1.0, ALU.subtract, ["nn", "NS"], ["NS%d" % s])
-            cp(T.PC[:, 0:12 * t + 12], T.PW[:, :, 4 - t:5], ["PW"], ["PC"])
+                level(nl)
+                act(blk(T.NS, s), T.fr[:], ["fr", "NS"], ["NS%d" % s], scale=8.0)
+                if t >= 3:
+                    act(T.x3[:], T.fr[:], ["fr"], ["x3"], func=AF.Relu, scale=8.0 * A * (RO - t), bias=-1.0 * A * (RO - t))
+                tt(T.x1[:], T.fr[:], up_, ALU.add, ["fr", "aLt%d" % s], ["x1"])
+                if t >= 3:
+                    tt(T.x1[:], T.x1[:], T.x3[:], ALU.add, ["x1", "x3"], ["x1"])
+                up_ = T.x1[:]
+            tt(T.x1[:], up_, blk(T.X1, s), ALU.min, ["x1", "X1", "aLt%d" % s], ["x1"])
+            tt(blk(T.U, 0), T.x1[:], nl, ALU.max, ["x1", "rs", "aL"], ["Ut"])
 
         def slots(_):
             if t == RO - 1:
                 for k in range(3):
-                    ts(T.YQ[:, 60 * k:60 * k + 60], T.NS[:], float(k), ALU.is_equal, ["NS", "NS1", "NS2", "NS3"], ["YQ%d" % k])
+                    ts(T.YQ[:, :, k, :], T.NS[:], float(k), ALU.not_equal, ["NS", "NS1", "NS2", "NS3"], ["YQ%d" % k], -BIG, ALU.mult)
 
-        if s:
-            act(T.Mn[:], T.CM[:, 0:A * nblk].indirect(T.noU[:]), keys("CM") + ["noU"], ["Mn"])
         if not EARLY:
             cp(T.cG[:], T.Cw[:].indirect(T.ctU[:]), CK + ["ctU"], ["cG"])
-        Mw = T.CM[:, A * t:A * t + A]
+        Mw = blk(T.CM, t, A)
         mk = "CM%d" % t
+
+        def sofar(_):
+            if s:
+                act(T.Mn[:], T.CM[:, 0:A * nblk].indirect(T.noU[:]), keys("CM") + ["noU"], ["Mn"])
 
         def most(_):
             if s:
@@ -665,16 +667,10 @@ def rank_program(g, core, T, topo):
                 cp(Mw, T.Fw[:].indirect(T.ctU[:]), FK + ["ctU"], [mk])
 
         def start(_):
-            mm(T.pb1[:, 0:192], T.Ib[:], Mw, True, True, ["Ib", mk], ["pb1"], True)
             mm(T.pb0[:, 0:192], T.Ib[:], T.PST[:], True, False, ["Ib", "PST"], ["pb0"])
 
         xs = lambda lo, hi, p: T.X[:, 16 * lo + (hi - lo) * p:16 * lo + (hi - lo) * (p + 1)]
         fs = lambda lo, hi, p: T.Fg[:, 16 * lo + p:16 * hi:16]
-
-        def top(lo, hi):
-            mm(T.pb0[:, lo:hi], T.NB16[:], T.CM[:, A * t + lo:A * t + hi], False, False, ["NB16", mk], ["pb0"])
-            for p in range(16):
-                tt(xs(lo, hi, p), fs(lo, hi, p), T.pb1[:, lo:hi], ALU.max, over("Fg", ORDER, lo, hi) + ["pb1"], ["X%d_%d" % (lo, p)])
 
         def sub(lo, hi):
             for p in range(16):
@@ -691,16 +687,17 @@ def rank_program(g, core, T, topo):
                 last = end and p == 15
                 mm(T.pb0[:, lo:hi], row(T.EG, p), xs(lo, hi, p), False, last, ["EG", "X%d_%d" % (lo, p)], ["pb0"], last)
 
-        steps = {"A": append, "N": near, "T": tables, "Y": slots, "M": most, "U": farkeys, "K": farkeep, "B": farbids, "I": start,
-                 "S": lambda _: act(T.CS[:, A * t:A * t + A], T.pb0[:, 0:192], ["pb0"], ["CS%d" % t]),
-                 "C": lambda _: cp(T.CC[:, A * t:A * t + A], T.cG[:], ["cG"], ["CC%d" % t])}
-        for e, lo, hi in spans(ORDER):
+        steps = {"A": append, "N": near, "T": tables, "Y": slots, "M": most, "H": sofar, "I": start, "L": place, "G": lost, "D": pieces,
+                 "S": lambda _: act(blk(T.CS, t, A), T.pb0[:, 0:192], ["pb0"], ["CS%d" % t]),
+                 "O": lambda _: act(T.pb4[:, 0:FO], own, [tc], ["pb4"]),
+                 "C": lambda _: act(blk(T.CC, t, A), T.Cw[:].indirect(T.ctU[:]), CK + ["ctU"], ["CC%d" % t])}
+        for e, lo, hi in spans(ORDER + " " + AFTER):
             if e in "av":
                 gather(e, T.Fg[:, 16 * lo:16 * hi], T.Fw[:], T.cG[:, lo:hi], FK + ["cG"], ["Fg%d" % lo])
             elif e in "tz":
                 tot(lo, hi, e == "z")
-            elif e in "xr":
-                (top if e == "x" else sub)(lo, hi)
+            elif e == "r":
+                sub(lo, hi)
             else:
                 steps[e](lo)
 

from concourse.bass import DstId, RemoteDMATransfer
from concourse.mybir import AluOpType as ALU, AxisListType, ActivationFunctionType as AF

N, Q, A, RO = 6, 640, 192, 5
W = N * Q
U24 = float(2 ** 24)
BIG = 65536.0
M1 = 1.5 * 2.0 ** 23
M16 = 1.5 * 2.0 ** 27
M256 = 1.5 * 2.0 ** 31
M1K = 1.5 * 2.0 ** 33
SAME = 12.0 * BIG
VW, FO = 4096, 256
SPLIT = 528
NMV = 4
NRED = 6
P0A = True
EARLY = True
ORDER = "H a0:64 a64:112 M v112:192 I r0:64 O L A r64:128 N T"
AFTER = "D2 t0:64 r128:192 D0 G D1 t64:128 z128:192 C S Y"
VP0 = "a0:32 v32:64 m0:64 a64:96 v96:128 m64:128 a128:160 v160:192 M128:192 C"
VP1 = "P K a0:36 v36:64 m0:64 a64:96 v96:128 m64:128 a128:160 v160:192 M128:192 k0"
VP2 = "P K a0:36 v36:64 m0:64 a64:96 v96:128 m64:128 a128:160 v160:192 M128:192 k0 k1"
VP3 = "P K a0:36 v36:64 m0:64 a64:96 v96:128 m64:128 a128:160 v160:192 M128:192 k0 k1 k2"
VP4 = "P K a0:40 v40:64 m0:64 a64:112 e0 v112:128 m64:128 a128:168 v168:192 Y0 M128:192 Y1 k1 k2 R k3"
VPLAN = (VP0, VP1, VP2, VP3, VP4)


def spans(plan_):
    return [(w_[0], int(w_[1:].split(":")[0] or 0), int(w_[1:].split(":")[-1] or 0)) for w_ in plan_.split()]


def over(name, plan_, lo, hi):
    return [name + str(a) for e, a, b in spans(plan_) if e in "av" and a < hi and b > lo]


f32, bf, i32, u16 = "float32", "bfloat16", "int32", "uint16"
SB = {
    bf: dict(Fw=W, Vw=VW, WM=128, NO=128, E1=160, ES=152, EG=160, EV=160, E16=160, EW=160, EL=160, EF=160, Z=320, BLK=128, Ib=128, Nb=128,
             WK=128, WT=128, UT=192, PST=192, MCb=8, MKb=8, SL=480, LO=768, Vg=3072, xx=12, H=192, Bt=192, B=192,
             junk=1536, Mn=192, CM=1152, Fg=3072, X=3072, Pc=3 * FO),
    u16: dict(Cu=W, hU=12, sgU=8, lU=48, koU=48, noU=12, cU=192, ctU=12, oU=12, poU=12, cG=192),
    i32: dict(Ci=Q, hI=12, pI=8),
    f32: dict(Cw=W, Tw=VW, CC=1152, CS=1152, KR=960, KM=768, col=24, AR=192, JG=128, XP=160, I24=128, NI=128, MC=8, FL=12, EQ=12,
              RJ=12, P2=12, OH=16, G8=8, CD=192, RS=192, aL=12, aT=12, aLt=48, C16=12, CG=12, CT=12, ZC=48, Y2=72, ZER=FO,
              ST=48, PW=48, DUM=48, NS=48, IN=48, X1=48, U=60, rs=12, S1=192, sc=192, sT=192, rm=192, Hh=12, ck=12, nbb=12,
              nob=12, Wr=12, t12=12, x1=12, x2=24, x3=12, fr=12, Sr=80, Tc=4 * FO, NL=4 * FO, NR=4 * FO, Vc=FO,
              yB=36, yE=24, y8=576, yo=768),
}
SCRATCH = {n_: ("sbuf", [128, c_], d_) for d_, t_ in SB.items() for n_, c_ in t_.items()}
SCRATCH["YQ"] = ("sbuf", [128, 4, 3, 12], f32)
SCRATCH["Abd"] = ("sbuf", [128, 12, 8, 16], bf)
BANKS = ["pb0", "pb1", "pb2", "pb3", "pb4", "pb5", "pS", "pP"]
SCRATCH.update({n_: ("psum", [128, 512], f32) for n_ in BANKS})
NDS = 40
SEMAPHORES = (["qv", "qa", "qp", "qg", "sent"] + ["a%s%d%d" % (k_, j, h) for k_ in "FC" for j in range(N) for h in range(2)]
              + ["aS%d" % j for j in range(N)]
              + ["a%s%d" % (k_, t) for k_ in "LR" for t in range(4)] + ["d%d" % i for i in range(NDS)])


def bits(es):
    m = 0
    for e in es:
        m |= 1 << e
    return m


def plan(T, topo):
    cores = list(T.cores)
    place = [(topo.host(c), topo.chip(c)) for c in cores]
    big = [r for r in range(N) if place[r] == place[0]]
    small = [r for r in range(N) if place[r] != place[0]]
    helper = {}
    for mine, other in ((big, small), (small, big)):
        c0 = cores[mine[0]]
        free = [c for c in topo.cores_of(c0) if c not in cores and topo.die(c) != topo.die(c0)
                and all(topo.may_write(c, cores[r]) for r in other)]
        helper.update(zip(mine, free))
    return cores, big, small, helper


def xfer(topo, src_core, dst_cores, src, dst, sem, engines):
    ids = []
    for d in dst_cores:
        rid, pid = topo.addr(d, src_core)
        ids.append(DstId(rid=rid, pnc=pid))
    return RemoteDMATransfer(dst_ids=ids, dma_engine_mask=bits(engines), remote_sem=sem, srcs=[src], dsts=[dst] * len(ids))


def span(big, kind, r, h):
    mid = SPLIT if kind == "C" and r in big else Q // 2
    return slice(r * Q + mid * h, r * Q + (Q if h else mid))


def piece(T, big, kind, r, h):
    return (T.Fw if kind == "F" else T.Cu)[:, span(big, kind, r, h)]


def helper_program(g, core, T, topo, cores, big, small, r):
    far = [cores[j] for j in (small if r in big else big)]
    off = topo.engines(core, far[0])
    n4 = len(off) // 2
    ap = T.SL[:, 80 * r:80 * r + 80]
    sem = T.sem["aS%d" % r]
    g.wait_ge(sem, n4)
    g.remote_dma_fused([xfer(topo, core, far[h::2], ap, ap, sem, off[h::2]) for h in range(2)], local_sem=T.sem.sent)
    sent = 2 * n4
    if r in big:
        for kind, es in (("C", off[0::2]), ("F", off[1::2])):
            ap = piece(T, big, kind, r, 1)
            sem = T.sem["a%s%d1" % (kind, r)]
            g.wait_ge(sem, n4)
            g.remote_dma_fused([xfer(topo, core, far, ap, ap, sem, es)], local_sem=T.sem.sent)
            sent += n4
    g.wait_ge(T.sem.sent, sent)


def rank_program(g, core, T, topo):
    cores, big, small, helper = plan(T, topo)
    rank = T.rank_of(core)
    if rank is None:
        for r, c in helper.items():
            if c == core:
                helper_program(g, core, T, topo, cores, big, small, r)
        return

    V, S, P = g.vector, g.scalar, g.tensor
    QU = {"v": V, "a": S, "p": P, "g": g, "s": g.sync}
    cnt = {"v": 0, "a": 0, "p": 0, "g": 0}
    seen = {q: {} for q in QU}
    wr, rd, total = {}, {}, {}
    nd, sent = [0], [0]

    def wait(q, ev):
        if seen[q].get(ev[0], 0) < ev[1]:
            QU[q].wait_ge(T.sem[ev[0]], ev[1])
            seen[q][ev[0]] = ev[1]

    def deps(q, r, w):
        need = {}
        own = "q" + q
        evs = [ev for k in r for ev in wr.get(k, [])]
        evs += [ev for k in w for ev in wr.get(k, []) + rd.get(k, [])]
        evs += [ev for k in r if k in BANKS for ev in rd.get(k, []) if ev[0] != own]
        for ev in evs:
            need[ev[0]] = max(need.get(ev[0], 0), ev[1])
        for s_, v_ in need.items():
            if not (q == "p" and s_ == own):
                wait(q, (s_, v_))

    def mark(ev, r, w):
        for k in r:
            rd.setdefault(k, []).append(ev)
        for k in w:
            wr[k] = [ev]
            rd[k] = []
        total[ev[0]] = max(total.get(ev[0], 0), ev[1])

    def op(q, fn, r, w, inc=True):
        deps(q, r, w)
        ins = fn()
        if inc:
            cnt[q] += 1
            ins.then_inc(T.sem["q" + q], 1)
            mark(("q" + q, cnt[q]), r, w)
        else:
            mark(("q" + q, cnt[q] + 1), r, w)

    def dma(q, out, in_, r, w):
        deps(q, r, w)
        s_ = "d%d" % nd[0]
        nd[0] += 1
        QU[q].dma_start(out, in_).then_inc(T.sem[s_], 16)
        mark((s_, 16), r, w)

    def ts(out, in0, s1, op0, r, w, s2=None, op1=None):
        if op1 is None:
            op("v", lambda: V.tensor_scalar(out, in0, s1, None, op0), r, w)
        else:
            op("v", lambda: V.tensor_scalar(out, in0, s1, s2, op0, op1), r, w)

    def tt(out, a, b, o, r, w):
        op("v", lambda: V.tensor_tensor(out, a, b, o), r, w)

    def cp(out, in_, r, w):
        op("v", lambda: V.tensor_copy(out, in_), r, w)

    def ms(ap, val, w):
        op("v", lambda: V.memset(ap, val), [], w)

    def scan(out, d0, d1, init, op0, op1, r, w):
        op("v", lambda: V.tensor_tensor_scan(out, d0, d1, init, op0, op1), r, w)

    def rnd(out, in_, m, r, w):
        ts(out, in_, m, ALU.add, r, w, m, ALU.subtract)

    def act(out, in_, r, w, func=AF.Copy, **kw):
        op("a", lambda: S.activation(out, in_, func, **kw), r, w)

    def aff(out, in_, scale, bias, r, w):
        act(out, in_, r, w, func=AF.Identity, scale=scale, bias=bias)

    def mm(out, lhsT, rhs, start, stop, r, w, inc=False):
        op("p", lambda: P.matmul(out, lhsT, rhs, start, stop), r, w, inc)

    def iota(out, pat, base, w):
        op("g", lambda: g.iota(out, pat, base, 0, allow_small_or_imprecise_dtypes=True), [], w)

    def gather(e, out, win, off_, r, w):
        if e == "v":
            cp(out, win.indirect(off_), r, w)
        else:
            act(out, win.indirect(off_), r, w)

    def put(e, win, off_, in_, r, wk):
        if e == "a":
            act(win[:].indirect(off_), in_, r, [wk], func=AF.Silu)
        else:
            cp(win[:].indirect(off_), in_, r, [wk])

    def send(trs, r):
        deps("g", r, [])
        g.remote_dma_fused([xfer(topo, core, d, a, b, T.sem[s_], es) for d, a, b, s_, es in trs], local_sem=T.sem.sent)
        sent[0] += sum(len(t_[4]) for t_ in trs)

    def row(E, q):
        return E[:, 23 - q:151 - q]

    def wrap(out, E, src, n_, first, r, w):
        for q in range(16):
            mm(out, row(E, q), src[:, q:n_:16], first and q == 0, q == 15, r, w, q == 15)

    FK = ["F%d%d" % (j, h) for j in range(N) for h in range(2)]
    CK = ["C%d%d" % (j, h) for j in range(N) for h in range(2)]
    VK = ["V0", "V1", "V2"]
    SK = ["S%d" % j for j in range(N)]
    me = slice(rank * Q, (rank + 1) * Q)
    fme = "F%d0" % rank
    blk = lambda X, k, n_=12: X[:, n_ * k:n_ * k + n_]

    dma("s", T.Fw[:, me], T.feat[:], [], [fme])
    dma("s", T.Ci[:], T.nb[:], [], ["Ci"])
    dma("a", T.hI[:], T.home[:], [], ["hI"])
    op("g", lambda: g.iota(T.pI[:, 0:1], [[0, 1]], 0, 1), [], ["pI"])
    iota(T.RJ[:], [[4, 4], [1, 3]], 1, ["RJ"])
    iota(T.AR[:], [[1, 192]], 0, ["AR"])
    iota(T.JG[:], [[1, 8], [0, 16]], 0, ["JG"])

    mine, other = (big, small) if rank in big else (small, big)
    i = mine.index(rank)
    peers = [cores[r] for r in mine if r != rank]
    on = topo.engines(core, peers[0])
    off = topo.engines(core, cores[other[0]])
    up = [e for e in on if e not in off]
    offC, offS = off[0::2], off[1::2]
    upA, upB = up[0::2], up[1::2]
    n4 = len(offC)
    left, right = (rank - 1) % N, (rank + 1) % N
    ring = sorted((left, right), key=lambda j: j in other)
    key = lambda kind, j, h: "%s%d%d" % ("F" if kind == "F" else "U", j, h)
    if rank in big:
        fwd = [(kind, small[i // 2], i % 2) for kind in "CF"]
    else:
        fwd = [(kind, r, 0) for kind in "CF" for r in big[i::2]]
    for j in range(N):
        if j != rank:
            mark(("aS%d" % j, n4), [], ["SL%d" % j])
            for kind in "FC":
                for h in range(2):
                    if j in mine and rank in big:
                        mark(("a%s%d%d" % (kind, j, h * (kind == "C")), len(up)), [], [key(kind, j, h)])
                        continue
                    n_ = n4
                    if j in other and rank in big and (kind, j, h) in fwd:
                        n_ = n4 // 2
                    elif j in other and rank in small and kind == "C" and h == 0 and (kind, j, h) not in fwd:
                        n_ = len(up)
                    mark(("a%s%d%d" % (kind, j, h), n_), [], [key(kind, j, h)])

    c_ = lambda j: T.col[:, j:j + 1]
    o_ = lambda j: T.OH[:, j:j + 1]
    for j, (v_, o) in enumerate(((15, ALU.bitwise_and), (4, ALU.arith_shift_right), (31, ALU.bitwise_and), (3, ALU.bitwise_and))):
        ts(T.pI[:, j + 1:j + 2], T.pI[:, 0:1], v_, o, ["pI"], ["pI%d" % j])
    cp(T.col[:, 0:5], T.pI[:, 0:5], ["pI", "pI0", "pI1", "pI2", "pI3"], ["c0"])
    ms(T.ZER[:], 0.0, ["ZER"])
    ts(T.EQ[:], T.RJ[:], c_(1), ALU.is_equal, ["RJ", "c0"], ["EQ"])
    ts(c_(6), c_(4), 0.0, ALU.not_equal, ["c0"], ["c6"])
    ts(c_(5), c_(2), 16.0, ALU.mult, ["c0"], ["c5"])
    ts(T.FL[:], T.EQ[:], -2.0, ALU.mult, ["EQ"], ["FL"], 1.0, ALU.add)
    cp(T.Vw[:, 0:1], c_(6), ["c6"], VK)
    ts(T.E1[:], T.AR[:, 0:160], c_(5), ALU.subtract, ["AR", "c5"], ["E1"], 23.0, ALU.is_equal)

    def double(j0, j1):
        for j in range(j0, j1):
            ts(T.Vw[:, 2 ** j:2 ** (j + 1)], T.Vw[:, 0:2 ** j], T.FL[:, j:j + 1], ALU.mult, VK + ["FL"], VK)

    double(0, 1)
    tt(T.ES[:], T.E1[:, 0:152], T.E1[:, 8:160], ALU.add, ["E1"], ["ES"])
    double(1, 3)
    dma("s", T.Tw[0:128:16, :], T.ZER[:], ["ZER"], ["Tw"])

    for E, b in ((T.ES, "pb0"), (T.E1, "pb1")):
        for h in range(8):
            mm(T[b][:, 0:80], E[:, 15 - h:143 - h], T.Fw[:, rank * Q + 80 * h:rank * Q + 80 * h + 80], h == 0, h == 7,
               ["ES", "E1", fme], [b], h == 7)
    a_ = blk(T.SL, rank, 80)
    rnd(T.Sr[:], T.pb0[:, 0:80], M16, ["pb0"], ["Sr"])
    tt(a_, T.Sr[:], T.pb1[:, 0:80], ALU.subtract, ["Sr", "pb1"], ["SL%d" % rank])
    cp(T.Cu[:, me], T.Ci[:], ["Ci"], ["U"])
    send([([helper[rank]], a_, a_, "aS%d" % rank, offS), (peers, a_, a_, "aS%d" % rank, upA)], ["SL%d" % rank])

    def part(dst, kind, j, h, es):
        a_ = piece(T, big, kind, j, h)
        return (dst, a_, a_, "a%s%d%d" % (kind, j, h), es)

    if rank in big:
        near_, far_ = [helper[rank]], [cores[small[i % 2]]]
        for h in range(2):
            send([part((far_, near_)[h], "C", rank, h, (offC, offS)[h]), part(peers, "C", rank, h, up)], ["U"])
        send([part(far_, "F", rank, 0, offC), part(near_, "F", rank, 1, offS)], [fme])
        for kind, j, h in fwd:
            send([part([d], kind, j, h, es) for d, es in zip(peers, (upA, upB, offS))], [key(kind, j, h)])
            if kind == "C":
                send([(peers, T.Fw[:, me], T.Fw[:, me], "aF%d0" % rank, up)], [fme])
    else:
        for kind in "CF":
            send([part([cores[big[2 * i + h]]], kind, rank, h, offC[2 * h:2 * h + 2]) for h in range(2)]
                 + [part(peers, kind, rank, h, (upA, upB)[h]) for h in range(2)], [fme, "U"])
        for c in fwd[0:2]:
            send([part(peers, *c, up)], [key(*c)])
        send([part(peers, *c, es) for c, es in zip(fwd[2:4], (upA, upB))], [key(*c) for c in fwd[2:4]])

    aff(T.aL[:], T.AR[:, 0:192:16], 1.0, c_(1), ["AR", "c0"], ["aL"])
    aff(T.XP[:], T.AR[:, 0:160], -1.0, c_(0), ["AR", "c0"], ["XP"])
    aff(c_(16), c_(1), -1.0, 7.5, ["c0"], ["c16"])
    aff(c_(17), c_(1), 1.0, (1087.0 - A * rank) / 128.0, ["c0"], ["c17"])
    aff(T.X1[:, 0:12], T.AR[:, 0:12], 0.0, 2.0, ["AR"], ["X1"])
    act(T.UT[:], T.AR[:], ["AR"], ["UT"], scale=0.0)
    between = [
        lambda: ts(T.OH[:], T.AR[:, 0:16], c_(1), ALU.is_equal, ["AR", "c0"], ["OH"]),
        lambda: ts(T.G8[:], T.AR[:, 0:8], c_(2), ALU.is_equal, ["AR", "c0"], ["G8"]),
        lambda: scan(T.P2[:], T.X1[:, 0:12], T.ZER[:, 0:12], -0.25, ALU.mult, ALU.add, ["X1", "ZER"], ["P2"]),
        lambda: ts(c_(7), c_(3), 16.0, ALU.is_lt, ["c0"], ["c7"]),
        lambda: tt(T.P2[:], T.P2[:], T.EQ[:], ALU.mult, ["P2", "EQ"], ["P2"]),
        lambda: cp(T.hU[:], T.hI[:], ["hI"], ["hU"]),
        lambda: ts(T.BLK[:], T.JG[:], c_(2), ALU.is_equal, ["JG", "c0"], ["BLK"])]
    for j, f in enumerate(between):
        double(3 + j, 4 + j)
        f()
    aff(c_(9), o_(0), 1.0, o_(8), ["OH"], ["c9"])
    act(c_(10), o_(4), ["OH"], ["c10"], scale=4096.0)
    act(c_(22), o_(8), ["OH"], ["c22"], scale=-16.0)
    act(c_(21), o_(12), ["OH"], ["c21"], scale=U24)
    act(c_(23), o_(4), ["OH"], ["c23"], scale=-2.0 * BIG)
    aff(c_(8), c_(7), -1.0, 1.0, ["c7"], ["c8"])
    aff(c_(11), o_(0), 16.0, c_(22), ["OH", "c22"], ["c11"])
    aff(c_(12), c_(9), BIG, c_(10), ["c9", "c10"], ["c12"])
    aff(c_(13), c_(9), 128.0, o_(4), ["c9", "OH"], ["c13"])
    aff(c_(14), c_(9), -2.0 * BIG, c_(23), ["c9", "c23"], ["c14"])
    aff(c_(15), o_(12), float(1856 - A * rank), c_(13), ["OH", "c13"], ["c15"])
    act(T.MC[:], T.G8[:], ["G8"], ["MC"], scale=BIG * BIG)
    act(T.MKb[:], T.G8[:], ["G8", "c12"], ["MKb"], func=AF.Identity, scale=c_(12))
    for j in (10, 11):
        act(T.Vw[:, 2 ** j:2 ** (j + 1)], T.Vw[:, 0:2 ** j], VK + ["FL"], VK, func=AF.Identity, scale=T.FL[:, j:j + 1])
    ts(T.sgU[:], T.ZER[:, 0:8], c_(1), ALU.add, ["c0", "ZER"], ["sgU"], float(FO), ALU.mult)
    for j in [rank] + [j for j in mine if j != rank] + other:
        dma("s", T.Vw[0:128:8, j * Q:(j + 1) * Q], blk(T.SL, j, 80), ["SL%d" % j, "V0"], ["S%d" % j])
    op("v", lambda: V.tensor_reduce(c_(18), T.P2[:], AxisListType.X, ALU.add), ["P2"], ["c18"])
    op("v", lambda: V.tensor_reduce(c_(19), T.P2[:, 0:8], AxisListType.X, ALU.add), ["P2"], ["c19"])
    ts(T.I24[:], T.XP[:, 0:128], 0.0, ALU.is_equal, ["XP"], ["I24"], U24, ALU.mult)
    ts(c_(20), c_(18), c_(19), ALU.not_equal, ["c18", "c19"], ["c20"], -U24 / 4, ALU.mult)
    ts(T.Z[:, 0:160], T.XP[:], -16.0, ALU.is_equal, ["XP", "c7"], ["Z0"], c_(7), ALU.mult)
    ts(T.Z[:, 160:320], T.XP[:], -16.0, ALU.is_equal, ["XP", "c8"], ["Z1"], c_(8), ALU.mult)
    cp(T.Cw[:, me], T.Ci[:], ["Ci"], ["C%d0" % rank])
    parts = [("C", j, h) for h in range(2) for j in mine if j != rank] + [c for c in fwd if c[0] == "C"]
    parts += [("C", j, h) for h in (1, 0) for j in other if ("C", j, h) not in parts]
    for c in parts:
        cp(T.Cw[:, span(big, *c)], T.Cu[:, span(big, *c)], [key(*c)], ["C%d%d" % c[1:]])

    zero = T.AR[:, 0:12]
    weigh = lambda out, in_, j, r, w: act(out[:], in_[:], r + ["c%d" % j], w, func=AF.Identity, scale=c_(j))
    weigh(T.E16, T.E1, 11, ["E1"], ["E16"])
    aff(T.PST[:], T.AR[:], 0.0, c_(16), ["AR", "c16"], ["PST"])
    act(T.Ib[:], T.I24[:], ["I24"], ["Ib"], scale=1.0 / U24)
    act(T.MCb[:], T.MC[:], ["MC"], ["MCb"])
    aff(T.RS[:], T.AR[:], 0.0, U24, ["AR"], ["RS"])
    aff(T.RS[:, 0:192:16], zero, 0.0, 7.5, ["AR", "RS"], ["RS"])
    for h in range(2):
        aff(T.aT[:, h:12:2], T.AR[:, 0:192:32], 1.0, c_(3), ["AR", "c0"], ["aT%d" % h])
    aff(T.UT[:, 4:192:16], T.aT[:], -1.0, 191.0, ["aT0", "aT1", "UT"], ["UTs"])
    aff(T.UT[:, 12:192:16], zero, 0.0, 1.0, ["AR", "UT"], ["UTo"])
    aff(T.C16[:], T.aL[:], 16.0 / U24, 7.5 / U24, ["aL"], ["C16"])
    aff(T.CG[:], T.aL[:], -1.0 / 16.0 / U24, (SAME + 191.0 / 16.0) / U24, ["aL"], ["CG"])
    aff(T.CT[:], zero, 0.0, 2047.5 / U24, ["AR"], ["CT"])
    DK = ["DUM%d" % k for k in range(4)]
    for k in range(4):
        act(blk(T.DUM, k), T.aL[:], ["aL"], [DK[k]], func=AF.Silu, bias=float(W))
    act(T.ST[:], T.DUM[:], DK, ["ST"])
    weigh(T.EW, T.E1, 18, ["E1"], ["EW"])
    weigh(T.WK, T.BLK, 15, ["BLK"], ["WK"])

    def later(k):
        if k == 2:
            for n_ in ("CM", "CC"):
                act(T[n_][:, 4 * A:6 * A], T.Cw[:, 0:2 * A], CK, [n_ + "4", n_ + "5"], scale=0.0)
            return
        if k == 0:
            act(T.Nb[:], T.I24[:], ["I24"], ["Nb"], scale=-1.0 / U24)
            act(T.EG[:], T.E1[:], ["E1"], ["EG"], scale=16.0)
            weigh(T.EV, T.E1, 14, ["E1"], ["EV"])
            weigh(T.EL, T.E1, 19, ["E1"], ["EL"])
            act(T.EF[:], T.E1[:], ["E1"], ["EF"], scale=-2.0 * BIG)
            act(T.NI[:], T.I24[:], ["I24"], ["NI"], scale=-BIG / U24)
            aff(T.CD[:], T.AR[:], -1.0 / 128.0, c_(17), ["AR", "c17"], ["CD"])
        else:
            act(blk(T.CM, 0, A), T.AR[:], ["AR"], ["CM0"], scale=0.0)
            act(T.NS[:], T.AR[:, 0:48], ["AR"], ["NS"], scale=0.0)
        for j in ((0,), (1, 2, 3))[k]:
            aff(blk(T.aLt, j), T.aL[:], 1.0, A * j + A + 0.125, ["aL"], ["aLt%d" % j])
            aff(blk(T.ZC, j), zero, 0.0, (A * j + A - 0.5) * BIG / U24, ["AR"], ["ZC%d" % j])
        if k == 1:
            aff(T.CS[:, 4 * A:6 * A], T.Cw[:, 0:2 * A], 0.0, -8.0, CK, ["CS4", "CS5"])
            weigh(T.WT, T.BLK, 18, ["BLK"], ["WT"])
            aff(T.yE[:, 12:24], T.aL[:], 1.0, 3.0 * A, ["aL"], ["yD"])

    def level(nl):
        rnd(T.fr[:], nl, M1, ["rs"], ["fr"])
        tt(T.fr[:], nl, T.fr[:], ALU.subtract, ["rs", "fr"], ["fr"])

    banks = [T.pb0, T.pb1, T.pb2, T.pb3, T.pb4, T.pb5]
    for t in range(1, RO + 1):
        s = t - 1
        lastr = t == RO
        nblk = t if t < 4 else 6
        keys = lambda n_: ["%s%d" % (n_, j) for j in range(nblk)]
        vk = VK if s else VK + SK
        if s:
            nl = T.rs[:]
            mm(T.pS[:, 0:192], T.I24[:], T.CD[:], True, False, ["I24", "CD"], ["pS"])
            mm(T.pb2[:, 0:12 * s], T.I24[:], T.ZC[:, 0:12 * s], True, False, ["I24"] + ["ZC%d" % k for k in range(s)], ["pb2"])
            mm(T.pP[:, 0:12 * s], T.I24[:], T.IN[:, 0:12 * s], True, False, ["I24", "IN"], ["pP"])
            wrap(T.pP[:, 0:12 * s], T.EF, T.LO, A * s, False, ["EF", "LO"], ["pP"])
            tt(T.U[:, 12:12 * t], T.pP[:, 0:12 * s], T.PW[:, 0:12 * s], ALU.max, ["pP"] + ["PW%d" % k for k in range(s)], ["U"])
            if s >= 3:
                tt(T.x2[:], T.U[:, 12 * s - 36:12 * s - 12], T.U[:, 12 * s - 12:12 * s + 12], ALU.min, ["U", "Ut"], ["x2"])
            pair = (T.x2[:, 0:12], T.x2[:, 12:24]) if s >= 3 else (blk(T.U, s - 1), blk(T.U, s))
            tt(T.x1[:] if s % 2 == 0 else nl, pair[0], pair[1], ALU.min, ["U", "Ut", "x2"], ["x1" if s % 2 == 0 else "rs"])
            if s % 2 == 0:
                tt(nl, T.x1[:], blk(T.U, 0), ALU.min, ["x1", "Ut"], ["rs"])
            cp(T.noU[:], nl, ["rs"], ["noU"])
            for k in range(s):
                mm(blk(T.pb2, k), T.NI[:], nl, False, k == s - 1, ["NI", "rs"], ["pb2"], k == s - 1)
            cp(T.cU[:], T.CC[:, 0:A * nblk].indirect(T.noU[:]), keys("CC") + ["noU"], ["cU"])

            def pick(_):
                cp(T.S1[:], T.CS[:, 0:A * nblk].indirect(T.noU[:]), keys("CS") + ["noU"], ["S1"])
                mm(T.pS[:, 0:192], T.I24[:], T.S1[:], False, False, ["S1"], ["pS"])

            def kill(_):
                st = T.ST[:, 0:12 * s]
                tt(st, T.pb2[:, 0:12 * s], st, ALU.max, ["ST", "pb2"], ["ST"])
                tt(st, st, T.DUM[:, 0:12 * s], ALU.min, ["ST"] + DK, ["ST"])
                cp(T.koU[:, 0:12 * s], st, ["ST"], ["koU"])

            def keep(e, k):
                put(e, T.Tw, blk(T.koU, k), blk(T.KR, k, A), ["koU", "KR%d" % k], "Tw")

            def bundle(_):
                if _ == 0:
                    ts(T.X1[:], T.ST[:], -BIG, ALU.mult, ["ST"], ["X1"], BIG * (W - 0.5), ALU.add)
                    rnd(T.fr[:], nl, M1, ["rs"], ["fr"])
                    tt(T.X1[:], T.X1[:], T.ST[:], ALU.min, ["X1", "ST"], ["X1"])
                    tt(T.fr[:], nl, T.fr[:], ALU.subtract, ["rs", "fr"], ["fr"])
                    for k in range(3):
                        tt(T.YQ[:, :, k, :], T.YQ[:, :, k, :], T.X1[:], ALU.add, ["YQ%d" % k, "X1"], ["YQ%d" % k])
                    ts(T.x3[:], T.fr[:], 8.0 * A, ALU.mult, ["fr"], ["x3"])
                else:
                    tt(T.Y2[:], T.YQ[:, 0:2, :, :], T.YQ[:, 2:4, :, :], ALU.max, ["YQ0", "YQ1", "YQ2"], ["Y2"])
                    tt(T.yE[:, 0:12], T.x3[:], T.aL[:], ALU.add, ["x3", "aL"], ["yE"])
                    tt(T.yB[:], T.Y2[:, 0:36], T.Y2[:, 36:72], ALU.max, ["Y2"], ["yB"])
                    ts(T.yB[:], T.yB[:], -1.0, ALU.max, ["yB"], ["yB"])

            def rows(_):
                for b, lo, hi in (("pb4", 0, 24), ("pb5", 24, 36)):
                    for q in range(16):
                        mm(T[b][0:8, q:16 * (hi - lo):16], T.I24[:, q:128:16], T.yB[:, lo:hi], True, True, ["yB"], [b], q == 15)
                    act(T.y8[0:8, 16 * lo:16 * hi], T[b][0:8, 0:16 * (hi - lo)], [b], ["y8" + b], scale=1.0 / U24)
                dma("s", T.yo[0:128:16, 0:576], T.y8[0:8, :], ["y8pb4", "y8pb5"], ["yo"])

            todo = {"P": pick, "K": kill, "Y": bundle, "R": rows, "k": lambda k: keep("a", k), "e": lambda k: keep("v", k)}
        else:
            nl = T.aL[:]
            cp(T.cU[:], T.Cw[:].indirect(T.hU[:]), CK + ["hU"], ["cU"])
            mm(T.pS[:, 0:192], T.Ib[:], T.PST[:], True, False, ["Ib", "PST"], ["pS"])
            todo = {"C": lambda _: act(T.CC[:, 0:A], T.Cw[:].indirect(T.hU[:]), CK + ["hU"], ["CC0"])}
        GK = []
        for e, lo, hi in spans(VPLAN[s]):
            if e in "av":
                GK.append("Vg%d" % lo)
                gather(e, T.Vg[:, 16 * lo:16 * hi], T.Vw[:], T.cU[:, lo:hi], vk + ["cU"], GK[-1:])
            elif e in "mM":
                for p in range(16):
                    last = e == "M" and p == 15
                    mm(T.pS[:, lo:hi], row(T.EV if s else T.E16, p), T.Vg[:, 16 * lo + p:16 * hi:16], False, last,
                       ["EV", "E16"] + over("Vg", VPLAN[s], lo, hi), ["pS"], last)
            else:
                todo[e](lo)
        if s < 3:
            later(s)
        if s == 0:
            ts(T.NO[:], T.Vw[:].indirect(T.sgU[:]), c_(20), ALU.mult, vk + ["sgU", "c20", "c21"], ["NO"], c_(21), ALU.add)
            tt(T.WM[:], T.NO[:], T.BLK[:], ALU.mult, ["NO", "BLK"], ["WM"])
        mm(T.pb0[:, 0:12], T.I24[:], T.C16[:], True, False, ["C16"], ["pb0"])
        mm(T.pb1[:, 0:12], T.I24[:], T.CG[:], True, False, ["CG"], ["pb1"])
        mm(T.pP[:, 0:12], T.I24[:], T.CT[:], True, False, ["CT"], ["pP"])

        if s:
            tt(T.sc[:], T.S1[:], T.pS[:, 0:192], ALU.min, ["S1", "pS"], ["sc"])
            op("v", lambda: V.transpose(T.sT[:], T.sc[:]), ["sc"], ["sT"])
        else:
            op("v", lambda: V.transpose(T.sT[:], T.pS[:, 0:192]), ["pS"], ["sT"])
            act(T.CS[:, 0:A], T.pS[:, 0:192], ["pS"], ["CS0"])
        scan(T.rm[:], T.RS[:], T.sT[:], U24, ALU.min, ALU.max, ["sT", "RS"], ["rm"])
        best = T.rm[:, 15:192:16]
        rnd(T.Hh[:], best, M16, ["rm"], ["Hh"])
        rnd(T.UT[:, 0:192:16], best, M1K, ["rm", "UT"], ["U0"])
        tt(T.xx[:], T.Hh[:], best, ALU.subtract, ["rm", "Hh"], ["xx"])
        tt(T.UT[:, 8:192:16], T.Hh[:], T.UT[:, 0:192:16], ALU.subtract, ["Hh", "U0"], ["U8"])
        uh = [(u, h) for u in range(2) for h in range(2)]
        zm = lambda u, h: T.Z[:, 160 * u + 16 - 16 * (h - u):160 * u + 144 - 16 * (h - u)]
        for u, h in uh:
            mm(T.pb0[:, u:12:2], zm(u, h), T.xx[:, h:12:2], False, u + h == 2, ["Z0", "Z1", "xx"], ["pb0"], u + h == 2)
        op("v", lambda: V.transpose(T.H[:], T.UT[:]), ["U0", "U8", "UTs", "UTo", "UT"], ["H"])
        cp(T.poU[:], T.pb0[:, 0:12], ["pb0"], ["poU"])
        ts(T.Bt[:], T.Vg[:].indirect(T.poU[:]), c_(6), ALU.mult, GK + ["poU", "c6"], ["Bt"])
        for u, h in uh:
            for j in (0, 8):
                last = u + h == 2 and j == 8
                mm(T.pb1[:, u:12:2], zm(u, h), T.UT[:, 16 * h + j:192:32], False, last, ["U0", "U8"], ["pb1"], last)
        act(T.nbb[:], T.pb1[:, 0:12], ["pb1"], ["nbb"], scale=-BIG)
        act(T.nob[:], T.pb1[:, 0:12], ["pb1"], ["nob"], func=AF.Relu, scale=-2048.0, bias=2048.0 * (SAME + 14.0))
        mm(T.pS[:, 256:448], T.WK[:], T.H[:], True, True, ["WK", "H"], ["pS"], True)
        wrap(T.pP[:, 0:12], T.EW, T.Bt, A, False, ["EW", "Bt"], ["pP"])
        for gq in range(NMV, 8):
            aff(T.Abd[:, :, gq, :], T.Bt[:], T.MC[:, gq:gq + 1], T.MKb[:, gq:gq + 1], ["Bt", "MC", "MKb"], ["A%d" % gq])
        tt(T.B[:], T.Bt[:], T.H[:], ALU.add, ["Bt", "H"], ["B"])
        for gq in range(NMV):
            ts(T.Abd[:, :, gq, :], T.Bt[:], T.MCb[:, gq:gq + 1], ALU.mult, ["Bt", "MCb", "MKb"], ["A%d" % gq],
               T.MKb[:, gq:gq + 1], ALU.add)
        tt(T.ck[:], T.pP[:, 0:12], T.nob[:], ALU.max, ["pP", "nob"], ["ck"])
        if not lastr:
            cp(T.ctU[:], T.pP[:, 0:12], ["pP"], ["ctU"])
            if EARLY:
                cp(T.cG[:], T.Cw[:].indirect(T.ctU[:]), CK + ["ctU"], ["cG"])
        else:
            tt(T.yE[:, 0:12], T.yE[:, 0:12], T.nob[:], ALU.add, ["yE", "nob"], ["yE"])
        kr = blk(T.KR, s, A)
        act(kr, T.pS[:, 256:448], ["pS"], ["KR%d" % s])
        AK = ["A%d" % j for j in range(8)] + ["B"]
        for b in (3, 0, 4, 1, 5, 2):
            for j in range(2):
                mm(banks[b][:, 192 * j:192 * j + 192], T.Abd[:, 2 * b + j, :, :], T.B[:], True, True, AK, ["pb%d" % b], j == 1)
            for j in range(2):
                m = 2 * b + j
                src = banks[b][:, 192 * j:192 * j + 192]
                if m < NRED:
                    op("v", lambda: V.tensor_reduce(T.Wr[:, m:m + 1], src, AxisListType.X, ALU.max), ["pb%d" % b], ["W%d" % m])
                else:
                    act(blk(T.junk, m - NRED, A), src, ["pb%d" % b, "nbb"], ["W%d" % m], func=AF.Relu,
                        bias=T.nbb[:, m:m + 1], accum_out=T.Wr[:, m:m + 1])
        if lastr:
            mm(T.pS[:, 0:192], T.WT[:], T.Bt[:], True, True, ["WT", "Bt"], ["pS"], True)
        WD = ["W%d" % m for m in range(NRED)]
        tt(T.Wr[:, 0:NRED], T.Wr[:, 0:NRED], T.nbb[:, 0:NRED], ALU.add, WD + ["nbb"], WD)
        tt(T.t12[:], T.Wr[:], T.ck[:], ALU.max, ["ck"] + ["W%d" % m for m in range(12)], ["t12"])
        new = T.x1[:] if lastr else blk(T.ST, s)
        if lastr:
            tt(T.yE[:, 0:12], T.Wr[:], T.yE[:, 0:12], ALU.add, ["yE"] + ["W%d" % m for m in range(12)], ["yE"])
            aff(T.S1[:], T.pS[:, 0:192], 1.0, 2047.5, ["pS"], ["S1"])
        tt(new, T.t12[:], blk(T.DUM, 0), ALU.min, ["t12", "DUM0", "ST"], ["x1" if lastr else "ST"])
        if lastr:
            tt(T.yE[:, 0:12], T.yE[:, 0:12], T.yE[:, 12:24], ALU.min, ["yE", "yD"], ["yE"])
        cp(T.oU[:], new, ["ST", "x1"], ["oU"])
        put("a" if lastr else "v", T.Tw, T.oU[:], kr, ["oU", "KR%d" % s], "Tw")

        if lastr:
            cp(T.noU[:], T.yE[:, 0:12], ["yE"], ["noU"])
            put("v", T.yo, T.noU[:], T.S1[:], ["noU", "S1"], "yo")
            dma("a", T.yt[:], T.Tw[0:128:16, 0:W], ["Tw"], ["yt"])
            dma("s", T.yb[:], T.yo[0:128:16, 0:576], ["yo"], ["yb"])
            break

        tc, own = "Tc%d" % t, blk(T.Tc, s, FO)
        dma("s", own, T.Tw[0:128:16, :], ["Tw"], [tc])
        send([([cores[j]], own, blk(T["N" + "RL"[j == right]], s, FO), "a%s%d" % ("RL"[j == right], s), es)
              for j, es in zip(ring, (up, off))], [tc])
        for j in ring:
            mark(("a%s%d" % ("LR"[j == right], s), len(up)), [], ["N" + "LR"[j == right]])
        dma("s", T.Tw[0:128:16, :], T.ZER[:], ["ZER"], ["Tw"])
        k1_, k2_ = ["N" + "LR"[j == right] for j in ring]

        def near(_):
            tt(T.pb5[:, 0:FO], T.pb4[:, 0:FO], blk(T[k1_], s, FO), ALU.max, ["pb4", k1_], ["pb5"])

        def tables(_):
            tt(T.Vc[:], T.pb5[:, 0:FO], blk(T[k2_], s, FO), ALU.max, ["pb5", k2_], ["Vc"])

        def lost(_):
            tt(T.LO[:, 0:A * t], T.Vc[:].indirect(T.lU[:, 0:12 * t]), T.KM[:, 0:A * t], ALU.is_gt,
               ["Vc"] + ["lU%d" % k for k in range(t)] + ["KM%d" % k for k in range(t)], ["LO"])

        def pieces(_):
            r_ = T.pb5[:, FO:2 * FO]
            if _ == 2:
                rnd(r_, T.Vc[:], M256, ["Vc"], ["pb5"])
                tt(blk(T.Pc, 2, FO), T.Vc[:], r_, ALU.subtract, ["pb5", "Vc"], ["P2"])
                dma("s", T.Vw[4:128:16, :], blk(T.Pc, 2, FO), ["P2"], ["V2"])
            elif _ == 0:
                (act if P0A else cp)(blk(T.Pc, 0, FO), T.Vc[:], ["Vc"], ["P0"])
                dma("a" if P0A else "s", T.Vw[0:128:16, :], blk(T.Pc, 0, FO), ["P0"], ["V0"] + SK)
            else:
                tt(blk(T.Pc, 1, FO), r_, blk(T.Pc, 0, FO), ALU.subtract, ["pb5", "P0"], ["P1"])
                dma("s", T.Vw[8:128:16, :], blk(T.Pc, 1, FO), ["P1"], ["V1"])

        def place(_):
            wrap(T.pb5[:, 0:12], T.EL, T.Bt, A, True, ["EL", "Bt"], ["pb5"])
            mm(T.pS[:, 0:192], T.WM[:], T.B[:], True, False, ["WM", "B"], ["pS"])
            mm(T.pS[:, 0:192], T.WK[:], T.H[:], False, True, ["WK", "H"], ["pS"], True)
            act(blk(T.KM, s, A), T.pS[:, 0:192], ["pS"], ["KM%d" % s])
            ts(blk(T.lU, s), T.pb5[:, 0:12], 127.5, ALU.add, ["pb5"], ["lU%d" % s])

        def append(_):
            aff(T.X1[:], T.ST[:], -BIG, BIG * (W - 0.5), ["ST"], ["X1"])
            act(blk(T.PW, s), nl, ["rs", "aL"], ["PW%d" % s])
            ts(T.IN[:], T.ST[:], W - 0.5, ALU.subtract, ["ST"], ["IN"], BIG / U24, ALU.max)
            up_ = blk(T.aLt, s)
            if s:
                level(nl)
                act(blk(T.NS, s), T.fr[:], ["fr", "NS"], ["NS%d" % s], scale=8.0)
                if t >= 3:
                    act(T.x3[:], T.fr[:], ["fr"], ["x3"], func=AF.Relu, scale=8.0 * A * (RO - t), bias=-1.0 * A * (RO - t))
                tt(T.x1[:], T.fr[:], up_, ALU.add, ["fr", "aLt%d" % s], ["x1"])
                if t >= 3:
                    tt(T.x1[:], T.x1[:], T.x3[:], ALU.add, ["x1", "x3"], ["x1"])
                up_ = T.x1[:]
            tt(T.x1[:], up_, blk(T.X1, s), ALU.min, ["x1", "X1", "aLt%d" % s], ["x1"])
            tt(blk(T.U, 0), T.x1[:], nl, ALU.max, ["x1", "rs", "aL"], ["Ut"])

        def slots(_):
            if t == RO - 1:
                for k in range(3):
                    ts(T.YQ[:, :, k, :], T.NS[:], float(k), ALU.not_equal, ["NS", "NS1", "NS2", "NS3"], ["YQ%d" % k], -BIG, ALU.mult)

        if not EARLY:
            cp(T.cG[:], T.Cw[:].indirect(T.ctU[:]), CK + ["ctU"], ["cG"])
        Mw = blk(T.CM, t, A)
        mk = "CM%d" % t

        def sofar(_):
            if s:
                act(T.Mn[:], T.CM[:, 0:A * nblk].indirect(T.noU[:]), keys("CM") + ["noU"], ["Mn"])

        def most(_):
            if s:
                tt(Mw, T.Fw[:].indirect(T.ctU[:]), T.Mn[:], ALU.max, FK + ["ctU", "Mn"], [mk])
            else:
                cp(Mw, T.Fw[:].indirect(T.ctU[:]), FK + ["ctU"], [mk])

        def start(_):
            mm(T.pb0[:, 0:192], T.Ib[:], T.PST[:], True, False, ["Ib", "PST"], ["pb0"])

        xs = lambda lo, hi, p: T.X[:, 16 * lo + (hi - lo) * p:16 * lo + (hi - lo) * (p + 1)]
        fs = lambda lo, hi, p: T.Fg[:, 16 * lo + p:16 * hi:16]

        def sub(lo, hi):
            for p in range(16):
                b = 2 + p // 8
                o = banks[b][:, 64 * (p % 8):64 * (p % 8) + hi - lo]
                mm(o, T.Nb[:], T.CM[:, A * t + lo:A * t + hi], True, False, ["Nb", mk], ["pb%d" % b])
                mm(o, T.Ib[:], fs(lo, hi, p), False, True, ["Ib"] + over("Fg", ORDER, lo, hi), ["pb%d" % b], p % 8 == 7)
            for h in range(2):
                act(T.X[:, 16 * lo + 512 * h:16 * lo + 512 * h + 512], banks[2 + h][:], ["pb%d" % (2 + h)],
                    ["X%d_%d" % (lo, p) for p in range(8 * h, 8 * h + 8)], func=AF.Relu)

        def tot(lo, hi, end):
            for p in range(16):
                last = end and p == 15
                mm(T.pb0[:, lo:hi], row(T.EG, p), xs(lo, hi, p), False, last, ["EG", "X%d_%d" % (lo, p)], ["pb0"], last)

        steps = {"A": append, "N": near, "T": tables, "Y": slots, "M": most, "H": sofar, "I": start, "L": place, "G": lost, "D": pieces,
                 "S": lambda _: act(blk(T.CS, t, A), T.pb0[:, 0:192], ["pb0"], ["CS%d" % t]),
                 "O": lambda _: act(T.pb4[:, 0:FO], own, [tc], ["pb4"]),
                 "C": lambda _: act(blk(T.CC, t, A), T.Cw[:].indirect(T.ctU[:]), CK + ["ctU"], ["CC%d" % t])}
        for e, lo, hi in spans(ORDER + " " + AFTER):
            if e in "av":
                gather(e, T.Fg[:, 16 * lo:16 * hi], T.Fw[:], T.cG[:, lo:hi], FK + ["cG"], ["Fg%d" % lo])
            elif e in "tz":
                tot(lo, hi, e == "z")
            elif e == "r":
                sub(lo, hi)
            else:
                steps[e](lo)

    total["sent"] = sent[0]
    for s_, v_ in total.items():
        wait("g", (s_, v_))
